import numpy as np
import ml_dtypes


def mxq(x, axis, fmt="e4m3"):
    dtype, down = {"e4m3": (ml_dtypes.float8_e4m3fn, 7), "e5m2": (ml_dtypes.float8_e5m2, 14)}[fmt]
    v = np.moveaxis(np.asarray(x, np.float32).astype(ml_dtypes.bfloat16).astype(np.float64), axis, -1)
    blocks = v.reshape(v.shape[:-1] + (-1, 32))
    amax = np.abs(blocks).max(-1, keepdims=True)
    byte = np.maximum(np.where(amax > 0, np.frexp(amax)[1] - 1 + 127, 0) - down, 1)
    scale = np.exp2(byte - 127.0)
    codes = (blocks / scale).astype(np.float32).astype(dtype).astype(np.float64)
    return np.moveaxis((codes * scale).reshape(v.shape), -1, axis)


WIDE = False


def mx_kscale(k):
    if not WIDE:
        return np.ones(k)
    levels = np.array([10, -10, 5, -5, 0])
    if k % 512:
        return np.exp2(np.random.permutation(np.resize(levels, k // 32))).repeat(32)
    a = np.empty((k // 512, 16))
    for p in range(k // 512):
        a[p, :8] = np.random.permutation(np.resize(levels, 8))
        for g in range(8):
            far = levels[np.abs(levels - a[p, g]) >= 10]
            a[p, g + 8] = far[np.random.randint(len(far))]
    return np.exp2(a.ravel()).repeat(32)


def f64(x):
    return np.asarray(x).astype(np.float64)


def striped(idx):
    return np.tile(idx.reshape(-1, 16).T, (8, 1)).astype(np.uint16)


def unstriped(offs):
    return offs[:16].T.reshape(-1).astype(np.int64)


def pack_weight(w):
    k, n = w.shape
    w = f64(np.asarray(w, np.float32).astype(ml_dtypes.bfloat16)).reshape(k // 32, 32, n)
    amax = np.abs(w).max(1)
    byte = np.clip(np.where(amax > 0, np.frexp(amax)[1] - 1 + 127 - 7, 1), 1, 254)
    scaled = (w * np.exp2(127.0 - byte)[:, None, :]).reshape(k, n).astype(np.float32)
    words = np.ascontiguousarray(scaled.reshape(k // 512, 128, 4, n).transpose(0, 1, 3, 2)).astype(ml_dtypes.float8_e4m3fn).view(np.uint8)
    return words, np.ascontiguousarray(byte.astype(np.uint8).reshape(k // 512, 16, n))


def unpack_weight(words, scales):
    g, p, n, _ = words.shape
    vals = np.ascontiguousarray(words).view(ml_dtypes.float8_e4m3fn).astype(np.float64) * np.repeat(np.exp2(scales.astype(np.float64) - 127.0), 8, axis=1)[..., None]
    return vals.transpose(0, 1, 3, 2).reshape(g * 512, n)


def silu(v):
    return v / (1.0 + np.exp(-np.maximum(v, -700.0)))


K, T, S, H, N = 512, 2048, 1024, 1024, 512


def setup_inputs():
    n = np.random.standard_normal
    s = mx_kscale(K)[:, None]
    u = mx_kscale(H)
    packed = pack_weight(n((K, T)) * s)
    return {
        "x_words": packed[0],
        "x_scales": packed[1],
        "w1": (n((K, H)) / np.sqrt(K) / s).astype(np.float32),
        "w3": (n((K, H)) / np.sqrt(K) / s * u).astype(np.float32),
        "w2": (n((H, N)) / np.sqrt(H) / u[:, None]).astype(np.float32),
        "offs": striped(np.sort(np.random.permutation(T)[:S])),
    }


def reference(x_words, x_scales, w1, w3, w2, offs):
    idx = unstriped(offs)
    xq = unpack_weight(x_words, x_scales)[:, idx]
    h = silu(mxq(f64(w1), 0, "e4m3").T @ xq) * (mxq(f64(w3), 0, "e4m3").T @ xq)
    y = mxq(f64(w2), 0, "e4m3").T @ mxq(h, 0, "e4m3")
    return y

@@ -1,0 +1,320 @@
+from contextlib import ExitStack
+
+import concourse.mybir as mybir
+
+K, T, S, H, N = 512, 2048, 1024, 1024, 512
+FLOPS = 2 * S * (2 * K * H + H * N)
+
+F32 = mybir.dt.float32
+BF16 = mybir.dt.bfloat16
+I32 = mybir.dt.int32
+U32 = mybir.dt.uint32
+U16 = mybir.dt.uint16
+U8 = mybir.dt.uint8
+FP8X4 = mybir.dt.float8_e4m3fn_x4
+SILU = mybir.ActivationFunctionType.Silu
+MULT = mybir.AluOpType.mult
+
+P = 128
+PACK = 4
+PASS = P * PACK
+PASSES = H // PASS
+HALF = PASS // 2
+CHUNK = 256
+CHUNKS = S // CHUNK
+SUB = 128
+SUBS = S // SUB
+LIST_ROWS = 16
+SPANS = [(0, 256), (256, 256), (512, 256), (768, 128), (896, 128)]
+LOADS = [
+    ("scales",),
+    ("x", 1, 1),
+    ("offs",),
+    ("x", 0, 0),
+    ("up0", "w1", 1, 2),
+    ("up0", "w1", 0, 2),
+    ("x", 2, 2),
+    ("up0", "w3", 0, 1),
+    ("up0", "w3", 1, 1),
+    ("up1", "w1"),
+    ("up1", "w3"),
+    ("down", 1),
+    ("x", 3, 3),
+    ("down", 0),
+]
+STEPS = [
+    ("ru", "w3", 0, 1, "vector"),
+    ("ru", "w1", 1, 1, "vector"),
+    ("ru", "w1", 0, 1, "scalar"),
+    ("gw", 0),
+    ("ru", "w1", 0, 0, "scalar"),
+    ("qu", "w1", 1, 1),
+    ("ru", "w3", 0, 0, "scalar"),
+    ("ru", "w1", 1, 0, "scalar"),
+    ("qu", "w3", 0, 0),
+    ("gs", 1),
+    ("ru", "w3", 1, 1, "scalar"),
+    ("rd", 1, 1, "vector"),
+    ("qu", "w1", 0, 0),
+    ("gs", 2),
+    ("qu", "w1", 0, 1),
+    ("qu", "w1", 1, 0),
+    ("ru", "w3", 1, 0, "scalar"),
+    ("gs", 0),
+    ("qu", "w3", 1, 0),
+    ("si", 0, 0),
+    ("gw", 1),
+    ("si", 0, 2),
+    ("qu", "w3", 0, 1),
+    ("rd", 0, 1, "scalar"),
+    ("gw", 3),
+    ("si", 1, 3),
+    ("si", 0, 3),
+    ("gs", 3),
+    ("si", 1, 1),
+    ("mu", 0, 2),
+    ("si", 0, 7),
+    ("si", 1, 0),
+    ("si", 0, 1),
+    ("si", 0, 6),
+    ("mu", 0, 1),
+    ("qu", "w3", 1, 1),
+    ("gw", 2),
+    ("mu", 1, 0),
+    ("mu", 1, 3),
+    ("si", 1, 5),
+    ("si", 1, 2),
+    ("mu", 1, 1),
+    ("si", 0, 5),
+    ("rd", 1, 0, "scalar"),
+    ("si", 0, 4),
+    ("qd", 0, 1),
+    ("qd", 1, 0),
+    ("mu", 0, 0),
+    ("mu", 0, 5),
+    ("si", 1, 7),
+    ("si", 1, 4),
+    ("mu", 0, 3),
+    ("qd", 1, 1),
+    ("mu", 0, 4),
+    ("qh", 1, 0),
+    ("mu", 1, 4),
+    ("mu", 1, 2),
+    ("qh", 0, 0),
+    ("rd", 0, 0, "vector"),
+    ("mu", 1, 5),
+    ("dn", 0, 1, "scalar"),
+    ("qd", 0, 0),
+    ("dn", 0, 0, "scalar"),
+    ("mu", 0, 7),
+    ("qh", 0, 2),
+    ("qh", 1, 1),
+    ("qh", 1, 2),
+    ("mu", 1, 7),
+    ("qh", 1, 4),
+    ("qh", 0, 1),
+    ("dn", 2, 0, "scalar"),
+    ("dn", 1, 0, "scalar"),
+    ("dn", 1, 1, "scalar"),
+    ("si", 1, 6),
+    ("mu", 0, 6),
+    ("mu", 1, 6),
+    ("dn", 2, 1, "scalar"),
+    ("qh", 0, 4),
+    ("dn", 4, 0, "scalar"),
+    ("qh", 1, 3),
+    ("qh", 0, 3),
+    ("dn", 4, 1, "vector"),
+    ("dn", 3, 1, "scalar"),
+    ("dn", 3, 0, "vector"),
+]
+
+
+def tile_picked_pick_glu_silu_srt_p_kernel(tc, x_words, x_scales, w1, w3, w2, offs, out):
+    nc = tc.nc
+    with ExitStack() as ctx:
+        keep = ctx.enter_context(tc.tile_pool(name="keep", bufs=1))
+        gates = ctx.enter_context(tc.tile_pool(name="gates", bufs=16))
+        psum = ctx.enter_context(tc.psum_pool(name="psum", bufs=8))
+
+        offsets = keep.tile([P, S // LIST_ROWS], U16, name="offsets")
+        word_table = keep.tile([P, T], I32, name="word_table")
+        scale_table = keep.tile([P, T], U8, name="scale_table")
+        warm = keep.tile([P, 8], F32, name="warm")
+        warm_out = keep.tile([P, 8], F32, name="warm_out")
+
+        nc.vector.memset(scale_table[:].bitcast(I32), 0)
+        nc.vector.memset(warm[:], 0.0)
+        nc.scalar.activation(warm_out[:], warm[:], SILU)
+
+        words_dram = x_words[0].rearrange("p n r -> p (n r)").bitcast(I32)
+        up_raw, down_raw = {}, {}
+
+        def window_cols(c):
+            return (c + 1) * CHUNK + T - S
+
+        def load(kind, *a):
+            if kind == "offs":
+                nc.sync.dma_start(offsets[:], offs)
+            elif kind == "scales":
+                for q in range(4):
+                    nc.sync.dma_start(scale_table[32 * q : 32 * q + 4, :].bitcast(I32), x_scales[0, 4 * q : 4 * q + 4, :].bitcast(I32))
+            elif kind == "x":
+                c0, c1 = a
+                lo = window_cols(c0 - 1) if c0 else 0
+                nc.sync.dma_start(word_table[:, lo : window_cols(c1)], words_dram[:, lo : window_cols(c1)])
+            elif kind == "up0":
+                name, half, parts = a
+                raw = keep.tile([P, PACK, HALF], F32, name="%s_raw0%d" % (name, half))
+                up_raw[name, 0, half] = raw
+                src = {"w1": w1, "w3": w3}[name][:, half * HALF : (half + 1) * HALF].rearrange("(p j) c -> p j c", j=PACK)
+                step = PACK // parts
+                for j in range(0, PACK, step):
+                    nc.sync.dma_start(raw[:, j : j + step, :], src[:, j : j + step, :])
+            elif kind == "up1":
+                name = a[0]
+                raw = keep.tile([P, PACK, PASS], F32, name="%s_raw1" % name)
+                up_raw[name, 1] = raw
+                nc.sync.dma_start(raw[:], {"w1": w1, "w3": w3}[name][:, PASS:].rearrange("(p j) c -> p j c", j=PACK))
+            else:
+                g = a[0]
+                down_raw[g] = keep.tile([P, PACK, N], F32, name="w2_raw%d" % g)
+                nc.sync.dma_start(down_raw[g][:], w2[g * PASS : (g + 1) * PASS, :].rearrange("(p j) n -> p j n", j=PACK))
+
+        for item in LOADS:
+            load(*item)
+
+        def copy_on(engine, dst, src):
+            if engine == "scalar":
+                nc.scalar.copy(dst, src)
+            else:
+                nc.vector.tensor_copy(dst, src)
+
+        up_codes, up_scales, up_bf = {}, {}, {}
+        for name in ("w1", "w3"):
+            for g in range(PASSES):
+                up_codes[name, g] = keep.tile([P, PASS], U32, name="%s_codes%d" % (name, g), align_bytes=64)
+                up_scales[name, g] = keep.tile([P, PASS], U8, name="%s_scales%d" % (name, g), align_bytes=64)
+        M_HALF = P // 2
+
+        def round_up(name, g, half, engine):
+            if g == 0:
+                bf = keep.tile([P, PACK, M_HALF, PACK], BF16, name="%s_bf%d%d" % (name, g, half), align_bytes=64)
+                src = up_raw[name, g, half][:].rearrange("p j (m t) -> p m j t", t=PACK)
+            else:
+                bf = keep.tile([P, 2, P, PACK], BF16, name="%s_bf%d%d" % (name, g, half), align_bytes=64)
+                src = up_raw[name, g][:].rearrange("p j (m t) -> p m j t", t=PACK)[:, :, :, 2 * half : 2 * half + 2]
+            up_bf[name, g, half] = bf
+            copy_on(engine, bf[:].rearrange("p t m j -> p m j t"), src)
+
+        def quantise_up(name, g, half):
+            bf = up_bf[name, g, half]
+            if g == 0:
+                pieces = [(slice(t * P + half * M_HALF, t * P + (half + 1) * M_HALF), bf[:, t, :, :].rearrange("p m j -> p (m j)")) for t in range(PACK)]
+            else:
+                pieces = [(slice(half * HALF, (half + 1) * HALF), bf[:].rearrange("p t m j -> p (t m j)"))]
+            for cols, src in pieces:
+                nc.vector.quantize_mx(out=up_codes[name, g][:, cols].bitcast(FP8X4), scales=up_scales[name, g][:, cols], in_=src)
+
+        down_codes, down_scales, down_bf = {}, {}, {}
+
+        def round_down(g, half, engine):
+            bf = keep.tile([P, HALF, PACK], BF16, name="w2_bf%d%d" % (g, half), align_bytes=64)
+            down_bf[g, half] = bf
+            src = down_raw[g][:, :, half * HALF : (half + 1) * HALF]
+            copy_on(engine, bf[:].rearrange("p (c i) j -> p c j i", i=4), src.rearrange("p j (c i) -> p c j i", i=4))
+
+        def quantise_down(g, half):
+            down_codes[g, half] = keep.tile([P, HALF], U32, name="w2_codes%d%d" % (g, half), align_bytes=64)
+            down_scales[g, half] = keep.tile([P, HALF], U8, name="w2_scales%d%d" % (g, half), align_bytes=64)
+            nc.vector.quantize_mx(
+                out=down_codes[g, half][:].bitcast(FP8X4),
+                scales=down_scales[g, half][:],
+                in_=down_bf[g, half][:].rearrange("p c j -> p (c j)"),
+            )
+
+        x_codes, x_bytes = {}, {}
+
+        def chunk_offsets(c):
+            return offsets[:, c * CHUNK // LIST_ROWS : (c + 1) * CHUNK // LIST_ROWS]
+
+        def gather_words(c):
+            x_codes[c] = keep.tile([P, CHUNK], U32, name="x_codes%d" % c, align_bytes=64)
+            width = window_cols(c)
+            nc.vector.tensor_copy(x_codes[c][:], word_table[:, :width].bitcast(U32).indirect(chunk_offsets(c)))
+
+        def gather_scales(c):
+            x_bytes[c] = keep.tile([P, CHUNK], U8, name="x_bytes%d" % c, align_bytes=64)
+            nc.vector.tensor_copy(x_bytes[c][:], scale_table[:].indirect(chunk_offsets(c)))
+
+        def up_product(name, g, s):
+            bank = psum.tile([P, PACK, SUB], F32, name="bank")
+            c, cols = divmod(s * SUB, CHUNK)
+            cols = slice(cols, cols + SUB)
+            for t in range(PACK):
+                nc.tensor.matmul_mx(
+                    out=bank[:, t, :],
+                    lhsT=up_codes[name, g][:, t * P : (t + 1) * P].bitcast(FP8X4),
+                    lhsT_scale=up_scales[name, g][:, t * P : (t + 1) * P],
+                    rhs=x_codes[c][:, cols].bitcast(FP8X4),
+                    rhs_scale=x_bytes[c][:, cols],
+                    start=True,
+                    stop=True,
+                )
+            return bank
+
+        gate = {}
+
+        def silu_step(g, s):
+            bank = up_product("w1", g, s)
+            gate[g, s] = gates.tile([P, SUB, PACK], F32, name="gate")
+            nc.scalar.activation(gate[g, s][:], bank[:].rearrange("p t n -> p n t"), SILU)
+
+        h_bf, h_codes, h_scales = {}, {}, {}
+        span_of = {}
+        for g in range(PASSES):
+            for c, (start, width) in enumerate(SPANS):
+                h_bf[g, c] = keep.tile([P, width, PACK], BF16, name="h_bf%d%d" % (g, c), align_bytes=64)
+                for s in range(start // SUB, (start + width) // SUB):
+                    span_of[s] = (c, s * SUB - start)
+
+        def mult_step(g, s):
+            bank = up_product("w3", g, s)
+            c, col = span_of[s]
+            nc.vector.tensor_tensor(h_bf[g, c][:, col : col + SUB, :], bank[:].rearrange("p t n -> p n t"), gate[g, s][:], MULT)
+
+        def quantise_h(g, c):
+            width = SPANS[c][1]
+            h_codes[g, c] = keep.tile([P, width], U32, name="h_codes%d%d" % (g, c), align_bytes=64)
+            h_scales[g, c] = keep.tile([P, width], U8, name="h_scales%d%d" % (g, c), align_bytes=64)
+            nc.vector.quantize_mx(
+                out=h_codes[g, c][:].bitcast(FP8X4),
+                scales=h_scales[g, c][:],
+                in_=h_bf[g, c][:].rearrange("p n j -> p (n j)"),
+            )
+
+        def down_step(c, half, engine):
+            start, width = SPANS[c]
+            bank = psum.tile([P, 2, width], F32, name="bank")
+            for mt in range(2):
+                for g in range(PASSES):
+                    nc.tensor.matmul_mx(
+                        out=bank[:, mt, :],
+                        lhsT=down_codes[g, half][:, mt * P : (mt + 1) * P].bitcast(FP8X4),
+                        lhsT_scale=down_scales[g, half][:, mt * P : (mt + 1) * P],
+                        rhs=h_codes[g, c][:].bitcast(FP8X4),
+                        rhs_scale=h_scales[g, c][:],
+                        start=(g == 0),
+                        stop=(g == PASSES - 1),
+                    )
+            y = keep.tile([P, 2, width], F32, name="y%d%d" % (c, half))
+            copy_on(engine, y[:], bank[:])
+            rows = out[half * HALF : (half + 1) * HALF, start : start + width]
+            nc.sync.dma_start(rows.rearrange("(mt p) n -> p mt n", p=P), y[:])
+
+        calls = {
+            "ru": round_up, "qu": quantise_up, "rd": round_down, "qd": quantise_down, "gw": gather_words, "gs": gather_scales,
+            "si": silu_step, "mu": mult_step, "qh": quantise_h, "dn": down_step,
+        }
+        for item in STEPS:
+            calls[item[0]](*item[1:])

@@ -23,110 +23,109 @@ HALF = PASS // 2
 CHUNK = 256
 CHUNKS = S // CHUNK
 SUB = 128
+BANKS = {"a": 3, "b": 3, "y": 2}
 SUBS = S // SUB
 LIST_ROWS = 16
 SPANS = [(0, 256), (256, 256), (512, 256), (768, 128), (896, 128)]
 LOADS = [
-    ("scales",),
-    ("x", 1, 1),
     ("offs",),
-    ("x", 0, 0),
-    ("up0", "w1", 1, 2),
+    ("up0", "w1", 1, 1),
+    ("scales",),
     ("up0", "w1", 0, 2),
-    ("x", 2, 2),
     ("up0", "w3", 0, 1),
+    ("x", 0, 1),
     ("up0", "w3", 1, 1),
+    ("x", 2, 3),
     ("up1", "w1"),
     ("up1", "w3"),
     ("down", 1),
-    ("x", 3, 3),
     ("down", 0),
 ]
 STEPS = [
-    ("ru", "w3", 0, 1, "vector"),
-    ("ru", "w1", 1, 1, "vector"),
-    ("ru", "w1", 0, 1, "scalar"),
-    ("gw", 0),
     ("ru", "w1", 0, 0, "scalar"),
-    ("qu", "w1", 1, 1),
-    ("ru", "w3", 0, 0, "scalar"),
-    ("ru", "w1", 1, 0, "scalar"),
-    ("qu", "w3", 0, 0),
-    ("gs", 1),
-    ("ru", "w3", 1, 1, "scalar"),
-    ("rd", 1, 1, "vector"),
+    ("gw", 0),
     ("qu", "w1", 0, 0),
-    ("gs", 2),
+    ("ru", "w3", 1, 0, "vector"),
+    ("gs", 1),
+    ("rd", 1, 0, "vector"),
+    ("ru", "w1", 0, 1, "vector"),
+    ("ru", "w3", 0, 0, "scalar"),
+    ("ru", "w3", 0, 1, "vector"),
     ("qu", "w1", 0, 1),
-    ("qu", "w1", 1, 0),
-    ("ru", "w3", 1, 0, "scalar"),
-    ("gs", 0),
-    ("qu", "w3", 1, 0),
-    ("si", 0, 0),
     ("gw", 1),
-    ("si", 0, 2),
-    ("qu", "w3", 0, 1),
-    ("rd", 0, 1, "scalar"),
-    ("gw", 3),
-    ("si", 1, 3),
-    ("si", 0, 3),
-    ("gs", 3),
-    ("si", 1, 1),
-    ("mu", 0, 2),
-    ("si", 0, 7),
-    ("si", 1, 0),
-    ("si", 0, 1),
-    ("si", 0, 6),
-    ("mu", 0, 1),
-    ("qu", "w3", 1, 1),
-    ("gw", 2),
-    ("mu", 1, 0),
-    ("mu", 1, 3),
-    ("si", 1, 5),
-    ("si", 1, 2),
-    ("mu", 1, 1),
-    ("si", 0, 5),
-    ("rd", 1, 0, "scalar"),
-    ("si", 0, 4),
-    ("qd", 0, 1),
-    ("qd", 1, 0),
-    ("mu", 0, 0),
-    ("mu", 0, 5),
-    ("si", 1, 7),
-    ("si", 1, 4),
-    ("mu", 0, 3),
-    ("qd", 1, 1),
-    ("mu", 0, 4),
-    ("qh", 1, 0),
-    ("mu", 1, 4),
-    ("mu", 1, 2),
-    ("qh", 0, 0),
-    ("rd", 0, 0, "vector"),
-    ("mu", 1, 5),
-    ("dn", 0, 1, "scalar"),
+    ("ru", "w3", 1, 1, "scalar"),
+    ("gs", 0),
+    ("rd", 0, 0, "scalar"),
+    ("rd", 1, 1, "scalar"),
     ("qd", 0, 0),
-    ("dn", 0, 0, "scalar"),
-    ("mu", 0, 7),
-    ("qh", 0, 2),
+    ("ru", "w1", 1, 0, "vector"),
+    ("si", 0, 0, "a"),
+    ("si", 0, 1, "a"),
+    ("qu", "w3", 0, 0),
+    ("si", 0, 2, "a"),
+    ("gw", 2),
+    ("qd", 1, 0),
+    ("gs", 2),
+    ("qu", "w3", 0, 1),
+    ("si", 0, 4, "a"),
+    ("mu", 0, 0, "b"),
+    ("gs", 3),
+    ("si", 0, 5, "a"),
+    ("qu", "w1", 1, 0),
+    ("qd", 1, 1),
+    ("ru", "w1", 1, 1, "scalar"),
+    ("qu", "w1", 1, 1),
+    ("mu", 0, 1, "b"),
+    ("mu", 0, 4, "b"),
+    ("si", 0, 3, "a"),
+    ("mu", 0, 2, "b"),
+    ("qh", 0, 0),
+    ("si", 1, 0, "a"),
+    ("qu", "w3", 1, 0),
+    ("si", 1, 2, "a"),
+    ("si", 1, 1, "a"),
+    ("qu", "w3", 1, 1),
+    ("mu", 1, 1, "b"),
+    ("si", 1, 3, "a"),
+    ("gw", 3),
+    ("mu", 0, 3, "b"),
+    ("mu", 1, 2, "b"),
+    ("si", 1, 4, "a"),
+    ("mu", 0, 5, "b"),
+    ("si", 1, 5, "a"),
+    ("mu", 1, 3, "b"),
+    ("si", 0, 6, "a"),
+    ("mu", 1, 0, "b"),
+    ("qh", 1, 0),
     ("qh", 1, 1),
-    ("qh", 1, 2),
-    ("mu", 1, 7),
-    ("qh", 1, 4),
+    ("rd", 0, 1, "scalar"),
+    ("mu", 1, 4, "b"),
+    ("si", 1, 6, "a"),
+    ("mu", 1, 6, "b"),
     ("qh", 0, 1),
-    ("dn", 2, 0, "scalar"),
-    ("dn", 1, 0, "scalar"),
-    ("dn", 1, 1, "scalar"),
-    ("si", 1, 6),
-    ("mu", 0, 6),
-    ("mu", 1, 6),
-    ("dn", 2, 1, "scalar"),
-    ("qh", 0, 4),
-    ("dn", 4, 0, "scalar"),
-    ("qh", 1, 3),
+    ("qd", 0, 1),
+    ("si", 0, 7, "a"),
+    ("mu", 1, 5, "b"),
+    ("dn", 0, 0, "scalar", "y"),
+    ("dn", 1, 0, "scalar", "y"),
+    ("qh", 0, 2),
+    ("si", 1, 7, "a"),
+    ("qh", 1, 2),
+    ("mu", 0, 6, "b"),
+    ("mu", 0, 7, "b"),
     ("qh", 0, 3),
-    ("dn", 4, 1, "vector"),
-    ("dn", 3, 1, "scalar"),
-    ("dn", 3, 0, "vector"),
+    ("qh", 1, 3),
+    ("mu", 1, 7, "b"),
+    ("dn", 1, 1, "scalar", "a"),
+    ("dn", 2, 1, "scalar", "a"),
+    ("dn", 0, 1, "scalar", "a"),
+    ("qh", 1, 4),
+    ("qh", 0, 4),
+    ("dn", 3, 0, "vector", "y"),
+    ("dn", 2, 0, "vector", "a"),
+    ("dn", 3, 1, "vector", "b"),
+    ("dn", 4, 0, "scalar", "y"),
+    ("dn", 4, 1, "scalar", "b"),
 ]
 
 
@@ -135,7 +134,7 @@ def tile_picked_pick_glu_silu_srt_p_kernel(tc, x_words, x_scales, w1, w3, w2, of
     with ExitStack() as ctx:
         keep = ctx.enter_context(tc.tile_pool(name="keep", bufs=1))
         gates = ctx.enter_context(tc.tile_pool(name="gates", bufs=16))
-        psum = ctx.enter_context(tc.psum_pool(name="psum", bufs=8))
+        psum = ctx.enter_context(tc.psum_pool(name="psum", bufs=1))
 
         offsets = keep.tile([P, S // LIST_ROWS], U16, name="offsets")
         word_table = keep.tile([P, T], I32, name="word_table")
@@ -247,8 +246,8 @@ def tile_picked_pick_glu_silu_srt_p_kernel(tc, x_words, x_scales, w1, w3, w2, of
             x_bytes[c] = keep.tile([P, CHUNK], U8, name="x_bytes%d" % c, align_bytes=64)
             nc.vector.tensor_copy(x_bytes[c][:], scale_table[:].indirect(chunk_offsets(c)))
 
-        def up_product(name, g, s):
-            bank = psum.tile([P, PACK, SUB], F32, name="bank")
+        def up_product(name, g, s, ring):
+            bank = psum.tile([P, PACK, SUB], F32, name=ring, bufs=BANKS[ring])
             c, cols = divmod(s * SUB, CHUNK)
             cols = slice(cols, cols + SUB)
             for t in range(PACK):
@@ -265,8 +264,8 @@ def tile_picked_pick_glu_silu_srt_p_kernel(tc, x_words, x_scales, w1, w3, w2, of
 
         gate = {}
 
-        def silu_step(g, s):
-            bank = up_product("w1", g, s)
+        def silu_step(g, s, ring):
+            bank = up_product("w1", g, s, ring)
             gate[g, s] = gates.tile([P, SUB, PACK], F32, name="gate")
             nc.scalar.activation(gate[g, s][:], bank[:].rearrange("p t n -> p n t"), SILU)
 
@@ -278,8 +277,8 @@ def tile_picked_pick_glu_silu_srt_p_kernel(tc, x_words, x_scales, w1, w3, w2, of
                 for s in range(start // SUB, (start + width) // SUB):
                     span_of[s] = (c, s * SUB - start)
 
-        def mult_step(g, s):
-            bank = up_product("w3", g, s)
+        def mult_step(g, s, ring):
+            bank = up_product("w3", g, s, ring)
             c, col = span_of[s]
             nc.vector.tensor_tensor(h_bf[g, c][:, col : col + SUB, :], bank[:].rearrange("p t n -> p n t"), gate[g, s][:], MULT)
 
@@ -293,9 +292,9 @@ def tile_picked_pick_glu_silu_srt_p_kernel(tc, x_words, x_scales, w1, w3, w2, of
                 in_=h_bf[g, c][:].rearrange("p n j -> p (n j)"),
             )
 
-        def down_step(c, half, engine):
+        def down_step(c, half, engine, ring):
             start, width = SPANS[c]
-            bank = psum.tile([P, 2, width], F32, name="bank")
+            bank = psum.tile([P, 2, width], F32, name=ring, bufs=BANKS[ring])
             for mt in range(2):
                 for g in range(PASSES):
                     nc.tensor.matmul_mx(

@@ -14,127 +14,31 @@ U8 = mybir.dt.uint8
 FP8X4 = mybir.dt.float8_e4m3fn_x4
 SILU = mybir.ActivationFunctionType.Silu
 MULT = mybir.AluOpType.mult
+ADD = mybir.AluOpType.add
 
 P = 128
 PACK = 4
 PASS = P * PACK
 PASSES = H // PASS
 HALF = PASS // 2
-CHUNK = 256
-CHUNKS = S // CHUNK
 SUB = 128
-BANKS = {"a": 3, "b": 3, "y": 2}
 SUBS = S // SUB
 LIST_ROWS = 16
-SPANS = [(0, 256), (256, 256), (512, 256), (768, 128), (896, 128)]
-LOADS = [
-    ("offs",),
-    ("up0", "w1", 1, 1),
-    ("scales",),
-    ("up0", "w1", 0, 2),
-    ("up0", "w3", 0, 1),
-    ("x", 0, 1),
-    ("up0", "w3", 1, 1),
-    ("x", 2, 3),
-    ("up1", "w1"),
-    ("up1", "w3"),
-    ("down", 1),
-    ("down", 0),
-]
-STEPS = [
-    ("ru", "w1", 0, 0, "scalar"),
-    ("gw", 0),
-    ("qu", "w1", 0, 0),
-    ("ru", "w3", 1, 0, "vector"),
-    ("gs", 1),
-    ("rd", 1, 0, "vector"),
-    ("ru", "w1", 0, 1, "vector"),
-    ("ru", "w3", 0, 0, "scalar"),
-    ("ru", "w3", 0, 1, "vector"),
-    ("qu", "w1", 0, 1),
-    ("gw", 1),
-    ("ru", "w3", 1, 1, "scalar"),
-    ("gs", 0),
-    ("rd", 0, 0, "scalar"),
-    ("rd", 1, 1, "scalar"),
-    ("qd", 0, 0),
-    ("ru", "w1", 1, 0, "vector"),
-    ("si", 0, 0, "a"),
-    ("si", 0, 1, "a"),
-    ("qu", "w3", 0, 0),
-    ("si", 0, 2, "a"),
-    ("gw", 2),
-    ("qd", 1, 0),
-    ("gs", 2),
-    ("qu", "w3", 0, 1),
-    ("si", 0, 4, "a"),
-    ("mu", 0, 0, "b"),
-    ("gs", 3),
-    ("si", 0, 5, "a"),
-    ("qu", "w1", 1, 0),
-    ("qd", 1, 1),
-    ("ru", "w1", 1, 1, "scalar"),
-    ("qu", "w1", 1, 1),
-    ("mu", 0, 1, "b"),
-    ("mu", 0, 4, "b"),
-    ("si", 0, 3, "a"),
-    ("mu", 0, 2, "b"),
-    ("qh", 0, 0),
-    ("si", 1, 0, "a"),
-    ("qu", "w3", 1, 0),
-    ("si", 1, 2, "a"),
-    ("si", 1, 1, "a"),
-    ("qu", "w3", 1, 1),
-    ("mu", 1, 1, "b"),
-    ("si", 1, 3, "a"),
-    ("gw", 3),
-    ("mu", 0, 3, "b"),
-    ("mu", 1, 2, "b"),
-    ("si", 1, 4, "a"),
-    ("mu", 0, 5, "b"),
-    ("si", 1, 5, "a"),
-    ("mu", 1, 3, "b"),
-    ("si", 0, 6, "a"),
-    ("mu", 1, 0, "b"),
-    ("qh", 1, 0),
-    ("qh", 1, 1),
-    ("rd", 0, 1, "scalar"),
-    ("mu", 1, 4, "b"),
-    ("si", 1, 6, "a"),
-    ("mu", 1, 6, "b"),
-    ("qh", 0, 1),
-    ("qd", 0, 1),
-    ("si", 0, 7, "a"),
-    ("mu", 1, 5, "b"),
-    ("dn", 0, 0, "scalar", "y"),
-    ("dn", 1, 0, "scalar", "y"),
-    ("qh", 0, 2),
-    ("si", 1, 7, "a"),
-    ("qh", 1, 2),
-    ("mu", 0, 6, "b"),
-    ("mu", 0, 7, "b"),
-    ("qh", 0, 3),
-    ("qh", 1, 3),
-    ("mu", 1, 7, "b"),
-    ("dn", 1, 1, "scalar", "a"),
-    ("dn", 2, 1, "scalar", "a"),
-    ("dn", 0, 1, "scalar", "a"),
-    ("qh", 1, 4),
-    ("qh", 0, 4),
-    ("dn", 3, 0, "vector", "y"),
-    ("dn", 2, 0, "vector", "a"),
-    ("dn", 3, 1, "vector", "b"),
-    ("dn", 4, 0, "scalar", "y"),
-    ("dn", 4, 1, "scalar", "b"),
-]
+CHUNK = 256
+CHUNKS = S // CHUNK
+BANKS = {"a": 3, "b": 3, "y": 2}
+SLOTS = {"scalar": 14, "vector": 36, "gpsimd": 4}
 
 
 def tile_picked_pick_glu_silu_srt_p_kernel(tc, x_words, x_scales, w1, w3, w2, offs, out):
     nc = tc.nc
     with ExitStack() as ctx:
         keep = ctx.enter_context(tc.tile_pool(name="keep", bufs=1))
-        gates = ctx.enter_context(tc.tile_pool(name="gates", bufs=16))
+        line = ctx.enter_context(tc.tile_pool(name="line", bufs=1))
         psum = ctx.enter_context(tc.psum_pool(name="psum", bufs=1))
+
+        def fresh(engine, shape, dtype, name):
+            return line.tile(shape, dtype, name=name, tag=engine, bufs=SLOTS[engine], align_bytes=64)
 
         offsets = keep.tile([P, S // LIST_ROWS], U16, name="offsets")
         word_table = keep.tile([P, T], I32, name="word_table")
@@ -144,88 +48,76 @@ def tile_picked_pick_glu_silu_srt_p_kernel(tc, x_words, x_scales, w1, w3, w2, of
 
         nc.vector.memset(scale_table[:].bitcast(I32), 0)
         nc.vector.memset(warm[:], 0.0)
-        nc.scalar.activation(warm_out[:], warm[:], SILU)
 
         words_dram = x_words[0].rearrange("p n r -> p (n r)").bitcast(I32)
+        up_dram = {"w1": w1, "w3": w3}
         up_raw, down_raw = {}, {}
 
-        def window_cols(c):
-            return (c + 1) * CHUNK + T - S
+        def load_scales():
+            for q in range(4):
+                nc.sync.dma_start(scale_table[32 * q : 32 * q + 4, :].bitcast(I32), x_scales[0, 4 * q : 4 * q + 4, :].bitcast(I32))
 
-        def load(kind, *a):
-            if kind == "offs":
-                nc.sync.dma_start(offsets[:], offs)
-            elif kind == "scales":
-                for q in range(4):
-                    nc.sync.dma_start(scale_table[32 * q : 32 * q + 4, :].bitcast(I32), x_scales[0, 4 * q : 4 * q + 4, :].bitcast(I32))
-            elif kind == "x":
-                c0, c1 = a
-                lo = window_cols(c0 - 1) if c0 else 0
-                nc.sync.dma_start(word_table[:, lo : window_cols(c1)], words_dram[:, lo : window_cols(c1)])
-            elif kind == "up0":
-                name, half, parts = a
-                raw = keep.tile([P, PACK, HALF], F32, name="%s_raw0%d" % (name, half))
-                up_raw[name, 0, half] = raw
-                src = {"w1": w1, "w3": w3}[name][:, half * HALF : (half + 1) * HALF].rearrange("(p j) c -> p j c", j=PACK)
-                step = PACK // parts
-                for j in range(0, PACK, step):
-                    nc.sync.dma_start(raw[:, j : j + step, :], src[:, j : j + step, :])
-            elif kind == "up1":
-                name = a[0]
-                raw = keep.tile([P, PACK, PASS], F32, name="%s_raw1" % name)
-                up_raw[name, 1] = raw
-                nc.sync.dma_start(raw[:], {"w1": w1, "w3": w3}[name][:, PASS:].rearrange("(p j) c -> p j c", j=PACK))
-            else:
-                g = a[0]
-                down_raw[g] = keep.tile([P, PACK, N], F32, name="w2_raw%d" % g)
-                nc.sync.dma_start(down_raw[g][:], w2[g * PASS : (g + 1) * PASS, :].rearrange("(p j) n -> p j n", j=PACK))
+        def load_words(lo, hi):
+            nc.sync.dma_start(word_table[:, lo:hi], words_dram[:, lo:hi])
 
-        for item in LOADS:
-            load(*item)
+        def load_up(name, g, lo, width):
+            raw = keep.tile([P, PACK, width], F32, name="%s_raw%d_%d" % (name, g, lo))
+            up_raw[name, g, lo] = raw
+            c0 = g * PASS + lo
+            nc.sync.dma_start(raw[:], up_dram[name][:, c0 : c0 + width].rearrange("(p j) c -> p j c", j=PACK))
+
+        def load_down(g):
+            raw = keep.tile([P, PACK, N], F32, name="w2_raw%d" % g)
+            down_raw[g] = raw
+            rows = w2[g * PASS : (g + 1) * PASS, :].rearrange("(b t r) n -> t b r n", t=PACK, r=PACK)
+            for t in range(PACK):
+                nc.sync.dma_start(raw[:, t, :], rows[t])
 
         def copy_on(engine, dst, src):
             if engine == "scalar":
                 nc.scalar.copy(dst, src)
+            elif engine == "gpsimd":
+                nc.gpsimd.tensor_copy(dst, src)
             else:
                 nc.vector.tensor_copy(dst, src)
 
-        up_codes, up_scales, up_bf = {}, {}, {}
-        for name in ("w1", "w3"):
-            for g in range(PASSES):
+        up_bf, up_codes, up_scales = {}, {}, {}
+        down_bf, down_codes, down_scales = {}, {}, {}
+        for g in range(PASSES):
+            for name in ("w1", "w3"):
                 up_codes[name, g] = keep.tile([P, PASS], U32, name="%s_codes%d" % (name, g), align_bytes=64)
-                up_scales[name, g] = keep.tile([P, PASS], U8, name="%s_scales%d" % (name, g), align_bytes=64)
-        M_HALF = P // 2
 
-        def round_up(name, g, half, engine):
-            if g == 0:
-                bf = keep.tile([P, PACK, M_HALF, PACK], BF16, name="%s_bf%d%d" % (name, g, half), align_bytes=64)
-                src = up_raw[name, g, half][:].rearrange("p j (m t) -> p m j t", t=PACK)
-            else:
-                bf = keep.tile([P, 2, P, PACK], BF16, name="%s_bf%d%d" % (name, g, half), align_bytes=64)
-                src = up_raw[name, g][:].rearrange("p j (m t) -> p m j t", t=PACK)[:, :, :, 2 * half : 2 * half + 2]
-            up_bf[name, g, half] = bf
-            copy_on(engine, bf[:].rearrange("p t m j -> p m j t"), src)
+        def round_up(name, g, raw_lo, lo, width, engine):
+            if (name, g) not in up_bf:
+                shape = [P, PACK, P, PACK]
+                if engine == "scalar":
+                    up_bf[name, g] = fresh(engine, shape, BF16, "%s_bf%d" % (name, g))
+                elif engine == "gpsimd" and name == "w1" or (name, g) == ("w3", 0):
+                    up_bf[name, g] = keep.tile(shape, BF16, name="%s_bf%d" % (name, g), tag="handover", align_bytes=64)
+                else:
+                    up_bf[name, g] = keep.tile(shape, BF16, name="%s_bf%d" % (name, g), align_bytes=64)
+            src = up_raw[name, g, raw_lo][:, :, lo - raw_lo : lo - raw_lo + width]
+            dst = up_bf[name, g][:, :, lo // PACK : (lo + width) // PACK, :]
+            walk = "p t b r j" if engine == "gpsimd" else "p b t j r"
+            copy_on(engine, dst.rearrange("p t (b r) j -> " + walk, r=PACK), src.rearrange("p j (b t r) -> " + walk, t=PACK, r=PACK))
 
-        def quantise_up(name, g, half):
-            bf = up_bf[name, g, half]
-            if g == 0:
-                pieces = [(slice(t * P + half * M_HALF, t * P + (half + 1) * M_HALF), bf[:, t, :, :].rearrange("p m j -> p (m j)")) for t in range(PACK)]
-            else:
-                pieces = [(slice(half * HALF, (half + 1) * HALF), bf[:].rearrange("p t m j -> p (t m j)"))]
-            for cols, src in pieces:
-                nc.vector.quantize_mx(out=up_codes[name, g][:, cols].bitcast(FP8X4), scales=up_scales[name, g][:, cols], in_=src)
-
-        down_codes, down_scales, down_bf = {}, {}, {}
+        def quantise_up(name, g):
+            up_scales[name, g] = fresh("vector", [P, PASS], U8, "%s_scales%d" % (name, g))
+            nc.vector.quantize_mx(
+                out=up_codes[name, g][:].bitcast(FP8X4),
+                scales=up_scales[name, g][:],
+                in_=up_bf[name, g][:].rearrange("p t m j -> p (t m j)"),
+            )
 
         def round_down(g, half, engine):
-            bf = keep.tile([P, HALF, PACK], BF16, name="w2_bf%d%d" % (g, half), align_bytes=64)
-            down_bf[g, half] = bf
             src = down_raw[g][:, :, half * HALF : (half + 1) * HALF]
-            copy_on(engine, bf[:].rearrange("p (c i) j -> p c j i", i=4), src.rearrange("p j (c i) -> p c j i", i=4))
+            down_bf[g, half] = fresh(engine, [P, HALF, PACK], BF16, "w2_bf%d%d" % (g, half))
+            walk = "p c i j" if engine == "gpsimd" else "p c j i"
+            copy_on(engine, down_bf[g, half][:].rearrange("p (c i) j -> " + walk, i=PACK), src.rearrange("p j (c i) -> " + walk, i=PACK))
 
         def quantise_down(g, half):
             down_codes[g, half] = keep.tile([P, HALF], U32, name="w2_codes%d%d" % (g, half), align_bytes=64)
-            down_scales[g, half] = keep.tile([P, HALF], U8, name="w2_scales%d%d" % (g, half), align_bytes=64)
+            down_scales[g, half] = fresh("vector", [P, HALF], U8, "w2_scales%d%d" % (g, half))
             nc.vector.quantize_mx(
                 out=down_codes[g, half][:].bitcast(FP8X4),
                 scales=down_scales[g, half][:],
@@ -234,86 +126,209 @@ def tile_picked_pick_glu_silu_srt_p_kernel(tc, x_words, x_scales, w1, w3, w2, of
 
         x_codes, x_bytes = {}, {}
 
-        def chunk_offsets(c):
-            return offsets[:, c * CHUNK // LIST_ROWS : (c + 1) * CHUNK // LIST_ROWS]
+        def list_slice(lo, width):
+            return offsets[:, lo // LIST_ROWS : (lo + width) // LIST_ROWS]
 
-        def gather_words(c):
-            x_codes[c] = keep.tile([P, CHUNK], U32, name="x_codes%d" % c, align_bytes=64)
-            width = window_cols(c)
-            nc.vector.tensor_copy(x_codes[c][:], word_table[:, :width].bitcast(U32).indirect(chunk_offsets(c)))
+        def gather_words(lo, width):
+            tile = fresh("vector", [P, width], U32, "x_codes%d" % lo)
+            for s in range(lo // SUB, (lo + width) // SUB):
+                x_codes[s] = tile[:, s * SUB - lo : (s + 1) * SUB - lo]
+            nc.vector.tensor_copy(tile[:], word_table[:, : lo + width + T - S].bitcast(U32).indirect(list_slice(lo, width)))
 
-        def gather_scales(c):
-            x_bytes[c] = keep.tile([P, CHUNK], U8, name="x_bytes%d" % c, align_bytes=64)
-            nc.vector.tensor_copy(x_bytes[c][:], scale_table[:].indirect(chunk_offsets(c)))
+        def gather_scales(lo, width):
+            tile = fresh("vector", [P, width], U8, "x_bytes%d" % lo)
+            for s in range(lo // SUB, (lo + width) // SUB):
+                x_bytes[s] = tile[:, s * SUB - lo : (s + 1) * SUB - lo]
+            nc.vector.tensor_copy(tile[:], scale_table[:].indirect(list_slice(lo, width)))
 
-        def up_product(name, g, s, ring):
-            bank = psum.tile([P, PACK, SUB], F32, name=ring, bufs=BANKS[ring])
-            c, cols = divmod(s * SUB, CHUNK)
-            cols = slice(cols, cols + SUB)
+        banks = {}
+
+        def up_product(name, g, s):
+            bank = psum.tile([P, PACK, SUB], F32, name="bank", bufs=8)
+            banks[name, g, s] = bank
             for t in range(PACK):
                 nc.tensor.matmul_mx(
                     out=bank[:, t, :],
                     lhsT=up_codes[name, g][:, t * P : (t + 1) * P].bitcast(FP8X4),
                     lhsT_scale=up_scales[name, g][:, t * P : (t + 1) * P],
-                    rhs=x_codes[c][:, cols].bitcast(FP8X4),
-                    rhs_scale=x_bytes[c][:, cols],
+                    rhs=x_codes[s].bitcast(FP8X4),
+                    rhs_scale=x_bytes[s],
                     start=True,
                     stop=True,
                 )
-            return bank
+
+        def prod_a(g, s):
+            up_product("w1", g, s)
+
+        def prod_b(g, s):
+            up_product("w3", g, s)
 
         gate = {}
 
-        def silu_step(g, s, ring):
-            bank = up_product("w1", g, s, ring)
-            gate[g, s] = gates.tile([P, SUB, PACK], F32, name="gate")
+        def silu(g, s):
+            bank = banks["w1", g, s]
+            gate[g, s] = fresh("scalar", [P, SUB, PACK], F32, "gate%d%d" % (g, s))
             nc.scalar.activation(gate[g, s][:], bank[:].rearrange("p t n -> p n t"), SILU)
 
         h_bf, h_codes, h_scales = {}, {}, {}
-        span_of = {}
-        for g in range(PASSES):
-            for c, (start, width) in enumerate(SPANS):
-                h_bf[g, c] = keep.tile([P, width, PACK], BF16, name="h_bf%d%d" % (g, c), align_bytes=64)
-                for s in range(start // SUB, (start + width) // SUB):
-                    span_of[s] = (c, s * SUB - start)
 
-        def mult_step(g, s, ring):
-            bank = up_product("w3", g, s, ring)
-            c, col = span_of[s]
-            nc.vector.tensor_tensor(h_bf[g, c][:, col : col + SUB, :], bank[:].rearrange("p t n -> p n t"), gate[g, s][:], MULT)
+        def mult(g, s):
+            bank = banks["w3", g, s]
+            c, part = divmod(s, CHUNK // SUB)
+            if part == 0:
+                h_bf[g, c] = fresh("vector", [P, CHUNK * PACK], BF16, "h_bf%d%d" % (g, c))
+            dst = h_bf[g, c][:, part * PASS : (part + 1) * PASS].rearrange("p (n t) -> p n t", t=PACK)
+            nc.vector.tensor_tensor(dst, bank[:].rearrange("p t n -> p n t"), gate[g, s][:], MULT)
 
-        def quantise_h(g, c):
-            width = SPANS[c][1]
-            h_codes[g, c] = keep.tile([P, width], U32, name="h_codes%d%d" % (g, c), align_bytes=64)
-            h_scales[g, c] = keep.tile([P, width], U8, name="h_scales%d%d" % (g, c), align_bytes=64)
-            nc.vector.quantize_mx(
-                out=h_codes[g, c][:].bitcast(FP8X4),
-                scales=h_scales[g, c][:],
-                in_=h_bf[g, c][:].rearrange("p n j -> p (n j)"),
-            )
+        def quantise_h(g, lo, width):
+            c, col = divmod(lo, CHUNK)
+            codes = keep.tile([P, width], U32, name="h_codes%d_%d" % (g, lo), align_bytes=64)
+            scales = fresh("vector", [P, width], U8, "h_scales%d_%d" % (g, lo))
+            for at in range(0, width, SUB):
+                h_codes[g, lo + at], h_scales[g, lo + at] = codes[:, at:], scales[:, at:]
+            nc.vector.quantize_mx(out=codes[:].bitcast(FP8X4), scales=scales[:], in_=h_bf[g, c][:, col * PACK : (col + width) * PACK])
 
-        def down_step(c, half, engine, ring):
-            start, width = SPANS[c]
-            bank = psum.tile([P, 2, width], F32, name=ring, bufs=BANKS[ring])
+        def prod_y(lo, width, half):
+            bank = psum.tile([P, 2, width], F32, name="bank", bufs=8)
+            banks["y", lo, half] = bank
             for mt in range(2):
                 for g in range(PASSES):
+                    cols = slice(mt * P, (mt + 1) * P)
                     nc.tensor.matmul_mx(
                         out=bank[:, mt, :],
-                        lhsT=down_codes[g, half][:, mt * P : (mt + 1) * P].bitcast(FP8X4),
-                        lhsT_scale=down_scales[g, half][:, mt * P : (mt + 1) * P],
-                        rhs=h_codes[g, c][:].bitcast(FP8X4),
-                        rhs_scale=h_scales[g, c][:],
+                        lhsT=down_codes[g, half][:, cols].bitcast(FP8X4),
+                        lhsT_scale=down_scales[g, half][:, cols],
+                        rhs=h_codes[g, lo][:, :width].bitcast(FP8X4),
+                        rhs_scale=h_scales[g, lo][:, :width],
                         start=(g == 0),
                         stop=(g == PASSES - 1),
                     )
-            y = keep.tile([P, 2, width], F32, name="y%d%d" % (c, half))
+
+        def out_y(lo, width, half, engine):
+            bank = banks["y", lo, half]
+            y = fresh(engine, [P, 2, width], F32, "y%d_%d" % (lo, half))
             copy_on(engine, y[:], bank[:])
-            rows = out[half * HALF : (half + 1) * HALF, start : start + width]
+            rows = out[half * HALF : (half + 1) * HALF, lo : lo + width]
             nc.sync.dma_start(rows.rearrange("(mt p) n -> p mt n", p=P), y[:])
 
-        calls = {
-            "ru": round_up, "qu": quantise_up, "rd": round_down, "qd": quantise_down, "gw": gather_words, "gs": gather_scales,
-            "si": silu_step, "mu": mult_step, "qh": quantise_h, "dn": down_step,
-        }
-        for item in STEPS:
-            calls[item[0]](*item[1:])
+        def clock(src, dtype, name):
+            tick = keep.tile([P, 1], dtype, name=name)
+            nc.gpsimd.tensor_copy(tick[:], src)
+
+        nc.scalar.activation(warm_out[:], warm[:], SILU)
+        nc.sync.dma_start(offsets[:], offs)
+        load_up("w1", 0, 0, HALF)
+        load_scales()
+        load_up("w1", 0, HALF, HALF)
+        load_words(0, 2 * CHUNK + T - S)
+        load_up("w3", 0, 0, HALF)
+        load_words(2 * CHUNK + T - S, T)
+        load_up("w3", 0, HALF, HALF)
+        load_up("w1", 1, 0, PASS)
+        load_up("w3", 1, 0, PASS)
+        load_down(0)
+        load_down(1)
+
+        gather_scales(0, S)
+        round_up("w1", 0, 0, 0, HALF, "scalar")
+        round_up("w1", 0, HALF, HALF, HALF, "scalar")
+        quantise_up("w1", 0)
+        gather_words(0, CHUNK)
+        gather_words(CHUNK, CHUNK)
+        round_up("w3", 0, 0, 0, HALF, "scalar")
+        gather_words(2 * CHUNK, CHUNK)
+        round_up("w3", 0, HALF, HALF, HALF, "vector")
+        quantise_up("w3", 0)
+        gather_words(3 * CHUNK, CHUNK)
+        for s in range(6):
+            prod_a(0, s)
+        for s in range(5):
+            silu(0, s)
+        prod_b(0, 0)
+        prod_b(0, 1)
+        prod_a(0, 6)
+        prod_a(0, 7)
+        prod_b(0, 2)
+        prod_b(0, 3)
+        round_up("w1", 1, 0, 0, PASS, "scalar")
+        for s in range(4):
+            mult(0, s)
+        quantise_up("w1", 1)
+        for s in range(5, 8):
+            silu(0, s)
+        for s in range(4, 8):
+            prod_b(0, s)
+        prod_a(1, 0)
+        prod_a(1, 1)
+        round_up("w3", 1, 0, 0, HALF, "vector")
+        round_up("w3", 1, 0, HALF, HALF, "scalar")
+        for s in range(4, 8):
+            mult(0, s)
+        quantise_up("w3", 1)
+        prod_a(1, 2)
+        prod_a(1, 3)
+        silu(1, 0)
+        silu(1, 1)
+        prod_b(1, 0)
+        prod_b(1, 1)
+        round_down(0, 0, "vector")
+        round_down(1, 0, "scalar")
+        round_down(0, 1, "scalar")
+        quantise_h(0, 0, CHUNK)
+        mult(1, 0)
+        mult(1, 1)
+        prod_a(1, 4)
+        prod_a(1, 5)
+        prod_b(1, 2)
+        prod_b(1, 3)
+        quantise_down(0, 0)
+        quantise_down(1, 0)
+        quantise_h(1, 0, CHUNK)
+        quantise_h(0, CHUNK, CHUNK)
+        silu(1, 2)
+        silu(1, 3)
+        prod_y(0, CHUNK, 0)
+        round_down(1, 1, "scalar")
+        prod_a(1, 6)
+        prod_a(1, 7)
+        mult(1, 2)
+        mult(1, 3)
+        prod_b(1, 4)
+        prod_b(1, 5)
+        silu(1, 4)
+        silu(1, 5)
+        quantise_down(0, 1)
+        quantise_h(1, CHUNK, CHUNK)
+        quantise_down(1, 1)
+        quantise_h(0, 2 * CHUNK, CHUNK)
+        out_y(0, CHUNK, 0, "scalar")
+        prod_y(CHUNK, CHUNK, 0)
+        prod_b(1, 6)
+        prod_b(1, 7)
+        prod_y(0, CHUNK, 1)
+        silu(1, 6)
+        silu(1, 7)
+        mult(1, 4)
+        mult(1, 5)
+        prod_y(CHUNK, CHUNK, 1)
+        quantise_h(0, 3 * CHUNK, CHUNK)
+        quantise_h(1, 2 * CHUNK, CHUNK)
+        out_y(CHUNK, CHUNK, 0, "scalar")
+        out_y(0, CHUNK, 1, "scalar")
+        out_y(CHUNK, CHUNK, 1, "scalar")
+        prod_y(2 * CHUNK, CHUNK, 0)
+        prod_y(2 * CHUNK, CHUNK, 1)
+        mult(1, 6)
+        mult(1, 7)
+        quantise_h(1, 6 * SUB, SUB)
+        quantise_h(1, 7 * SUB, SUB)
+        out_y(2 * CHUNK, CHUNK, 0, "scalar")
+        out_y(2 * CHUNK, CHUNK, 1, "vector")
+        prod_y(6 * SUB, SUB, 0)
+        prod_y(6 * SUB, SUB, 1)
+        prod_y(7 * SUB, SUB, 0)
+        prod_y(7 * SUB, SUB, 1)
+        out_y(6 * SUB, SUB, 0, "scalar")
+        out_y(6 * SUB, SUB, 1, "vector")
+        out_y(7 * SUB, SUB, 0, "scalar")
+        out_y(7 * SUB, SUB, 1, "vector")

@@ -28,6 +28,7 @@ CHUNK = 256
 CHUNKS = S // CHUNK
 BANKS = {"a": 3, "b": 3, "y": 2}
 SLOTS = {"scalar": 14, "vector": 36, "gpsimd": 4}
+PAIR = 2
 
 
 def tile_picked_pick_glu_silu_srt_p_kernel(tc, x_words, x_scales, w1, w3, w2, offs, out):
@@ -69,7 +70,7 @@ def tile_picked_pick_glu_silu_srt_p_kernel(tc, x_words, x_scales, w1, w3, w2, of
         def load_down(g):
             raw = keep.tile([P, PACK, N], F32, name="w2_raw%d" % g)
             down_raw[g] = raw
-            rows = w2[g * PASS : (g + 1) * PASS, :].rearrange("(b t r) n -> t b r n", t=PACK, r=PACK)
+            rows = w2[g * PASS : (g + 1) * PASS, :].rearrange("(b t r) n -> t b r n", t=PACK, r=PAIR)
             for t in range(PACK):
                 nc.sync.dma_start(raw[:, t, :], rows[t])
 
@@ -99,7 +100,7 @@ def tile_picked_pick_glu_silu_srt_p_kernel(tc, x_words, x_scales, w1, w3, w2, of
             src = up_raw[name, g, raw_lo][:, :, lo - raw_lo : lo - raw_lo + width]
             dst = up_bf[name, g][:, :, lo // PACK : (lo + width) // PACK, :]
             walk = "p t b r j" if engine == "gpsimd" else "p b t j r"
-            copy_on(engine, dst.rearrange("p t (b r) j -> " + walk, r=PACK), src.rearrange("p j (b t r) -> " + walk, t=PACK, r=PACK))
+            copy_on(engine, dst.rearrange("p t (b r) j -> " + walk, r=PAIR), src.rearrange("p j (b t r) -> " + walk, t=PACK, r=PAIR))
 
         def quantise_up(name, g):
             up_scales[name, g] = fresh("vector", [P, PASS], U8, "%s_scales%d" % (name, g))
@@ -113,7 +114,7 @@ def tile_picked_pick_glu_silu_srt_p_kernel(tc, x_words, x_scales, w1, w3, w2, of
             src = down_raw[g][:, :, half * HALF : (half + 1) * HALF]
             down_bf[g, half] = fresh(engine, [P, HALF, PACK], BF16, "w2_bf%d%d" % (g, half))
             walk = "p c i j" if engine == "gpsimd" else "p c j i"
-            copy_on(engine, down_bf[g, half][:].rearrange("p (c i) j -> " + walk, i=PACK), src.rearrange("p j (c i) -> " + walk, i=PACK))
+            copy_on(engine, down_bf[g, half][:].rearrange("p (c i) j -> " + walk, i=PAIR), src.rearrange("p j (c i) -> " + walk, i=PAIR))
 
         def quantise_down(g, half):
             down_codes[g, half] = keep.tile([P, HALF], U32, name="w2_codes%d%d" % (g, half), align_bytes=64)

@@ -70,9 +70,7 @@ def tile_picked_pick_glu_silu_srt_p_kernel(tc, x_words, x_scales, w1, w3, w2, of
         def load_down(g):
             raw = keep.tile([P, PACK, N], F32, name="w2_raw%d" % g)
             down_raw[g] = raw
-            rows = w2[g * PASS : (g + 1) * PASS, :].rearrange("(b t r) n -> t b r n", t=PACK, r=PAIR)
-            for t in range(PACK):
-                nc.sync.dma_start(raw[:, t, :], rows[t])
+            nc.sync.dma_start(raw[:], w2[g * PASS : (g + 1) * PASS, :].rearrange("(p j) n -> p j n", j=PACK))
 
         def copy_on(engine, dst, src):
             if engine == "scalar":
@@ -99,8 +97,7 @@ def tile_picked_pick_glu_silu_srt_p_kernel(tc, x_words, x_scales, w1, w3, w2, of
                     up_bf[name, g] = keep.tile(shape, BF16, name="%s_bf%d" % (name, g), align_bytes=64)
             src = up_raw[name, g, raw_lo][:, :, lo - raw_lo : lo - raw_lo + width]
             dst = up_bf[name, g][:, :, lo // PACK : (lo + width) // PACK, :]
-            walk = "p t b r j" if engine == "gpsimd" else "p b t j r"
-            copy_on(engine, dst.rearrange("p t (b r) j -> " + walk, r=PAIR), src.rearrange("p j (b t r) -> " + walk, t=PACK, r=PAIR))
+            copy_on(engine, dst.rearrange("p t m j -> p m j t"), src.rearrange("p j (m t) -> p m j t", t=PACK))
 
         def quantise_up(name, g):
             up_scales[name, g] = fresh("vector", [P, PASS], U8, "%s_scales%d" % (name, g))
@@ -232,11 +229,11 @@ def tile_picked_pick_glu_silu_srt_p_kernel(tc, x_words, x_scales, w1, w3, w2, of
 
         gather_scales(0, S)
         round_up("w1", 0, 0, 0, HALF, "scalar")
-        round_up("w1", 0, HALF, HALF, HALF, "scalar")
+        round_up("w1", 0, HALF, HALF, HALF, "vector")
         quantise_up("w1", 0)
         gather_words(0, CHUNK)
         gather_words(CHUNK, CHUNK)
-        round_up("w3", 0, 0, 0, HALF, "scalar")
+        round_up("w3", 0, 0, 0, HALF, "vector")
         gather_words(2 * CHUNK, CHUNK)
         round_up("w3", 0, HALF, HALF, HALF, "vector")
         quantise_up("w3", 0)
@@ -251,85 +248,75 @@ def tile_picked_pick_glu_silu_srt_p_kernel(tc, x_words, x_scales, w1, w3, w2, of
         prod_a(0, 7)
         prod_b(0, 2)
         prod_b(0, 3)
-        round_up("w1", 1, 0, 0, PASS, "scalar")
-        for s in range(4):
-            mult(0, s)
-        quantise_up("w1", 1)
+        round_up("w1", 1, 0, 0, HALF, "scalar")
         for s in range(5, 8):
             silu(0, s)
+        mult(0, 0)
+        mult(0, 1)
+        round_up("w1", 1, 0, HALF, HALF, "vector")
         for s in range(4, 8):
             prod_b(0, s)
-        prod_a(1, 0)
-        prod_a(1, 1)
-        round_up("w3", 1, 0, 0, HALF, "vector")
-        round_up("w3", 1, 0, HALF, HALF, "scalar")
-        for s in range(4, 8):
+        mult(0, 2)
+        quantise_up("w1", 1)
+        round_up("w3", 1, 0, 0, HALF, "scalar")
+        for s in range(3, 6):
             mult(0, s)
+        for s in range(4):
+            prod_a(1, s)
+        round_up("w3", 1, 0, HALF, HALF, "vector")
+        mult(0, 6)
         quantise_up("w3", 1)
-        prod_a(1, 2)
-        prod_a(1, 3)
-        silu(1, 0)
-        silu(1, 1)
-        prod_b(1, 0)
-        prod_b(1, 1)
-        round_down(0, 0, "vector")
-        round_down(1, 0, "scalar")
+        mult(0, 7)
+
+        for s in range(2):
+            silu(1, s)
+            prod_b(1, s)
+        round_down(0, 0, "scalar")
         round_down(0, 1, "scalar")
         quantise_h(0, 0, CHUNK)
-        mult(1, 0)
-        mult(1, 1)
-        prod_a(1, 4)
-        prod_a(1, 5)
-        prod_b(1, 2)
-        prod_b(1, 3)
-        quantise_down(0, 0)
-        quantise_down(1, 0)
-        quantise_h(1, 0, CHUNK)
-        quantise_h(0, CHUNK, CHUNK)
-        silu(1, 2)
-        silu(1, 3)
-        prod_y(0, CHUNK, 0)
-        round_down(1, 1, "scalar")
-        prod_a(1, 6)
-        prod_a(1, 7)
-        mult(1, 2)
-        mult(1, 3)
-        prod_b(1, 4)
-        prod_b(1, 5)
-        silu(1, 4)
-        silu(1, 5)
-        quantise_down(0, 1)
-        quantise_h(1, CHUNK, CHUNK)
-        quantise_down(1, 1)
-        quantise_h(0, 2 * CHUNK, CHUNK)
-        out_y(0, CHUNK, 0, "scalar")
-        prod_y(CHUNK, CHUNK, 0)
-        prod_b(1, 6)
-        prod_b(1, 7)
-        prod_y(0, CHUNK, 1)
-        silu(1, 6)
-        silu(1, 7)
-        mult(1, 4)
-        mult(1, 5)
-        prod_y(CHUNK, CHUNK, 1)
-        quantise_h(0, 3 * CHUNK, CHUNK)
-        quantise_h(1, 2 * CHUNK, CHUNK)
-        out_y(CHUNK, CHUNK, 0, "scalar")
-        out_y(0, CHUNK, 1, "scalar")
-        out_y(CHUNK, CHUNK, 1, "scalar")
-        prod_y(2 * CHUNK, CHUNK, 0)
-        prod_y(2 * CHUNK, CHUNK, 1)
+        for s in range(2, 4):
+            silu(1, s)
+            prod_b(1, s)
+        for c in range(CHUNKS - 1):
+            later = range(2 * c + 4, min(2 * c + 6, SUBS))
+            for s in later:
+                prod_a(1, s)
+            mult(1, 2 * c)
+            mult(1, 2 * c + 1)
+            for s in later:
+                prod_b(1, s)
+            if c == 0:
+                round_down(1, 0, "vector")
+                round_down(1, 1, "scalar")
+            else:
+                out_y((c - 1) * CHUNK, CHUNK, 0, "scalar")
+                out_y((c - 1) * CHUNK, CHUNK, 1, "scalar")
+            for s in later:
+                silu(1, s)
+            if c == 0:
+                quantise_h(1, 0, CHUNK)
+                for half in range(2):
+                    quantise_down(0, half)
+                    quantise_down(1, half)
+                    prod_y(0, CHUNK, half)
+                quantise_h(0, CHUNK, CHUNK)
+            else:
+                if c + 1 < CHUNKS - 1:
+                    quantise_h(0, (c + 1) * CHUNK, CHUNK)
+                quantise_h(1, c * CHUNK, CHUNK)
+                prod_y(c * CHUNK, CHUNK, 0)
+                prod_y(c * CHUNK, CHUNK, 1)
         mult(1, 6)
-        mult(1, 7)
-        quantise_h(1, 6 * SUB, SUB)
-        quantise_h(1, 7 * SUB, SUB)
         out_y(2 * CHUNK, CHUNK, 0, "scalar")
-        out_y(2 * CHUNK, CHUNK, 1, "vector")
+        out_y(2 * CHUNK, CHUNK, 1, "scalar")
+        quantise_h(0, 3 * CHUNK, CHUNK)
+        quantise_h(1, 6 * SUB, SUB)
         prod_y(6 * SUB, SUB, 0)
         prod_y(6 * SUB, SUB, 1)
+        mult(1, 7)
+        quantise_h(1, 7 * SUB, SUB)
         prod_y(7 * SUB, SUB, 0)
         prod_y(7 * SUB, SUB, 1)
-        out_y(6 * SUB, SUB, 0, "scalar")
-        out_y(6 * SUB, SUB, 1, "vector")
-        out_y(7 * SUB, SUB, 0, "scalar")
-        out_y(7 * SUB, SUB, 1, "vector")
+        for s in (6, 7):
+            out_y(s * SUB, SUB, 0, "vector")
+            out_y(s * SUB, SUB, 1, "scalar")

@@ -76,7 +76,7 @@ def tile_picked_pick_glu_silu_srt_p_kernel(tc, x_words, x_scales, w1, w3, w2, of
             if engine == "scalar":
                 nc.scalar.copy(dst, src)
             elif engine == "gpsimd":
-                nc.gpsimd.tensor_copy(dst, src)
+                nc.gpsimd.tensor_scalar(dst, src, 1.0, 0.0, MULT, ADD)
             else:
                 nc.vector.tensor_copy(dst, src)
 
@@ -89,9 +89,9 @@ def tile_picked_pick_glu_silu_srt_p_kernel(tc, x_words, x_scales, w1, w3, w2, of
         def round_up(name, g, raw_lo, lo, width, engine):
             if (name, g) not in up_bf:
                 shape = [P, PACK, P, PACK]
-                if engine == "scalar":
+                if engine == "scalar" and (name, g) != ("w3", 1):
                     up_bf[name, g] = fresh(engine, shape, BF16, "%s_bf%d" % (name, g))
-                elif engine == "gpsimd" and name == "w1" or (name, g) == ("w3", 0):
+                elif (name, g) == ("w3", 1):
                     up_bf[name, g] = keep.tile(shape, BF16, name="%s_bf%d" % (name, g), tag="handover", align_bytes=64)
                 else:
                     up_bf[name, g] = keep.tile(shape, BF16, name="%s_bf%d" % (name, g), align_bytes=64)
@@ -109,7 +109,10 @@ def tile_picked_pick_glu_silu_srt_p_kernel(tc, x_words, x_scales, w1, w3, w2, of
 
         def round_down(g, half, engine):
             src = down_raw[g][:, :, half * HALF : (half + 1) * HALF]
-            down_bf[g, half] = fresh(engine, [P, HALF, PACK], BF16, "w2_bf%d%d" % (g, half))
+            if (g, half) == (0, 0):
+                down_bf[g, half] = keep.tile([P, HALF, PACK], BF16, name="w2_bf00", tag="handover", align_bytes=64)
+            else:
+                down_bf[g, half] = fresh(engine, [P, HALF, PACK], BF16, "w2_bf%d%d" % (g, half))
             walk = "p c i j" if engine == "gpsimd" else "p c j i"
             copy_on(engine, down_bf[g, half][:].rearrange("p (c i) j -> " + walk, i=PAIR), src.rearrange("p j (c i) -> " + walk, i=PAIR))
 
@@ -219,8 +222,8 @@ def tile_picked_pick_glu_silu_srt_p_kernel(tc, x_words, x_scales, w1, w3, w2, of
         load_scales()
         load_up("w1", 0, HALF, HALF)
         load_words(0, 2 * CHUNK + T - S)
-        load_up("w3", 0, 0, HALF)
         load_words(2 * CHUNK + T - S, T)
+        load_up("w3", 0, 0, HALF)
         load_up("w3", 0, HALF, HALF)
         load_up("w1", 1, 0, PASS)
         load_up("w3", 1, 0, PASS)
@@ -229,94 +232,78 @@ def tile_picked_pick_glu_silu_srt_p_kernel(tc, x_words, x_scales, w1, w3, w2, of
 
         gather_scales(0, S)
         round_up("w1", 0, 0, 0, HALF, "scalar")
-        round_up("w1", 0, HALF, HALF, HALF, "vector")
+        round_up("w1", 0, HALF, HALF, HALF, "scalar")
         quantise_up("w1", 0)
-        gather_words(0, CHUNK)
-        gather_words(CHUNK, CHUNK)
+        for c in range(CHUNKS):
+            gather_words(c * CHUNK, CHUNK)
         round_up("w3", 0, 0, 0, HALF, "vector")
-        gather_words(2 * CHUNK, CHUNK)
         round_up("w3", 0, HALF, HALF, HALF, "vector")
         quantise_up("w3", 0)
-        gather_words(3 * CHUNK, CHUNK)
-        for s in range(6):
+        for s in range(SUBS):
             prod_a(0, s)
-        for s in range(5):
             silu(0, s)
-        prod_b(0, 0)
-        prod_b(0, 1)
-        prod_a(0, 6)
-        prod_a(0, 7)
-        prod_b(0, 2)
-        prod_b(0, 3)
-        round_up("w1", 1, 0, 0, HALF, "scalar")
-        for s in range(5, 8):
-            silu(0, s)
-        mult(0, 0)
-        mult(0, 1)
-        round_up("w1", 1, 0, HALF, HALF, "vector")
-        for s in range(4, 8):
-            prod_b(0, s)
-        mult(0, 2)
-        quantise_up("w1", 1)
+        round_up("w1", 1, 0, 0, PASS, "scalar")
         round_up("w3", 1, 0, 0, HALF, "scalar")
-        for s in range(3, 6):
+        for s in range(SUBS):
+            prod_b(0, s)
+        for s in range(5):
             mult(0, s)
+        quantise_up("w1", 1)
         for s in range(4):
             prod_a(1, s)
+        mult(0, 5)
         round_up("w3", 1, 0, HALF, HALF, "vector")
         mult(0, 6)
         quantise_up("w3", 1)
         mult(0, 7)
 
-        for s in range(2):
+        round_down(0, 0, "gpsimd")
+        round_down(0, 1, "gpsimd")
+        prod_a(1, 4)
+        prod_a(1, 5)
+        for s in range(6):
             silu(1, s)
+        for s in range(4):
             prod_b(1, s)
-        round_down(0, 0, "scalar")
-        round_down(0, 1, "scalar")
+        prod_a(1, 6)
+        prod_a(1, 7)
+        for s in range(4):
+            mult(1, s)
+            prod_b(1, s + 4)
+        round_down(1, 0, "scalar")
+        round_down(1, 1, "scalar")
+        silu(1, 6)
+        silu(1, 7)
         quantise_h(0, 0, CHUNK)
-        for s in range(2, 4):
-            silu(1, s)
-            prod_b(1, s)
-        for c in range(CHUNKS - 1):
-            later = range(2 * c + 4, min(2 * c + 6, SUBS))
-            for s in later:
-                prod_a(1, s)
-            mult(1, 2 * c)
-            mult(1, 2 * c + 1)
-            for s in later:
-                prod_b(1, s)
-            if c == 0:
-                round_down(1, 0, "vector")
-                round_down(1, 1, "scalar")
-            else:
-                out_y((c - 1) * CHUNK, CHUNK, 0, "scalar")
-                out_y((c - 1) * CHUNK, CHUNK, 1, "scalar")
-            for s in later:
-                silu(1, s)
-            if c == 0:
-                quantise_h(1, 0, CHUNK)
-                for half in range(2):
-                    quantise_down(0, half)
-                    quantise_down(1, half)
-                    prod_y(0, CHUNK, half)
-                quantise_h(0, CHUNK, CHUNK)
-            else:
-                if c + 1 < CHUNKS - 1:
-                    quantise_h(0, (c + 1) * CHUNK, CHUNK)
-                quantise_h(1, c * CHUNK, CHUNK)
-                prod_y(c * CHUNK, CHUNK, 0)
-                prod_y(c * CHUNK, CHUNK, 1)
+        quantise_h(1, 0, CHUNK)
+        quantise_down(0, 0)
+        quantise_down(1, 0)
+        prod_y(0, CHUNK, 0)
+        quantise_h(0, CHUNK, CHUNK)
+        quantise_h(1, CHUNK, CHUNK)
+        prod_y(CHUNK, CHUNK, 0)
+        quantise_down(0, 1)
+        quantise_down(1, 1)
+        prod_y(0, CHUNK, 1)
+        prod_y(CHUNK, CHUNK, 1)
+        for half in range(2):
+            for c in range(2):
+                out_y(c * CHUNK, CHUNK, half, "scalar")
+        mult(1, 4)
+        mult(1, 5)
+        quantise_h(0, 2 * CHUNK, CHUNK)
+        quantise_h(1, 2 * CHUNK, CHUNK)
+        for half in range(2):
+            prod_y(2 * CHUNK, CHUNK, half)
+            out_y(2 * CHUNK, CHUNK, half, "scalar")
         mult(1, 6)
-        out_y(2 * CHUNK, CHUNK, 0, "scalar")
-        out_y(2 * CHUNK, CHUNK, 1, "scalar")
         quantise_h(0, 3 * CHUNK, CHUNK)
         quantise_h(1, 6 * SUB, SUB)
-        prod_y(6 * SUB, SUB, 0)
-        prod_y(6 * SUB, SUB, 1)
         mult(1, 7)
         quantise_h(1, 7 * SUB, SUB)
-        prod_y(7 * SUB, SUB, 0)
-        prod_y(7 * SUB, SUB, 1)
+        for s in (6, 7):
+            for half in range(2):
+                prod_y(s * SUB, SUB, half)
         for s in (6, 7):
             out_y(s * SUB, SUB, 0, "vector")
             out_y(s * SUB, SUB, 1, "scalar")

@@ -20,15 +20,20 @@ P = 128
 PACK = 4
 PASS = P * PACK
 PASSES = H // PASS
-HALF = PASS // 2
-SUB = 128
-SUBS = S // SUB
-LIST_ROWS = 16
+HALF = 256
+PAIR = 2
+SLICE = 128
+SLICES = S // SLICE
 CHUNK = 256
 CHUNKS = S // CHUNK
-BANKS = {"a": 3, "b": 3, "y": 2}
-SLOTS = {"scalar": 14, "vector": 36, "gpsimd": 4}
-PAIR = 2
+LIST_ROWS = 16
+BANKS = 8
+SLOTS = {"scalar": 14, "vector": 36}
+GPSIMD_COLUMNS = 320
+MULTS_BEFORE_LOW = 4
+MULTS_BEFORE_HIGH = 5
+EARLY_GATES = 6
+EARLY_MULTS = 4
 
 
 def tile_picked_pick_glu_silu_srt_p_kernel(tc, x_words, x_scales, w1, w3, w2, offs, out):
@@ -38,8 +43,11 @@ def tile_picked_pick_glu_silu_srt_p_kernel(tc, x_words, x_scales, w1, w3, w2, of
         line = ctx.enter_context(tc.tile_pool(name="line", bufs=1))
         psum = ctx.enter_context(tc.psum_pool(name="psum", bufs=1))
 
-        def fresh(engine, shape, dtype, name):
+        def in_line(engine, shape, dtype, name):
             return line.tile(shape, dtype, name=name, tag=engine, bufs=SLOTS[engine], align_bytes=64)
+
+        def handed_over(shape, name):
+            return keep.tile(shape, BF16, name=name, tag="handover", align_bytes=64)
 
         offsets = keep.tile([P, S // LIST_ROWS], U16, name="offsets")
         word_table = keep.tile([P, T], I32, name="word_table")
@@ -49,261 +57,236 @@ def tile_picked_pick_glu_silu_srt_p_kernel(tc, x_words, x_scales, w1, w3, w2, of
 
         nc.vector.memset(scale_table[:].bitcast(I32), 0)
         nc.vector.memset(warm[:], 0.0)
+        nc.scalar.activation(warm_out[:], warm[:], SILU)
 
         words_dram = x_words[0].rearrange("p n r -> p (n r)").bitcast(I32)
         up_dram = {"w1": w1, "w3": w3}
         up_raw, down_raw = {}, {}
 
-        def load_scales():
-            for q in range(4):
-                nc.sync.dma_start(scale_table[32 * q : 32 * q + 4, :].bitcast(I32), x_scales[0, 4 * q : 4 * q + 4, :].bitcast(I32))
-
-        def load_words(lo, hi):
-            nc.sync.dma_start(word_table[:, lo:hi], words_dram[:, lo:hi])
+        def window(chunks):
+            return chunks * CHUNK + T - S
 
         def load_up(name, g, lo, width):
-            raw = keep.tile([P, PACK, width], F32, name="%s_raw%d_%d" % (name, g, lo))
-            up_raw[name, g, lo] = raw
-            c0 = g * PASS + lo
-            nc.sync.dma_start(raw[:], up_dram[name][:, c0 : c0 + width].rearrange("(p j) c -> p j c", j=PACK))
+            up_raw[name, g, lo] = keep.tile([P, PACK, width], F32, name="%s_raw%d_%d" % (name, g, lo))
+            columns = up_dram[name][:, g * PASS + lo : g * PASS + lo + width]
+            nc.sync.dma_start(up_raw[name, g, lo][:], columns.rearrange("(p j) c -> p j c", j=PACK))
 
-        def load_down(g):
-            raw = keep.tile([P, PACK, N], F32, name="w2_raw%d" % g)
-            down_raw[g] = raw
-            nc.sync.dma_start(raw[:], w2[g * PASS : (g + 1) * PASS, :].rearrange("(p j) n -> p j n", j=PACK))
+        nc.sync.dma_start(offsets[:], offs)
+        load_up("w1", 0, 0, HALF)
+        for q in range(4):
+            nc.sync.dma_start(scale_table[32 * q : 32 * q + 4, :].bitcast(I32), x_scales[0, 4 * q : 4 * q + 4, :].bitcast(I32))
+        load_up("w1", 0, HALF, HALF)
+        nc.sync.dma_start(word_table[:, : window(CHUNKS // 2)], words_dram[:, : window(CHUNKS // 2)])
+        nc.sync.dma_start(word_table[:, window(CHUNKS // 2) :], words_dram[:, window(CHUNKS // 2) :])
+        load_up("w3", 0, 0, HALF)
+        load_up("w3", 0, HALF, HALF)
+        load_up("w1", 1, 0, PASS)
+        load_up("w3", 1, 0, PASS)
+        for g in range(PASSES):
+            down_raw[g] = keep.tile([P, PACK, N], F32, name="w2_raw%d" % g)
+            nc.sync.dma_start(down_raw[g][:], w2[g * PASS : (g + 1) * PASS, :].rearrange("(p j) n -> p j n", j=PACK))
 
         def copy_on(engine, dst, src):
             if engine == "scalar":
                 nc.scalar.copy(dst, src)
-            elif engine == "gpsimd":
-                nc.gpsimd.tensor_scalar(dst, src, 1.0, 0.0, MULT, ADD)
             else:
                 nc.vector.tensor_copy(dst, src)
 
-        up_bf, up_codes, up_scales = {}, {}, {}
-        down_bf, down_codes, down_scales = {}, {}, {}
-        for g in range(PASSES):
-            for name in ("w1", "w3"):
-                up_codes[name, g] = keep.tile([P, PASS], U32, name="%s_codes%d" % (name, g), align_bytes=64)
+        def quantise(codes, src, name):
+            scales = in_line("vector", list(codes.shape), U8, name)
+            nc.vector.quantize_mx(out=codes.bitcast(FP8X4), scales=scales[:], in_=src)
+            return scales
 
-        def round_up(name, g, raw_lo, lo, width, engine):
-            if (name, g) not in up_bf:
-                shape = [P, PACK, P, PACK]
-                if engine == "scalar" and (name, g) != ("w3", 1):
-                    up_bf[name, g] = fresh(engine, shape, BF16, "%s_bf%d" % (name, g))
-                elif (name, g) == ("w3", 1):
-                    up_bf[name, g] = keep.tile(shape, BF16, name="%s_bf%d" % (name, g), tag="handover", align_bytes=64)
-                else:
-                    up_bf[name, g] = keep.tile(shape, BF16, name="%s_bf%d" % (name, g), align_bytes=64)
-            src = up_raw[name, g, raw_lo][:, :, lo - raw_lo : lo - raw_lo + width]
-            dst = up_bf[name, g][:, :, lo // PACK : (lo + width) // PACK, :]
-            copy_on(engine, dst.rearrange("p t m j -> p m j t"), src.rearrange("p j (m t) -> p m j t", t=PACK))
+        def round_up(engine, dst, raw, slots):
+            copy_on(engine, dst.rearrange("p t m j -> p m j t"), raw.rearrange("p j (m t) -> p m j t", t=PACK)[:, :, :, slots])
 
-        def quantise_up(name, g):
-            up_scales[name, g] = fresh("vector", [P, PASS], U8, "%s_scales%d" % (name, g))
-            nc.vector.quantize_mx(
-                out=up_codes[name, g][:].bitcast(FP8X4),
-                scales=up_scales[name, g][:],
-                in_=up_bf[name, g][:].rearrange("p t m j -> p (t m j)"),
-            )
+        up_codes, up_scales = {}, {}
 
-        def round_down(g, half, engine):
-            src = down_raw[g][:, :, half * HALF : (half + 1) * HALF]
-            if (g, half) == (0, 0):
-                down_bf[g, half] = keep.tile([P, HALF, PACK], BF16, name="w2_bf00", tag="handover", align_bytes=64)
+        def quantise_up(name, g, rounded, first_slot):
+            slots = rounded.shape[1]
+            codes = keep.tile([P, slots * P], U32, name="%s_codes%d%d" % (name, g, first_slot), align_bytes=64)
+            scales = quantise(codes[:], rounded[:].rearrange("p t m j -> p (t m j)"), "%s_scales%d%d" % (name, g, first_slot))
+            for t in range(slots):
+                up_codes[name, g, first_slot + t] = codes[:, t * P : (t + 1) * P]
+                up_scales[name, g, first_slot + t] = scales[:, t * P : (t + 1) * P]
+
+        down_rounded, down_codes, down_scales = {}, {}, {}
+
+        def round_down(engine, g, half, lo, hi):
+            dst = down_rounded[g, half][:, lo:hi, :]
+            src = down_raw[g][:, :, half * HALF + lo : half * HALF + hi]
+            if engine == "gpsimd":
+                nc.gpsimd.tensor_scalar(dst, src.rearrange("p j c -> p c j"), 1.0, 0.0, MULT, ADD)
             else:
-                down_bf[g, half] = fresh(engine, [P, HALF, PACK], BF16, "w2_bf%d%d" % (g, half))
-            walk = "p c i j" if engine == "gpsimd" else "p c j i"
-            copy_on(engine, down_bf[g, half][:].rearrange("p (c i) j -> " + walk, i=PAIR), src.rearrange("p j (c i) -> " + walk, i=PAIR))
+                copy_on(engine, dst.rearrange("p (c i) j -> p c j i", i=PAIR), src.rearrange("p j (c i) -> p c j i", i=PAIR))
 
         def quantise_down(g, half):
             down_codes[g, half] = keep.tile([P, HALF], U32, name="w2_codes%d%d" % (g, half), align_bytes=64)
-            down_scales[g, half] = fresh("vector", [P, HALF], U8, "w2_scales%d%d" % (g, half))
-            nc.vector.quantize_mx(
-                out=down_codes[g, half][:].bitcast(FP8X4),
-                scales=down_scales[g, half][:],
-                in_=down_bf[g, half][:].rearrange("p c j -> p (c j)"),
-            )
+            src = down_rounded[g, half][:].rearrange("p c j -> p (c j)")
+            down_scales[g, half] = quantise(down_codes[g, half][:], src, "w2_scales%d%d" % (g, half))
 
-        x_codes, x_bytes = {}, {}
+        x_codes, banks, gate = {}, {}, {}
 
-        def list_slice(lo, width):
-            return offsets[:, lo // LIST_ROWS : (lo + width) // LIST_ROWS]
+        def gather_words(c):
+            x_codes[c] = in_line("vector", [P, CHUNK], U32, "x_codes%d" % c)
+            entries = offsets[:, c * CHUNK // LIST_ROWS : (c + 1) * CHUNK // LIST_ROWS]
+            nc.vector.tensor_copy(x_codes[c][:], word_table[:, : window(c + 1)].bitcast(U32).indirect(entries))
 
-        def gather_words(lo, width):
-            tile = fresh("vector", [P, width], U32, "x_codes%d" % lo)
-            for s in range(lo // SUB, (lo + width) // SUB):
-                x_codes[s] = tile[:, s * SUB - lo : (s + 1) * SUB - lo]
-            nc.vector.tensor_copy(tile[:], word_table[:, : lo + width + T - S].bitcast(U32).indirect(list_slice(lo, width)))
-
-        def gather_scales(lo, width):
-            tile = fresh("vector", [P, width], U8, "x_bytes%d" % lo)
-            for s in range(lo // SUB, (lo + width) // SUB):
-                x_bytes[s] = tile[:, s * SUB - lo : (s + 1) * SUB - lo]
-            nc.vector.tensor_copy(tile[:], scale_table[:].indirect(list_slice(lo, width)))
-
-        banks = {}
-
-        def up_product(name, g, s):
-            bank = psum.tile([P, PACK, SUB], F32, name="bank", bufs=8)
-            banks[name, g, s] = bank
-            for t in range(PACK):
+        def up_product(name, g, s, slots=range(PACK)):
+            if slots[0] == 0:
+                banks[name, g, s] = psum.tile([P, PACK, SLICE], F32, name="bank", bufs=BANKS)
+            c, col = divmod(s * SLICE, CHUNK)
+            for t in slots:
                 nc.tensor.matmul_mx(
-                    out=bank[:, t, :],
-                    lhsT=up_codes[name, g][:, t * P : (t + 1) * P].bitcast(FP8X4),
-                    lhsT_scale=up_scales[name, g][:, t * P : (t + 1) * P],
-                    rhs=x_codes[s].bitcast(FP8X4),
-                    rhs_scale=x_bytes[s],
+                    out=banks[name, g, s][:, t, :],
+                    lhsT=up_codes[name, g, t].bitcast(FP8X4),
+                    lhsT_scale=up_scales[name, g, t],
+                    rhs=x_codes[c][:, col : col + SLICE].bitcast(FP8X4),
+                    rhs_scale=x_bytes[:, s * SLICE : (s + 1) * SLICE],
                     start=True,
                     stop=True,
                 )
 
-        def prod_a(g, s):
-            up_product("w1", g, s)
-
-        def prod_b(g, s):
-            up_product("w3", g, s)
-
-        gate = {}
-
         def silu(g, s):
-            bank = banks["w1", g, s]
-            gate[g, s] = fresh("scalar", [P, SUB, PACK], F32, "gate%d%d" % (g, s))
-            nc.scalar.activation(gate[g, s][:], bank[:].rearrange("p t n -> p n t"), SILU)
+            gate[g, s] = in_line("scalar", [P, SLICE, PACK], F32, "gate%d%d" % (g, s))
+            nc.scalar.activation(gate[g, s][:], banks["w1", g, s][:].rearrange("p t n -> p n t"), SILU)
 
-        h_bf, h_codes, h_scales = {}, {}, {}
+        h_rounded, h_codes, h_scales = {}, {}, {}
 
         def mult(g, s):
-            bank = banks["w3", g, s]
-            c, part = divmod(s, CHUNK // SUB)
-            if part == 0:
-                h_bf[g, c] = fresh("vector", [P, CHUNK * PACK], BF16, "h_bf%d%d" % (g, c))
-            dst = h_bf[g, c][:, part * PASS : (part + 1) * PASS].rearrange("p (n t) -> p n t", t=PACK)
-            nc.vector.tensor_tensor(dst, bank[:].rearrange("p t n -> p n t"), gate[g, s][:], MULT)
+            c, col = divmod(s * SLICE, CHUNK)
+            if col == 0:
+                h_rounded[g, c] = in_line("vector", [P, CHUNK, PACK], BF16, "h_rounded%d%d" % (g, c))
+            nc.vector.tensor_tensor(h_rounded[g, c][:, col : col + SLICE, :], banks["w3", g, s][:].rearrange("p t n -> p n t"), gate[g, s][:], MULT)
 
         def quantise_h(g, lo, width):
             c, col = divmod(lo, CHUNK)
             codes = keep.tile([P, width], U32, name="h_codes%d_%d" % (g, lo), align_bytes=64)
-            scales = fresh("vector", [P, width], U8, "h_scales%d_%d" % (g, lo))
-            for at in range(0, width, SUB):
+            src = h_rounded[g, c][:, col : col + width, :].rearrange("p n t -> p (n t)")
+            scales = quantise(codes[:], src, "h_scales%d_%d" % (g, lo))
+            for at in range(0, width, SLICE):
                 h_codes[g, lo + at], h_scales[g, lo + at] = codes[:, at:], scales[:, at:]
-            nc.vector.quantize_mx(out=codes[:].bitcast(FP8X4), scales=scales[:], in_=h_bf[g, c][:, col * PACK : (col + width) * PACK])
 
-        def prod_y(lo, width, half):
-            bank = psum.tile([P, 2, width], F32, name="bank", bufs=8)
-            banks["y", lo, half] = bank
-            for mt in range(2):
+        def down_product(lo, width, half):
+            banks["w2", lo, half] = psum.tile([P, HALF // P, width], F32, name="bank", bufs=BANKS)
+            for r in range(HALF // P):
                 for g in range(PASSES):
-                    cols = slice(mt * P, (mt + 1) * P)
                     nc.tensor.matmul_mx(
-                        out=bank[:, mt, :],
-                        lhsT=down_codes[g, half][:, cols].bitcast(FP8X4),
-                        lhsT_scale=down_scales[g, half][:, cols],
+                        out=banks["w2", lo, half][:, r, :],
+                        lhsT=down_codes[g, half][:, r * P : (r + 1) * P].bitcast(FP8X4),
+                        lhsT_scale=down_scales[g, half][:, r * P : (r + 1) * P],
                         rhs=h_codes[g, lo][:, :width].bitcast(FP8X4),
                         rhs_scale=h_scales[g, lo][:, :width],
                         start=(g == 0),
                         stop=(g == PASSES - 1),
                     )
 
-        def out_y(lo, width, half, engine):
-            bank = banks["y", lo, half]
-            y = fresh(engine, [P, 2, width], F32, "y%d_%d" % (lo, half))
-            copy_on(engine, y[:], bank[:])
+        def store(engine, lo, width, half):
+            y = in_line(engine, [P, HALF // P, width], F32, "y%d_%d" % (lo, half))
+            copy_on(engine, y[:], banks["w2", lo, half][:])
             rows = out[half * HALF : (half + 1) * HALF, lo : lo + width]
-            nc.sync.dma_start(rows.rearrange("(mt p) n -> p mt n", p=P), y[:])
+            nc.sync.dma_start(rows.rearrange("(r p) n -> p r n", p=P), y[:])
 
-        def clock(src, dtype, name):
-            tick = keep.tile([P, 1], dtype, name=name)
-            nc.gpsimd.tensor_copy(tick[:], src)
+        all_slots = slice(0, PACK)
+        half_m = HALF // PACK
 
-        nc.scalar.activation(warm_out[:], warm[:], SILU)
-        nc.sync.dma_start(offsets[:], offs)
-        load_up("w1", 0, 0, HALF)
-        load_scales()
-        load_up("w1", 0, HALF, HALF)
-        load_words(0, 2 * CHUNK + T - S)
-        load_words(2 * CHUNK + T - S, T)
-        load_up("w3", 0, 0, HALF)
-        load_up("w3", 0, HALF, HALF)
-        load_up("w1", 1, 0, PASS)
-        load_up("w3", 1, 0, PASS)
-        load_down(0)
-        load_down(1)
-
-        gather_scales(0, S)
-        round_up("w1", 0, 0, 0, HALF, "scalar")
-        round_up("w1", 0, HALF, HALF, HALF, "scalar")
-        quantise_up("w1", 0)
+        x_bytes = in_line("vector", [P, S], U8, "x_bytes")
+        nc.vector.tensor_copy(x_bytes[:], scale_table[:].indirect(offsets[:]))
+        w1_first = in_line("scalar", [P, PACK, P, PACK], BF16, "w1_first")
+        for half in range(2):
+            round_up("scalar", w1_first[:, :, half * half_m : (half + 1) * half_m, :], up_raw["w1", 0, half * HALF][:], all_slots)
+        quantise_up("w1", 0, w1_first, 0)
         for c in range(CHUNKS):
-            gather_words(c * CHUNK, CHUNK)
-        round_up("w3", 0, 0, 0, HALF, "vector")
-        round_up("w3", 0, HALF, HALF, HALF, "vector")
-        quantise_up("w3", 0)
-        for s in range(SUBS):
-            prod_a(0, s)
+            gather_words(c)
+        w3_first = keep.tile([P, PACK, P, PACK], BF16, name="w3_first", align_bytes=64)
+        for half in range(2):
+            round_up("vector", w3_first[:, :, half * half_m : (half + 1) * half_m, :], up_raw["w3", 0, half * HALF][:], all_slots)
+        quantise_up("w3", 0, w3_first, 0)
+        for s in range(SLICES):
+            up_product("w1", 0, s)
             silu(0, s)
-        round_up("w1", 1, 0, 0, PASS, "scalar")
-        round_up("w3", 1, 0, 0, HALF, "scalar")
-        for s in range(SUBS):
-            prod_b(0, s)
-        for s in range(5):
-            mult(0, s)
-        quantise_up("w1", 1)
-        for s in range(4):
-            prod_a(1, s)
-        mult(0, 5)
-        round_up("w3", 1, 0, HALF, HALF, "vector")
-        mult(0, 6)
-        quantise_up("w3", 1)
-        mult(0, 7)
 
-        round_down(0, 0, "gpsimd")
-        round_down(0, 1, "gpsimd")
-        prod_a(1, 4)
-        prod_a(1, 5)
-        for s in range(6):
+        w1_low = in_line("scalar", [P, PAIR, P, PACK], BF16, "w1_low")
+        round_up("scalar", w1_low[:], up_raw["w1", 1, 0][:], slice(0, PAIR))
+        w1_high = in_line("scalar", [P, PAIR, P, PACK], BF16, "w1_high")
+        round_up("scalar", w1_high[:], up_raw["w1", 1, 0][:], slice(PAIR, PACK))
+        w3_low = in_line("scalar", [P, PAIR, P, PACK], BF16, "w3_low")
+        round_up("scalar", w3_low[:], up_raw["w3", 1, 0][:], slice(0, PAIR))
+        for s in range(SLICES):
+            up_product("w3", 0, s)
+        for s in range(MULTS_BEFORE_LOW):
+            mult(0, s)
+        quantise_up("w1", 1, w1_low, 0)
+        for s in range(MULTS_BEFORE_LOW):
+            up_product("w1", 1, s, range(PAIR))
+        for s in range(MULTS_BEFORE_LOW, MULTS_BEFORE_HIGH):
+            mult(0, s)
+        quantise_up("w1", 1, w1_high, PAIR)
+        for s in range(MULTS_BEFORE_LOW):
+            up_product("w1", 1, s, range(PAIR, PACK))
+        for s in range(MULTS_BEFORE_LOW, EARLY_GATES):
+            up_product("w1", 1, s)
+        mult(0, SLICES - 3)
+        w3_high = handed_over([P, PAIR, P, PACK], "w3_high")
+        round_up("vector", w3_high[:], up_raw["w3", 1, 0][:], slice(PAIR, PACK))
+        mult(0, SLICES - 2)
+        quantise_up("w3", 1, w3_low, 0)
+        quantise_up("w3", 1, w3_high, PAIR)
+        mult(0, SLICES - 1)
+
+        last = SLICES - 1
+        down_rounded[0, 0] = handed_over([P, HALF, PACK], "w2_rounded00")
+        round_down("gpsimd", 0, 0, 0, HALF)
+        for s in range(EARLY_GATES):
             silu(1, s)
-        for s in range(4):
-            prod_b(1, s)
-        prod_a(1, 6)
-        prod_a(1, 7)
-        for s in range(4):
+        for s in range(EARLY_MULTS):
+            up_product("w3", 1, s)
+        for s in range(EARLY_GATES, SLICES):
+            up_product("w1", 1, s)
+        for s in range(EARLY_MULTS, SLICES):
+            up_product("w3", 1, s)
+        for s in range(EARLY_MULTS):
             mult(1, s)
-            prod_b(1, s + 4)
-        round_down(1, 0, "scalar")
-        round_down(1, 1, "scalar")
-        silu(1, 6)
-        silu(1, 7)
-        quantise_h(0, 0, CHUNK)
-        quantise_h(1, 0, CHUNK)
-        quantise_down(0, 0)
-        quantise_down(1, 0)
-        prod_y(0, CHUNK, 0)
-        quantise_h(0, CHUNK, CHUNK)
-        quantise_h(1, CHUNK, CHUNK)
-        prod_y(CHUNK, CHUNK, 0)
-        quantise_down(0, 1)
-        quantise_down(1, 1)
-        prod_y(0, CHUNK, 1)
-        prod_y(CHUNK, CHUNK, 1)
+        down_rounded[0, 1] = in_line("scalar", [P, HALF, PACK], BF16, "w2_rounded01")
+        round_down("scalar", 0, 1, GPSIMD_COLUMNS - HALF, HALF)
+        round_down("gpsimd", 0, 1, 0, GPSIMD_COLUMNS - HALF)
+        for half in range(2):
+            down_rounded[1, half] = in_line("scalar", [P, HALF, PACK], BF16, "w2_rounded1%d" % half)
+            round_down("scalar", 1, half, 0, HALF)
+        for s in range(EARLY_GATES, SLICES):
+            silu(1, s)
+
+        for c in range(2):
+            for g in range(PASSES):
+                quantise_h(g, c * CHUNK, CHUNK)
+            if c == 0:
+                for g in range(PASSES):
+                    quantise_down(g, 0)
+            down_product(c * CHUNK, CHUNK, 0)
+        for g in range(PASSES):
+            quantise_down(g, 1)
+        for c in range(2):
+            down_product(c * CHUNK, CHUNK, 1)
         for half in range(2):
             for c in range(2):
-                out_y(c * CHUNK, CHUNK, half, "scalar")
-        mult(1, 4)
-        mult(1, 5)
-        quantise_h(0, 2 * CHUNK, CHUNK)
-        quantise_h(1, 2 * CHUNK, CHUNK)
+                store("scalar", c * CHUNK, CHUNK, half)
+
+        for s in range(EARLY_MULTS, last - 1):
+            mult(1, s)
+        for g in range(PASSES):
+            quantise_h(g, 2 * CHUNK, CHUNK)
         for half in range(2):
-            prod_y(2 * CHUNK, CHUNK, half)
-            out_y(2 * CHUNK, CHUNK, half, "scalar")
-        mult(1, 6)
+            down_product(2 * CHUNK, CHUNK, half)
+            store("scalar", 2 * CHUNK, CHUNK, half)
+
+        mult(1, last - 1)
         quantise_h(0, 3 * CHUNK, CHUNK)
-        quantise_h(1, 6 * SUB, SUB)
-        mult(1, 7)
-        quantise_h(1, 7 * SUB, SUB)
-        for s in (6, 7):
+        quantise_h(1, (last - 1) * SLICE, SLICE)
+        mult(1, last)
+        quantise_h(1, last * SLICE, SLICE)
+        for s in (last - 1, last):
             for half in range(2):
-                prod_y(s * SUB, SUB, half)
-        for s in (6, 7):
-            out_y(s * SUB, SUB, 0, "vector")
-            out_y(s * SUB, SUB, 1, "scalar")
+                down_product(s * SLICE, SLICE, half)
+        for s in (last - 1, last):
+            store("vector", s * SLICE, SLICE, 0)
+            store("scalar", s * SLICE, SLICE, 1)

@@ -29,7 +29,6 @@ CHUNKS = S // CHUNK
 LIST_ROWS = 16
 BANKS = 8
 SLOTS = {"scalar": 14, "vector": 36}
-GPSIMD_COLUMNS = 320
 MULTS_BEFORE_LOW = 4
 MULTS_BEFORE_HIGH = 5
 EARLY_GATES = 6
@@ -46,8 +45,8 @@ def tile_picked_pick_glu_silu_srt_p_kernel(tc, x_words, x_scales, w1, w3, w2, of
         def in_line(engine, shape, dtype, name):
             return line.tile(shape, dtype, name=name, tag=engine, bufs=SLOTS[engine], align_bytes=64)
 
-        def handed_over(shape, name):
-            return keep.tile(shape, BF16, name=name, tag="handover", align_bytes=64)
+        def handed_over(tag, shape, name):
+            return keep.tile(shape, BF16, name=name, tag=tag, align_bytes=64)
 
         offsets = keep.tile([P, S // LIST_ROWS], U16, name="offsets")
         word_table = keep.tile([P, T], I32, name="word_table")
@@ -81,7 +80,8 @@ def tile_picked_pick_glu_silu_srt_p_kernel(tc, x_words, x_scales, w1, w3, w2, of
         load_up("w3", 0, 0, HALF)
         load_up("w3", 0, HALF, HALF)
         load_up("w1", 1, 0, PASS)
-        load_up("w3", 1, 0, PASS)
+        load_up("w3", 1, 0, HALF)
+        load_up("w3", 1, HALF, HALF)
         for g in range(PASSES):
             down_raw[g] = keep.tile([P, PACK, N], F32, name="w2_raw%d" % g)
             nc.sync.dma_start(down_raw[g][:], w2[g * PASS : (g + 1) * PASS, :].rearrange("(p j) n -> p j n", j=PACK))
@@ -89,8 +89,10 @@ def tile_picked_pick_glu_silu_srt_p_kernel(tc, x_words, x_scales, w1, w3, w2, of
         def copy_on(engine, dst, src):
             if engine == "scalar":
                 nc.scalar.copy(dst, src)
-            else:
+            elif engine == "vector":
                 nc.vector.tensor_copy(dst, src)
+            else:
+                nc.gpsimd.tensor_scalar(dst, src, 1.0, 0.0, MULT, ADD)
 
         def quantise(codes, src, name):
             scales = in_line("vector", list(codes.shape), U8, name)
@@ -98,7 +100,9 @@ def tile_picked_pick_glu_silu_srt_p_kernel(tc, x_words, x_scales, w1, w3, w2, of
             return scales
 
         def round_up(engine, dst, raw, slots):
-            copy_on(engine, dst.rearrange("p t m j -> p m j t"), raw.rearrange("p j (m t) -> p m j t", t=PACK)[:, :, :, slots])
+            src = raw.rearrange("p j (m t) -> p t m j", t=PACK)[:, slots]
+            walk = "p t m j -> p t m j" if engine == "gpsimd" else "p t m j -> p m j t"
+            copy_on(engine, dst.rearrange(walk), src.rearrange(walk))
 
         up_codes, up_scales = {}, {}
 
@@ -112,13 +116,11 @@ def tile_picked_pick_glu_silu_srt_p_kernel(tc, x_words, x_scales, w1, w3, w2, of
 
         down_rounded, down_codes, down_scales = {}, {}, {}
 
-        def round_down(engine, g, half, lo, hi):
-            dst = down_rounded[g, half][:, lo:hi, :]
-            src = down_raw[g][:, :, half * HALF + lo : half * HALF + hi]
-            if engine == "gpsimd":
-                nc.gpsimd.tensor_scalar(dst, src.rearrange("p j c -> p c j"), 1.0, 0.0, MULT, ADD)
-            else:
-                copy_on(engine, dst.rearrange("p (c i) j -> p c j i", i=PAIR), src.rearrange("p j (c i) -> p c j i", i=PAIR))
+        def round_down(engine, g, half, rounded):
+            down_rounded[g, half] = rounded
+            src = down_raw[g][:, :, half * HALF : (half + 1) * HALF]
+            walk = "p c i j" if engine == "gpsimd" else "p c j i"
+            copy_on(engine, rounded[:].rearrange("p (c i) j -> " + walk, i=PAIR), src.rearrange("p j (c i) -> " + walk, i=PAIR))
 
         def quantise_down(g, half):
             down_codes[g, half] = keep.tile([P, HALF], U32, name="w2_codes%d%d" % (g, half), align_bytes=64)
@@ -155,7 +157,7 @@ def tile_picked_pick_glu_silu_srt_p_kernel(tc, x_words, x_scales, w1, w3, w2, of
 
         def mult(g, s):
             c, col = divmod(s * SLICE, CHUNK)
-            if col == 0:
+            if (g, c) not in h_rounded:
                 h_rounded[g, c] = in_line("vector", [P, CHUNK, PACK], BF16, "h_rounded%d%d" % (g, c))
             nc.vector.tensor_tensor(h_rounded[g, c][:, col : col + SLICE, :], banks["w3", g, s][:].rearrange("p t n -> p n t"), gate[g, s][:], MULT)
 
@@ -181,11 +183,11 @@ def tile_picked_pick_glu_silu_srt_p_kernel(tc, x_words, x_scales, w1, w3, w2, of
                         stop=(g == PASSES - 1),
                     )
 
-        def store(engine, lo, width, half):
+        def store(engine, lo, width, half, queue=nc.sync):
             y = in_line(engine, [P, HALF // P, width], F32, "y%d_%d" % (lo, half))
             copy_on(engine, y[:], banks["w2", lo, half][:])
             rows = out[half * HALF : (half + 1) * HALF, lo : lo + width]
-            nc.sync.dma_start(rows.rearrange("(r p) n -> p r n", p=P), y[:])
+            queue.dma_start(rows.rearrange("(r p) n -> p r n", p=P), y[:])
 
         all_slots = slice(0, PACK)
         half_m = HALF // PACK
@@ -198,7 +200,7 @@ def tile_picked_pick_glu_silu_srt_p_kernel(tc, x_words, x_scales, w1, w3, w2, of
         quantise_up("w1", 0, w1_first, 0)
         for c in range(CHUNKS):
             gather_words(c)
-        w3_first = keep.tile([P, PACK, P, PACK], BF16, name="w3_first", align_bytes=64)
+        w3_first = handed_over("before_w1", [P, PACK, P, PACK], "w3_first")
         for half in range(2):
             round_up("vector", w3_first[:, :, half * half_m : (half + 1) * half_m, :], up_raw["w3", 0, half * HALF][:], all_slots)
         quantise_up("w3", 0, w3_first, 0)
@@ -206,14 +208,19 @@ def tile_picked_pick_glu_silu_srt_p_kernel(tc, x_words, x_scales, w1, w3, w2, of
             up_product("w1", 0, s)
             silu(0, s)
 
+        w1_raw = up_raw["w1", 1, 0]
         w1_low = in_line("scalar", [P, PAIR, P, PACK], BF16, "w1_low")
-        round_up("scalar", w1_low[:], up_raw["w1", 1, 0][:], slice(0, PAIR))
-        w1_high = in_line("scalar", [P, PAIR, P, PACK], BF16, "w1_high")
-        round_up("scalar", w1_high[:], up_raw["w1", 1, 0][:], slice(PAIR, PACK))
-        w3_low = in_line("scalar", [P, PAIR, P, PACK], BF16, "w3_low")
-        round_up("scalar", w3_low[:], up_raw["w3", 1, 0][:], slice(0, PAIR))
+        round_up("scalar", w1_low[:], w1_raw[:], slice(0, PAIR))
+        w1_high = handed_over("before_w1", [P, PAIR, P, PACK], "w1_high")
+        round_up("gpsimd", w1_high[:, :, :half_m, :], w1_raw[:, :, :HALF], slice(PAIR, PACK))
+        round_up("scalar", w1_high[:, :, half_m:, :], w1_raw[:, :, HALF:], slice(PAIR, PACK))
+        w3_second = in_line("scalar", [P, PACK, P, PACK], BF16, "w3_second")
+        for half in range(2):
+            round_up("scalar", w3_second[:, :, half * half_m : (half + 1) * half_m, :], up_raw["w3", 1, half * HALF][:], all_slots)
+
         for s in range(SLICES):
             up_product("w3", 0, s)
+        h_rounded[0, 0] = handed_over("before_w2", [P, CHUNK, PACK], "h_rounded00")
         for s in range(MULTS_BEFORE_LOW):
             mult(0, s)
         quantise_up("w1", 1, w1_low, 0)
@@ -224,22 +231,22 @@ def tile_picked_pick_glu_silu_srt_p_kernel(tc, x_words, x_scales, w1, w3, w2, of
         quantise_up("w1", 1, w1_high, PAIR)
         for s in range(MULTS_BEFORE_LOW):
             up_product("w1", 1, s, range(PAIR, PACK))
-        for s in range(MULTS_BEFORE_LOW, EARLY_GATES):
-            up_product("w1", 1, s)
-        mult(0, SLICES - 3)
-        w3_high = handed_over([P, PAIR, P, PACK], "w3_high")
-        round_up("vector", w3_high[:], up_raw["w3", 1, 0][:], slice(PAIR, PACK))
-        mult(0, SLICES - 2)
-        quantise_up("w3", 1, w3_low, 0)
-        quantise_up("w3", 1, w3_high, PAIR)
-        mult(0, SLICES - 1)
-
         last = SLICES - 1
-        down_rounded[0, 0] = handed_over([P, HALF, PACK], "w2_rounded00")
-        round_down("gpsimd", 0, 0, 0, HALF)
+        for s in range(MULTS_BEFORE_HIGH, last):
+            mult(0, s)
+        quantise_h(0, CHUNK, CHUNK)
+        quantise_up("w3", 1, w3_second, 0)
+        quantise_h(0, 0, CHUNK)
+        mult(0, last)
+
+        round_down("gpsimd", 0, 0, handed_over("before_w2", [P, HALF, PACK], "w2_rounded00"))
+        up_product("w1", 1, EARLY_GATES - 2)
+        for s in range(2):
+            up_product("w3", 1, s)
+        up_product("w1", 1, EARLY_GATES - 1)
         for s in range(EARLY_GATES):
             silu(1, s)
-        for s in range(EARLY_MULTS):
+        for s in range(2, EARLY_MULTS):
             up_product("w3", 1, s)
         for s in range(EARLY_GATES, SLICES):
             up_product("w1", 1, s)
@@ -247,22 +254,18 @@ def tile_picked_pick_glu_silu_srt_p_kernel(tc, x_words, x_scales, w1, w3, w2, of
             up_product("w3", 1, s)
         for s in range(EARLY_MULTS):
             mult(1, s)
-        down_rounded[0, 1] = in_line("scalar", [P, HALF, PACK], BF16, "w2_rounded01")
-        round_down("scalar", 0, 1, GPSIMD_COLUMNS - HALF, HALF)
-        round_down("gpsimd", 0, 1, 0, GPSIMD_COLUMNS - HALF)
-        for half in range(2):
-            down_rounded[1, half] = in_line("scalar", [P, HALF, PACK], BF16, "w2_rounded1%d" % half)
-            round_down("scalar", 1, half, 0, HALF)
+        for g in range(PASSES):
+            round_down("scalar", g, 1, in_line("scalar", [P, HALF, PACK], BF16, "w2_rounded%d1" % g))
         for s in range(EARLY_GATES, SLICES):
             silu(1, s)
 
-        for c in range(2):
-            for g in range(PASSES):
-                quantise_h(g, c * CHUNK, CHUNK)
-            if c == 0:
-                for g in range(PASSES):
-                    quantise_down(g, 0)
-            down_product(c * CHUNK, CHUNK, 0)
+        round_down("vector", 1, 0, in_line("vector", [P, HALF, PACK], BF16, "w2_rounded10"))
+        quantise_h(1, 0, CHUNK)
+        for g in range(PASSES):
+            quantise_down(g, 0)
+        down_product(0, CHUNK, 0)
+        quantise_h(1, CHUNK, CHUNK)
+        down_product(CHUNK, CHUNK, 0)
         for g in range(PASSES):
             quantise_down(g, 1)
         for c in range(2):
@@ -289,4 +292,4 @@ def tile_picked_pick_glu_silu_srt_p_kernel(tc, x_words, x_scales, w1, w3, w2, of
                 down_product(s * SLICE, SLICE, half)
         for s in (last - 1, last):
             store("vector", s * SLICE, SLICE, 0)
-            store("scalar", s * SLICE, SLICE, 1)
+            store("scalar", s * SLICE, SLICE, 1, nc.scalar if s == last else nc.sync)

@@ -27,12 +27,8 @@ SLICES = S // SLICE
 CHUNK = 256
 CHUNKS = S // CHUNK
 LIST_ROWS = 16
-BANKS = 8
+BANKS = {"ring": 6, "held": 2}
 SLOTS = {"scalar": 14, "vector": 36}
-MULTS_BEFORE_LOW = 4
-MULTS_BEFORE_HIGH = 5
-EARLY_GATES = 6
-EARLY_MULTS = 4
 
 
 def tile_picked_pick_glu_silu_srt_p_kernel(tc, x_words, x_scales, w1, w3, w2, offs, out):
@@ -59,32 +55,22 @@ def tile_picked_pick_glu_silu_srt_p_kernel(tc, x_words, x_scales, w1, w3, w2, of
         nc.scalar.activation(warm_out[:], warm[:], SILU)
 
         words_dram = x_words[0].rearrange("p n r -> p (n r)").bitcast(I32)
-        up_dram = {"w1": w1, "w3": w3}
-        up_raw, down_raw = {}, {}
+        scales_dram = x_scales[0].bitcast(I32)
+        raw = {}
 
         def window(chunks):
             return chunks * CHUNK + T - S
 
-        def load_up(name, g, lo, width):
-            up_raw[name, g, lo] = keep.tile([P, PACK, width], F32, name="%s_raw%d_%d" % (name, g, lo))
-            columns = up_dram[name][:, g * PASS + lo : g * PASS + lo + width]
-            nc.sync.dma_start(up_raw[name, g, lo][:], columns.rearrange("(p j) c -> p j c", j=PACK))
+        def load(name, rows):
+            raw[name] = keep.tile([P, PACK, rows.shape[1]], F32, name=name)
+            nc.sync.dma_start(raw[name][:], rows.rearrange("(p j) c -> p j c", j=PACK))
 
-        nc.sync.dma_start(offsets[:], offs)
-        load_up("w1", 0, 0, HALF)
-        for q in range(4):
-            nc.sync.dma_start(scale_table[32 * q : 32 * q + 4, :].bitcast(I32), x_scales[0, 4 * q : 4 * q + 4, :].bitcast(I32))
-        load_up("w1", 0, HALF, HALF)
-        nc.sync.dma_start(word_table[:, : window(CHUNKS // 2)], words_dram[:, : window(CHUNKS // 2)])
-        nc.sync.dma_start(word_table[:, window(CHUNKS // 2) :], words_dram[:, window(CHUNKS // 2) :])
-        load_up("w3", 0, 0, HALF)
-        load_up("w3", 0, HALF, HALF)
-        load_up("w1", 1, 0, PASS)
-        load_up("w3", 1, 0, HALF)
-        load_up("w3", 1, HALF, HALF)
-        for g in range(PASSES):
-            down_raw[g] = keep.tile([P, PACK, N], F32, name="w2_raw%d" % g)
-            nc.sync.dma_start(down_raw[g][:], w2[g * PASS : (g + 1) * PASS, :].rearrange("(p j) n -> p j n", j=PACK))
+        def load_scales():
+            for r in range(4):
+                nc.sync.dma_start(scale_table[r:P:32, :].bitcast(I32), scales_dram[r:16:4, :])
+
+        def load_words(lo, hi):
+            nc.sync.dma_start(word_table[:, lo:hi], words_dram[:, lo:hi])
 
         def copy_on(engine, dst, src):
             if engine == "scalar":
@@ -94,202 +80,227 @@ def tile_picked_pick_glu_silu_srt_p_kernel(tc, x_words, x_scales, w1, w3, w2, of
             else:
                 nc.gpsimd.tensor_scalar(dst, src, 1.0, 0.0, MULT, ADD)
 
-        def quantise(codes, src, name):
-            scales = in_line("vector", list(codes.shape), U8, name)
-            nc.vector.quantize_mx(out=codes.bitcast(FP8X4), scales=scales[:], in_=src)
-            return scales
+        def quantise(src, width, name):
+            codes = keep.tile([P, width], U32, name=name + "_codes", align_bytes=64)
+            scales = in_line("vector", [P, width], U8, name + "_scales")
+            nc.vector.quantize_mx(out=codes[:].bitcast(FP8X4), scales=scales[:], in_=src)
+            return codes, scales
 
-        def round_up(engine, dst, raw, slots):
-            src = raw.rearrange("p j (m t) -> p t m j", t=PACK)[:, slots]
+        def round_up(engine, dst, src, lo, hi, at=0):
+            src = src[:, :, PACK * (lo - at) : PACK * (hi - at)].rearrange("p j (m t) -> p t m j", t=PACK)
             walk = "p t m j -> p t m j" if engine == "gpsimd" else "p t m j -> p m j t"
-            copy_on(engine, dst.rearrange(walk), src.rearrange(walk))
+            copy_on(engine, dst[:, :, lo:hi, :].rearrange(walk), src.rearrange(walk))
 
-        up_codes, up_scales = {}, {}
-
-        def quantise_up(name, g, rounded, first_slot):
-            slots = rounded.shape[1]
-            codes = keep.tile([P, slots * P], U32, name="%s_codes%d%d" % (name, g, first_slot), align_bytes=64)
-            scales = quantise(codes[:], rounded[:].rearrange("p t m j -> p (t m j)"), "%s_scales%d%d" % (name, g, first_slot))
-            for t in range(slots):
-                up_codes[name, g, first_slot + t] = codes[:, t * P : (t + 1) * P]
-                up_scales[name, g, first_slot + t] = scales[:, t * P : (t + 1) * P]
-
-        down_rounded, down_codes, down_scales = {}, {}, {}
-
-        def round_down(engine, g, half, rounded):
-            down_rounded[g, half] = rounded
-            src = down_raw[g][:, :, half * HALF : (half + 1) * HALF]
+        def round_down(engine, dst, g, half):
+            src = raw["w2_%d" % g][:, :, half * HALF : (half + 1) * HALF]
             walk = "p c i j" if engine == "gpsimd" else "p c j i"
-            copy_on(engine, rounded[:].rearrange("p (c i) j -> " + walk, i=PAIR), src.rearrange("p j (c i) -> " + walk, i=PAIR))
+            copy_on(engine, dst[:].rearrange("p (c i) j -> " + walk, i=PAIR), src.rearrange("p j (c i) -> " + walk, i=PAIR))
+            return dst
 
-        def quantise_down(g, half):
-            down_codes[g, half] = keep.tile([P, HALF], U32, name="w2_codes%d%d" % (g, half), align_bytes=64)
-            src = down_rounded[g, half][:].rearrange("p c j -> p (c j)")
-            down_scales[g, half] = quantise(down_codes[g, half][:], src, "w2_scales%d%d" % (g, half))
+        up, down, x_codes, gate_banks, value_banks, out_banks, gate, h_rounded, h = {}, {}, {}, {}, {}, {}, {}, {}, {}
 
-        x_codes, banks, gate = {}, {}, {}
+        def quantise_up(name, g, rounded):
+            up[name, g] = quantise(rounded[:].rearrange("p t m j -> p (t m j)"), PASS, "%s_%d" % (name, g))
+
+        def quantise_down(g, lo, rounded):
+            width = rounded.shape[1]
+            codes, scales = quantise(rounded[:].rearrange("p c j -> p (c j)"), width, "w2_%d_%d" % (g, lo))
+            for at in range(0, width, P):
+                down[g, (lo + at) // P] = codes[:, at : at + P], scales[:, at : at + P]
 
         def gather_words(c):
             x_codes[c] = in_line("vector", [P, CHUNK], U32, "x_codes%d" % c)
             entries = offsets[:, c * CHUNK // LIST_ROWS : (c + 1) * CHUNK // LIST_ROWS]
             nc.vector.tensor_copy(x_codes[c][:], word_table[:, : window(c + 1)].bitcast(U32).indirect(entries))
 
-        def up_product(name, g, s, slots=range(PACK)):
-            if slots[0] == 0:
-                banks[name, g, s] = psum.tile([P, PACK, SLICE], F32, name="bank", bufs=BANKS)
-            c, col = divmod(s * SLICE, CHUNK)
-            for t in slots:
-                nc.tensor.matmul_mx(
-                    out=banks[name, g, s][:, t, :],
-                    lhsT=up_codes[name, g, t].bitcast(FP8X4),
-                    lhsT_scale=up_scales[name, g, t],
-                    rhs=x_codes[c][:, col : col + SLICE].bitcast(FP8X4),
-                    rhs_scale=x_bytes[:, s * SLICE : (s + 1) * SLICE],
-                    start=True,
-                    stop=True,
-                )
-
-        def silu(g, s):
-            gate[g, s] = in_line("scalar", [P, SLICE, PACK], F32, "gate%d%d" % (g, s))
-            nc.scalar.activation(gate[g, s][:], banks["w1", g, s][:].rearrange("p t n -> p n t"), SILU)
-
-        h_rounded, h_codes, h_scales = {}, {}, {}
-
-        def mult(g, s):
-            c, col = divmod(s * SLICE, CHUNK)
-            if (g, c) not in h_rounded:
-                h_rounded[g, c] = in_line("vector", [P, CHUNK, PACK], BF16, "h_rounded%d%d" % (g, c))
-            nc.vector.tensor_tensor(h_rounded[g, c][:, col : col + SLICE, :], banks["w3", g, s][:].rearrange("p t n -> p n t"), gate[g, s][:], MULT)
-
-        def quantise_h(g, lo, width):
+        def product(bank, weights, t, lo, width):
             c, col = divmod(lo, CHUNK)
-            codes = keep.tile([P, width], U32, name="h_codes%d_%d" % (g, lo), align_bytes=64)
-            src = h_rounded[g, c][:, col : col + width, :].rearrange("p n t -> p (n t)")
-            scales = quantise(codes[:], src, "h_scales%d_%d" % (g, lo))
-            for at in range(0, width, SLICE):
-                h_codes[g, lo + at], h_scales[g, lo + at] = codes[:, at:], scales[:, at:]
+            codes, scales = weights
+            nc.tensor.matmul_mx(
+                out=bank,
+                lhsT=codes[:, t * P : (t + 1) * P].bitcast(FP8X4),
+                lhsT_scale=scales[:, t * P : (t + 1) * P],
+                rhs=x_codes[c][:, col : col + width].bitcast(FP8X4),
+                rhs_scale=x_bytes[:, lo : lo + width],
+                start=True,
+                stop=True,
+            )
 
-        def down_product(lo, width, half):
-            banks["w2", lo, half] = psum.tile([P, HALF // P, width], F32, name="bank", bufs=BANKS)
-            for r in range(HALF // P):
-                for g in range(PASSES):
+        def next_bank(shape, tag="ring"):
+            return psum.tile(shape, F32, name="bank", tag=tag, bufs=BANKS[tag])
+
+        def gate_products(g, c, tag="ring"):
+            for a in range(PAIR):
+                gate_banks[g, c, a] = next_bank([P, PAIR, CHUNK], tag)
+                for b in range(PAIR):
+                    product(gate_banks[g, c, a][:, b, :], up["w1", g], PAIR * a + b, c * CHUNK, CHUNK)
+
+        def silu(g, c, pairs=range(PAIR)):
+            for a in pairs:
+                if a == 0:
+                    gate[g, c] = in_line("scalar", [P, PAIR, CHUNK, PAIR], F32, "gate%d%d" % (g, c))
+                nc.scalar.activation(gate[g, c][:, a], gate_banks[g, c, a][:].rearrange("p b n -> p n b"), SILU)
+
+        def value_products(g, s):
+            value_banks[g, s] = next_bank([P, PACK, SLICE])
+            for t in range(PACK):
+                product(value_banks[g, s][:, t, :], up["w3", g], t, s * SLICE, SLICE)
+
+        def mult(g, s, tile=None):
+            c, col = divmod(s * SLICE, CHUNK)
+            if (g, s) not in value_banks:
+                value_products(g, s)
+            bank = value_banks[g, s]
+            if (g, c) not in h_rounded:
+                h_rounded[g, c] = in_line("vector", [P, CHUNK, PACK], BF16, "h_rounded%d%d" % (g, c)) if tile is None else tile
+            nc.vector.tensor_tensor(
+                h_rounded[g, c][:, col : col + SLICE, :].rearrange("p n (a b) -> p n a b", b=PAIR),
+                bank[:].rearrange("p (a b) n -> p n a b", b=PAIR),
+                gate[g, c][:, :, col : col + SLICE, :].rearrange("p a n b -> p n a b"),
+                MULT,
+            )
+
+        def quantise_h(g, lo, width=CHUNK):
+            c, col = divmod(lo, CHUNK)
+            src = h_rounded[g, c][:, col : col + width, :]
+            codes, scales = quantise(src.rearrange("p n t -> p (n t)"), width, "h_%d_%d" % (g, lo))
+            for at in range(0, width, SLICE):
+                h[g, lo + at] = codes[:, at:], scales[:, at:]
+
+        def down_products(lo, width, first, passes=range(PASSES), tag="ring"):
+            blocks = min(PASS // width, PAIR)
+            if passes[0] == 0:
+                out_banks[lo, first] = next_bank([P, blocks, width], tag)
+            for g in passes:
+                for r in range(blocks):
                     nc.tensor.matmul_mx(
-                        out=banks["w2", lo, half][:, r, :],
-                        lhsT=down_codes[g, half][:, r * P : (r + 1) * P].bitcast(FP8X4),
-                        lhsT_scale=down_scales[g, half][:, r * P : (r + 1) * P],
-                        rhs=h_codes[g, lo][:, :width].bitcast(FP8X4),
-                        rhs_scale=h_scales[g, lo][:, :width],
-                        start=(g == 0),
-                        stop=(g == PASSES - 1),
+                        out=out_banks[lo, first][:, r, :],
+                        lhsT=down[g, first + r][0].bitcast(FP8X4),
+                        lhsT_scale=down[g, first + r][1],
+                        rhs=h[g, lo][0][:, :width].bitcast(FP8X4),
+                        rhs_scale=h[g, lo][1][:, :width],
+                        start=(g == 0 and r == 0),
+                        stop=(g == PASSES - 1 and r == blocks - 1),
                     )
 
-        def store(engine, lo, width, half, queue=nc.sync):
-            y = in_line(engine, [P, HALF // P, width], F32, "y%d_%d" % (lo, half))
-            copy_on(engine, y[:], banks["w2", lo, half][:])
-            rows = out[half * HALF : (half + 1) * HALF, lo : lo + width]
+        def store(engines, lo, width, first, queue=nc.sync):
+            blocks = min(PASS // width, PAIR)
+            y = in_line(engines[0], [P, blocks * len(engines), width], F32, "y%d_%d" % (lo, first))
+            for i, engine in enumerate(engines):
+                if (lo, first + i * blocks) not in out_banks:
+                    down_products(lo, width, first + i * blocks)
+                copy_on(engine, y[:, i * blocks : (i + 1) * blocks, :], out_banks[lo, first + i * blocks][:])
+            rows = out[first * P : (first + blocks * len(engines)) * P, lo : lo + width]
             queue.dma_start(rows.rearrange("(r p) n -> p r n", p=P), y[:])
 
-        all_slots = slice(0, PACK)
-        half_m = HALF // PACK
+        up_shape = [P, PACK, P, PACK]
+        down_shape = [P, HALF, PACK]
+
+        nc.sync.dma_start(offsets[:], offs)
+        load_words(0, 640)
+        load_scales()
+        load("w1_0", w1[:, :PASS])
+        load_words(640, window(2))
+        load("w3_0", w3[:, :PASS])
+        load_words(window(2), T)
+        load("w1_1", w1[:, PASS:])
+        load("w2_0", w2[:PASS, :])
+        load("w3_1", w3[:, PASS:])
+        load("w2_1", w2[PASS:, :])
 
         x_bytes = in_line("vector", [P, S], U8, "x_bytes")
         nc.vector.tensor_copy(x_bytes[:], scale_table[:].indirect(offsets[:]))
-        w1_first = in_line("scalar", [P, PACK, P, PACK], BF16, "w1_first")
-        for half in range(2):
-            round_up("scalar", w1_first[:, :, half * half_m : (half + 1) * half_m, :], up_raw["w1", 0, half * HALF][:], all_slots)
-        quantise_up("w1", 0, w1_first, 0)
-        for c in range(CHUNKS):
-            gather_words(c)
-        w3_first = handed_over("before_w1", [P, PACK, P, PACK], "w3_first")
-        for half in range(2):
-            round_up("vector", w3_first[:, :, half * half_m : (half + 1) * half_m, :], up_raw["w3", 0, half * HALF][:], all_slots)
-        quantise_up("w3", 0, w3_first, 0)
-        for s in range(SLICES):
-            up_product("w1", 0, s)
-            silu(0, s)
-
-        w1_raw = up_raw["w1", 1, 0]
-        w1_low = in_line("scalar", [P, PAIR, P, PACK], BF16, "w1_low")
-        round_up("scalar", w1_low[:], w1_raw[:], slice(0, PAIR))
-        w1_high = handed_over("before_w1", [P, PAIR, P, PACK], "w1_high")
-        round_up("gpsimd", w1_high[:, :, :half_m, :], w1_raw[:, :, :HALF], slice(PAIR, PACK))
-        round_up("scalar", w1_high[:, :, half_m:, :], w1_raw[:, :, HALF:], slice(PAIR, PACK))
-        w3_second = in_line("scalar", [P, PACK, P, PACK], BF16, "w3_second")
-        for half in range(2):
-            round_up("scalar", w3_second[:, :, half * half_m : (half + 1) * half_m, :], up_raw["w3", 1, half * HALF][:], all_slots)
-
-        for s in range(SLICES):
-            up_product("w3", 0, s)
-        h_rounded[0, 0] = handed_over("before_w2", [P, CHUNK, PACK], "h_rounded00")
-        for s in range(MULTS_BEFORE_LOW):
-            mult(0, s)
-        quantise_up("w1", 1, w1_low, 0)
-        for s in range(MULTS_BEFORE_LOW):
-            up_product("w1", 1, s, range(PAIR))
-        for s in range(MULTS_BEFORE_LOW, MULTS_BEFORE_HIGH):
-            mult(0, s)
-        quantise_up("w1", 1, w1_high, PAIR)
-        for s in range(MULTS_BEFORE_LOW):
-            up_product("w1", 1, s, range(PAIR, PACK))
-        last = SLICES - 1
-        for s in range(MULTS_BEFORE_HIGH, last):
-            mult(0, s)
-        quantise_h(0, CHUNK, CHUNK)
-        quantise_up("w3", 1, w3_second, 0)
-        quantise_h(0, 0, CHUNK)
-        mult(0, last)
-
-        round_down("gpsimd", 0, 0, handed_over("before_w2", [P, HALF, PACK], "w2_rounded00"))
-        up_product("w1", 1, EARLY_GATES - 2)
-        for s in range(2):
-            up_product("w3", 1, s)
-        up_product("w1", 1, EARLY_GATES - 1)
-        for s in range(EARLY_GATES):
-            silu(1, s)
-        for s in range(2, EARLY_MULTS):
-            up_product("w3", 1, s)
-        for s in range(EARLY_GATES, SLICES):
-            up_product("w1", 1, s)
-        for s in range(EARLY_MULTS, SLICES):
-            up_product("w3", 1, s)
-        for s in range(EARLY_MULTS):
-            mult(1, s)
-        for g in range(PASSES):
-            round_down("scalar", g, 1, in_line("scalar", [P, HALF, PACK], BF16, "w2_rounded%d1" % g))
-        for s in range(EARLY_GATES, SLICES):
-            silu(1, s)
-
-        round_down("vector", 1, 0, in_line("vector", [P, HALF, PACK], BF16, "w2_rounded10"))
-        quantise_h(1, 0, CHUNK)
-        for g in range(PASSES):
-            quantise_down(g, 0)
-        down_product(0, CHUNK, 0)
-        quantise_h(1, CHUNK, CHUNK)
-        down_product(CHUNK, CHUNK, 0)
-        for g in range(PASSES):
-            quantise_down(g, 1)
+        w1_0 = in_line("scalar", up_shape, BF16, "w1_0r")
+        round_up("scalar", w1_0, raw["w1_0"], 84, P)
+        round_up("vector", w1_0, raw["w1_0"], 0, 84)
+        quantise_up("w1", 0, w1_0)
+        gather_words(0)
+        gather_words(1)
+        w3_0 = in_line("scalar", up_shape, BF16, "w3_0r")
+        round_up("scalar", w3_0, raw["w3_0"], 84, P)
+        round_up("vector", w3_0, raw["w3_0"], 0, 84)
+        quantise_up("w3", 0, w3_0)
+        gather_words(2)
+        gather_words(3)
         for c in range(2):
-            down_product(c * CHUNK, CHUNK, 1)
-        for half in range(2):
-            for c in range(2):
-                store("scalar", c * CHUNK, CHUNK, half)
+            gate_products(0, c, "ring" if c else "held")
+            silu(0, c)
 
-        for s in range(EARLY_MULTS, last - 1):
+        w1_1 = in_line("scalar", up_shape, BF16, "w1_1r")
+        round_up("gpsimd", w1_1, raw["w1_1"], 0, 48)
+        round_up("scalar", w1_1, raw["w1_1"], 48, P)
+        mult(0, 0, handed_over("h00", [P, CHUNK, PACK], "h00"))
+        for s in range(1, 4):
+            mult(0, s)
+        gate_products(0, 2)
+        silu(0, 2)
+        quantise_up("w1", 1, w1_1)
+        quantise_h(0, 0)
+        w2_00 = round_down("gpsimd", handed_over("h00", down_shape, "w2_00r"), 0, 0)
+        mult(0, 4, handed_over("h02", [P, CHUNK, PACK], "h02"))
+        gate_products(0, 3)
+        silu(0, 3)
+        mult(0, 5)
+        w2_01 = round_down("scalar", in_line("scalar", down_shape, BF16, "w2_01r"), 0, 1)
+        mult(0, 6)
+        mult(0, 7)
+        for c in range(3):
+            gate_products(1, c)
+        w3_1 = in_line("scalar", up_shape, BF16, "w3_1r")
+        round_up("scalar", w3_1, raw["w3_1"], 68, P)
+        round_up("vector", w3_1, raw["w3_1"], 0, 68)
+        quantise_down(0, 0, w2_00)
+        down_products(0, CHUNK, 0, [0], "held")
+        for c in range(3):
+            silu(1, c)
+        quantise_up("w3", 1, w3_1)
+        quantise_down(0, HALF, w2_01)
+        quantise_h(0, CHUNK)
+        quantise_h(0, 2 * CHUNK)
+        value_products(1, 0)
+        value_products(1, 1)
+        down_products(0, CHUNK, 2, [0], "held")
+        value_products(1, 2)
+        value_products(1, 3)
+        gate_products(1, 3)
+        w2_10 = round_down("gpsimd", handed_over("h02", down_shape, "w2_10r"), 1, 0)
+        w2_11 = round_down("scalar", in_line("scalar", down_shape, BF16, "w2_11r"), 1, 1)
+        silu(1, 3)
+        for s in range(3):
             mult(1, s)
-        for g in range(PASSES):
-            quantise_h(g, 2 * CHUNK, CHUNK)
-        for half in range(2):
-            down_product(2 * CHUNK, CHUNK, half)
-            store("scalar", 2 * CHUNK, CHUNK, half)
-
-        mult(1, last - 1)
-        quantise_h(0, 3 * CHUNK, CHUNK)
-        quantise_h(1, (last - 1) * SLICE, SLICE)
-        mult(1, last)
-        quantise_h(1, last * SLICE, SLICE)
-        for s in (last - 1, last):
-            for half in range(2):
-                down_product(s * SLICE, SLICE, half)
-        for s in (last - 1, last):
-            store("vector", s * SLICE, SLICE, 0)
-            store("scalar", s * SLICE, SLICE, 1, nc.scalar if s == last else nc.sync)
+        value_products(1, 4)
+        value_products(1, 5)
+        quantise_down(1, 0, w2_10)
+        quantise_h(1, 0)
+        value_products(1, 6)
+        down_products(0, CHUNK, 0, [1])
+        mult(1, 3)
+        quantise_down(1, HALF, w2_11)
+        quantise_h(1, CHUNK)
+        down_products(0, CHUNK, 2, [1])
+        value_products(1, 7)
+        store(["scalar"], 0, CHUNK, 0)
+        store(["scalar"], 0, CHUNK, 2)
+        store(["scalar"], CHUNK, CHUNK, 0)
+        store(["scalar"], CHUNK, CHUNK, 2)
+        mult(1, 4)
+        mult(1, 5)
+        quantise_h(0, 3 * CHUNK)
+        quantise_h(1, 2 * CHUNK)
+        for first in (0, 2):
+            down_products(2 * CHUNK, CHUNK, first, [0])
+        for first in (0, 2):
+            down_products(2 * CHUNK, CHUNK, first, [1])
+            store(["scalar"], 2 * CHUNK, CHUNK, first)
+        mult(1, 6)
+        mult(1, 7)
+        for first in (0, 2):
+            down_products(6 * SLICE, SLICE, first, [0], "held")
+        for first in (0, 2):
+            down_products(7 * SLICE, SLICE, first, [0])
+        for s in (6, 7):
+            quantise_h(1, s * SLICE, SLICE)
+            for first in (0, 2):
+                down_products(s * SLICE, SLICE, first, [1])
+        store(["vector", "vector"], 6 * SLICE, SLICE, 0)
+        store(["vector", "scalar"], 7 * SLICE, SLICE, 0, nc.scalar)

@@ -26,9 +26,11 @@ SLICE = 128
 SLICES = S // SLICE
 CHUNK = 256
 CHUNKS = S // CHUNK
+GROUP = 512
 LIST_ROWS = 16
 BANKS = {"ring": 6, "held": 2}
-SLOTS = {"scalar": 14, "vector": 36}
+SLOTS = {"scalar": 9, "vector": 30}
+VECTOR_SHARE = 84
 
 
 def tile_picked_pick_glu_silu_srt_p_kernel(tc, x_words, x_scales, w1, w3, w2, offs, out):
@@ -58,6 +60,8 @@ def tile_picked_pick_glu_silu_srt_p_kernel(tc, x_words, x_scales, w1, w3, w2, of
         scales_dram = x_scales[0].bitcast(I32)
         raw = {}
 
+        planes_of = {}
+
         def window(chunks):
             return chunks * CHUNK + T - S
 
@@ -86,21 +90,40 @@ def tile_picked_pick_glu_silu_srt_p_kernel(tc, x_words, x_scales, w1, w3, w2, of
             nc.vector.quantize_mx(out=codes[:].bitcast(FP8X4), scales=scales[:], in_=src)
             return codes, scales
 
-        def round_up(engine, dst, src, lo, hi, at=0):
-            src = src[:, :, PACK * (lo - at) : PACK * (hi - at)].rearrange("p j (m t) -> p t m j", t=PACK)
-            walk = "p t m j -> p t m j" if engine == "gpsimd" else "p t m j -> p m j t"
-            copy_on(engine, dst[:, :, lo:hi, :].rearrange(walk), src.rearrange(walk))
+        def round_up(engine, dst, src):
+            copy_on(engine, dst.rearrange("p t m j -> p m j t"), src.rearrange("p j m t -> p m j t"))
 
-        def round_down(engine, dst, g, half):
-            src = raw["w2_%d" % g][:, :, half * HALF : (half + 1) * HALF]
-            walk = "p c i j" if engine == "gpsimd" else "p c j i"
-            copy_on(engine, dst[:].rearrange("p (c i) j -> " + walk, i=PAIR), src.rearrange("p j (c i) -> " + walk, i=PAIR))
+        def by_slot(name):
+            return raw[name][:].rearrange("p j (m t) -> p j m t", t=PACK)
+
+        def round_shared(name):
+            rounded = in_line("scalar", [P, PACK, P, PACK], BF16, name + "r")
+            round_up("scalar", rounded[:, :, VECTOR_SHARE:, :], by_slot(name)[:, :, VECTOR_SHARE:, :])
+            round_up("vector", rounded[:, :, :VECTOR_SHARE, :], by_slot(name)[:, :, :VECTOR_SHARE, :])
+            return rounded
+
+        def round_halves(name):
+            rounded = in_line("scalar", [P, PACK, P, PACK], BF16, name + "r")
+            round_up("scalar", rounded[:, :, : P // 2, :], by_slot(name + "a"))
+            round_up("vector", rounded[:, :, P // 2 :, :], by_slot(name + "b"))
+            return rounded
+
+        def round_pair(engine, rounded, name, first_slot, lo=0, hi=P):
+            round_up(engine, rounded[:, :, lo:hi, :], by_slot(name)[:, :, lo:hi, first_slot : first_slot + PAIR])
+            return rounded
+
+        def round_down(engine, dst, g, half, lo=0, hi=HALF):
+            src = raw["w2_%d_%d" % (g, half)][:, :, lo:hi]
+            copy_on(engine, dst[:, lo:hi, :].rearrange("p (c i) j -> p c j i", i=PAIR), src.rearrange("p j (c i) -> p c j i", i=PAIR))
             return dst
 
-        up, down, x_codes, gate_banks, value_banks, out_banks, gate, h_rounded, h = {}, {}, {}, {}, {}, {}, {}, {}, {}
+        up, down, x_codes, gate_banks, slice_banks, out_banks, gate, gate_of, h_rounded, h = {}, {}, {}, {}, {}, {}, {}, {}, {}, {}
 
-        def quantise_up(name, g, rounded):
-            up[name, g] = quantise(rounded[:].rearrange("p t m j -> p (t m j)"), PASS, "%s_%d" % (name, g))
+        def quantise_up(name, g, rounded, first_slot=0):
+            slots = rounded.shape[1]
+            codes, scales = quantise(rounded[:].rearrange("p t m j -> p (t m j)"), slots * P, "%s_%d_%d" % (name, g, first_slot))
+            for t in range(slots):
+                up[name, g, first_slot + t] = codes[:, t * P : (t + 1) * P], scales[:, t * P : (t + 1) * P]
 
         def quantise_down(g, lo, rounded):
             width = rounded.shape[1]
@@ -108,18 +131,27 @@ def tile_picked_pick_glu_silu_srt_p_kernel(tc, x_words, x_scales, w1, w3, w2, of
             for at in range(0, width, P):
                 down[g, (lo + at) // P] = codes[:, at : at + P], scales[:, at : at + P]
 
-        def gather_words(c):
-            x_codes[c] = in_line("vector", [P, CHUNK], U32, "x_codes%d" % c)
-            entries = offsets[:, c * CHUNK // LIST_ROWS : (c + 1) * CHUNK // LIST_ROWS]
-            nc.vector.tensor_copy(x_codes[c][:], word_table[:, : window(c + 1)].bitcast(U32).indirect(entries))
+        def quantise_both(rounded):
+            codes, scales = quantise(rounded[:].rearrange("p g c j -> p (g c j)"), PASSES * HALF, "w2_low")
+            for g in range(PASSES):
+                for r in range(HALF // P):
+                    at = g * HALF + r * P
+                    down[g, r] = codes[:, at : at + P], scales[:, at : at + P]
 
-        def product(bank, weights, t, lo, width):
-            c, col = divmod(lo, CHUNK)
+        def gather_words(c):
+            if c % PAIR == 0:
+                x_codes[c // PAIR] = in_line("vector", [P, GROUP], U32, "x_codes%d" % c)
+            entries = offsets[:, c * CHUNK // LIST_ROWS : (c + 1) * CHUNK // LIST_ROWS]
+            at = c % PAIR * CHUNK
+            nc.vector.tensor_copy(x_codes[c // PAIR][:, at : at + CHUNK], word_table[:, : window(c + 1)].bitcast(U32).indirect(entries))
+
+        def product(bank, weights, lo, width):
+            c, col = divmod(lo, GROUP)
             codes, scales = weights
             nc.tensor.matmul_mx(
                 out=bank,
-                lhsT=codes[:, t * P : (t + 1) * P].bitcast(FP8X4),
-                lhsT_scale=scales[:, t * P : (t + 1) * P],
+                lhsT=codes.bitcast(FP8X4),
+                lhsT_scale=scales,
                 rhs=x_codes[c][:, col : col + width].bitcast(FP8X4),
                 rhs_scale=x_bytes[:, lo : lo + width],
                 start=True,
@@ -129,43 +161,71 @@ def tile_picked_pick_glu_silu_srt_p_kernel(tc, x_words, x_scales, w1, w3, w2, of
         def next_bank(shape, tag="ring"):
             return psum.tile(shape, F32, name="bank", tag=tag, bufs=BANKS[tag])
 
-        def gate_products(g, c, tag="ring"):
-            for a in range(PAIR):
+        def gate_products(g, c, tag="ring", pairs=range(PAIR)):
+            for a in pairs:
                 gate_banks[g, c, a] = next_bank([P, PAIR, CHUNK], tag)
                 for b in range(PAIR):
-                    product(gate_banks[g, c, a][:, b, :], up["w1", g], PAIR * a + b, c * CHUNK, CHUNK)
+                    product(gate_banks[g, c, a][:, b, :], up["w1", g, PAIR * a + b], c * CHUNK, CHUNK)
 
-        def silu(g, c, pairs=range(PAIR)):
-            for a in pairs:
-                if a == 0:
-                    gate[g, c] = in_line("scalar", [P, PAIR, CHUNK, PAIR], F32, "gate%d%d" % (g, c))
-                nc.scalar.activation(gate[g, c][:, a], gate_banks[g, c, a][:].rearrange("p b n -> p n b"), SILU)
+        def silu(g, c):
+            planes = in_line("scalar", [P, PACK, CHUNK], F32, "gate%d%d" % (g, c))
+            for a in range(PAIR):
+                nc.scalar.activation(planes[:, PAIR * a : PAIR * (a + 1), :], gate_banks[g, c, a][:], SILU)
+            for i in range(PAIR):
+                planes_of[g, PAIR * c + i] = planes[:, :, i * SLICE : (i + 1) * SLICE]
 
-        def value_products(g, s):
-            value_banks[g, s] = next_bank([P, PACK, SLICE])
-            for t in range(PACK):
-                product(value_banks[g, s][:, t, :], up["w3", g], t, s * SLICE, SLICE)
+        def plane_products(g, slots, tag="ring"):
+            for t in slots:
+                gate_banks[g, t] = next_bank([P, GROUP], tag)
+                product(gate_banks[g, t][:], up["w1", g, t], 0, GROUP)
 
-        def mult(g, s, tile=None):
-            c, col = divmod(s * SLICE, CHUNK)
-            if (g, s) not in value_banks:
-                value_products(g, s)
-            bank = value_banks[g, s]
-            if (g, c) not in h_rounded:
-                h_rounded[g, c] = in_line("vector", [P, CHUNK, PACK], BF16, "h_rounded%d%d" % (g, c)) if tile is None else tile
+        def silu_planes(g, order):
+            planes = in_line("scalar", [P, PACK, GROUP], F32, "gate_planes%d" % g)
+            for t in order:
+                nc.scalar.activation(planes[:, t, :], gate_banks[g, t][:], SILU)
+            for s in range(GROUP // SLICE):
+                planes_of[g, s] = planes[:, :, s * SLICE : (s + 1) * SLICE]
+
+        def slice_products(name, g, s, tag="ring"):
+            slice_banks[name, g, s] = next_bank([P, PACK, SLICE], tag)
+            for t in reversed(range(PACK)):
+                product(slice_banks[name, g, s][:, t, :], up[name, g, t], s * SLICE, SLICE)
+
+        def silu_slice(g, s):
+            planes_of[g, s] = in_line("scalar", [P, PACK, SLICE], F32, "gate_slice%d%d" % (g, s))[:]
+            nc.scalar.activation(planes_of[g, s], slice_banks["w1", g, s][:], SILU)
+
+        def value_products(g, s, tag="ring"):
+            slice_products("w3", g, s, tag)
+
+        def mult(g, s):
+            width = GROUP if s < GROUP // SLICE else CHUNK
+            if s * SLICE % width == 0:
+                tile = in_line("vector", [P, CHUNK, PACK], BF16, "h%d_%d" % (g, s)) if width == CHUNK else keep.tile([P, GROUP, PACK], BF16, name="h%d_%d" % (g, s), align_bytes=64)
+                for i in range(width // SLICE):
+                    h_rounded[g, s + i] = tile[:, i * SLICE :, :]
+            dst, bank = h_rounded[g, s][:, :SLICE, :], slice_banks["w3", g, s][:]
             nc.vector.tensor_tensor(
-                h_rounded[g, c][:, col : col + SLICE, :].rearrange("p n (a b) -> p n a b", b=PAIR),
-                bank[:].rearrange("p (a b) n -> p n a b", b=PAIR),
-                gate[g, c][:, :, col : col + SLICE, :].rearrange("p a n b -> p n a b"),
+                dst.rearrange("p (n i) t -> p n t i", i=PACK),
+                bank.rearrange("p t (n i) -> p n t i", i=PACK),
+                planes_of[g, s].rearrange("p t (n i) -> p n t i", i=PACK),
                 MULT,
             )
 
         def quantise_h(g, lo, width=CHUNK):
-            c, col = divmod(lo, CHUNK)
-            src = h_rounded[g, c][:, col : col + width, :]
+            src = h_rounded[g, lo // SLICE][:, :width, :]
             codes, scales = quantise(src.rearrange("p n t -> p (n t)"), width, "h_%d_%d" % (g, lo))
             for at in range(0, width, SLICE):
                 h[g, lo + at] = codes[:, at:], scales[:, at:]
+
+        def quantise_slices(g, c):
+            codes = keep.tile([P, CHUNK], U32, name="h_%d_%d_codes" % (g, c * CHUNK), align_bytes=64)
+            scales = in_line("vector", [P, CHUNK], U8, "h_%d_%d_scales" % (g, c * CHUNK))
+            for i in range(PAIR):
+                columns = slice(i * SLICE, (i + 1) * SLICE)
+                src = h_rounded[g, PAIR * c + i].rearrange("p n t -> p (n t)")
+                nc.vector.quantize_mx(out=codes[:, columns].bitcast(FP8X4), scales=scales[:, columns], in_=src)
+            h[g, c * CHUNK] = codes[:], scales[:]
 
         def down_products(lo, width, first, passes=range(PASSES), tag="ring"):
             blocks = min(PASS // width, PAIR)
@@ -193,114 +253,112 @@ def tile_picked_pick_glu_silu_srt_p_kernel(tc, x_words, x_scales, w1, w3, w2, of
             rows = out[first * P : (first + blocks * len(engines)) * P, lo : lo + width]
             queue.dma_start(rows.rearrange("(r p) n -> p r n", p=P), y[:])
 
-        up_shape = [P, PACK, P, PACK]
+        pair_shape = [P, PAIR, P, PACK]
         down_shape = [P, HALF, PACK]
 
         nc.sync.dma_start(offsets[:], offs)
         load_words(0, 640)
         load_scales()
         load("w1_0", w1[:, :PASS])
-        load_words(640, window(2))
-        load("w3_0", w3[:, :PASS])
-        load_words(window(2), T)
+        load_words(640, window(3))
+        load("w3_0a", w3[:, :256])
+        load("w3_0b", w3[:, 256:PASS])
+        load_words(window(3), T)
         load("w1_1", w1[:, PASS:])
-        load("w2_0", w2[:PASS, :])
         load("w3_1", w3[:, PASS:])
-        load("w2_1", w2[PASS:, :])
+        load("w2_0", w2[:PASS, :])
+        for half in range(2):
+            raw["w2_0_%d" % half] = raw["w2_0"][:, :, half * HALF : (half + 1) * HALF]
+            load("w2_1_%d" % half, w2[PASS:, half * HALF : (half + 1) * HALF])
 
         x_bytes = in_line("vector", [P, S], U8, "x_bytes")
         nc.vector.tensor_copy(x_bytes[:], scale_table[:].indirect(offsets[:]))
-        w1_0 = in_line("scalar", up_shape, BF16, "w1_0r")
-        round_up("scalar", w1_0, raw["w1_0"], 84, P)
-        round_up("vector", w1_0, raw["w1_0"], 0, 84)
-        quantise_up("w1", 0, w1_0)
-        gather_words(0)
-        gather_words(1)
-        w3_0 = in_line("scalar", up_shape, BF16, "w3_0r")
-        round_up("scalar", w3_0, raw["w3_0"], 84, P)
-        round_up("vector", w3_0, raw["w3_0"], 0, 84)
-        quantise_up("w3", 0, w3_0)
-        gather_words(2)
+        quantise_up("w1", 0, round_shared("w1_0"))
+        for c in range(3):
+            gather_words(c)
+        quantise_up("w3", 0, round_halves("w3_0"))
         gather_words(3)
-        for c in range(2):
+        for c in range(3):
             gate_products(0, c, "ring" if c else "held")
             silu(0, c)
-
-        w1_1 = in_line("scalar", up_shape, BF16, "w1_1r")
-        round_up("gpsimd", w1_1, raw["w1_1"], 0, 48)
-        round_up("scalar", w1_1, raw["w1_1"], 48, P)
-        mult(0, 0, handed_over("h00", [P, CHUNK, PACK], "h00"))
-        for s in range(1, 4):
-            mult(0, s)
-        gate_products(0, 2)
-        silu(0, 2)
-        quantise_up("w1", 1, w1_1)
-        quantise_h(0, 0)
-        w2_00 = round_down("gpsimd", handed_over("h00", down_shape, "w2_00r"), 0, 0)
-        mult(0, 4, handed_over("h02", [P, CHUNK, PACK], "h02"))
+        w1_low = round_pair("gpsimd", handed_over("gpsimd", pair_shape, "w1_low"), "w1_1", 0)
+        w1_high = round_pair("scalar", in_line("scalar", pair_shape, BF16, "w1_high"), "w1_1", PAIR)
+        value_products(0, 0)
+        value_products(0, 1)
+        value_products(0, 2, "held")
+        value_products(0, 3, "held")
         gate_products(0, 3)
         silu(0, 3)
-        mult(0, 5)
-        w2_01 = round_down("scalar", in_line("scalar", down_shape, BF16, "w2_01r"), 0, 1)
-        mult(0, 6)
-        mult(0, 7)
-        for c in range(3):
-            gate_products(1, c)
-        w3_1 = in_line("scalar", up_shape, BF16, "w3_1r")
-        round_up("scalar", w3_1, raw["w3_1"], 68, P)
-        round_up("vector", w3_1, raw["w3_1"], 0, 68)
-        quantise_down(0, 0, w2_00)
-        down_products(0, CHUNK, 0, [0], "held")
+        value_products(0, 4)
+        for s in range(4):
+            mult(0, s)
+        quantise_up("w1", 1, w1_high, PAIR)
+        quantise_up("w1", 1, w1_low)
+        quantise_h(0, 0)
+        value_products(0, 5)
+        value_products(0, 6, "held")
+        value_products(0, 7, "held")
+        gate_products(1, 0)
+        w3_high = round_pair("scalar", in_line("scalar", pair_shape, BF16, "w3_high"), "w3_1", PAIR)
+        w3_low = round_pair("gpsimd", handed_over("gpsimd", pair_shape, "w3_low"), "w3_1", 0, 0, 68)
+        gate_products(1, 1)
+        gate_products(1, 2)
         for c in range(3):
             silu(1, c)
-        quantise_up("w3", 1, w3_1)
-        quantise_down(0, HALF, w2_01)
-        quantise_h(0, CHUNK)
-        quantise_h(0, 2 * CHUNK)
-        value_products(1, 0)
-        value_products(1, 1)
-        down_products(0, CHUNK, 2, [0], "held")
-        value_products(1, 2)
-        value_products(1, 3)
-        gate_products(1, 3)
-        w2_10 = round_down("gpsimd", handed_over("h02", down_shape, "w2_10r"), 1, 0)
+        mult(0, 4)
+        mult(0, 5)
+        round_pair("vector", w3_low, "w3_1", 0, 68, P)
+        quantise_up("w3", 1, w3_high, PAIR)
+        quantise_up("w3", 1, w3_low)
+        mult(0, 6)
+        mult(0, 7)
+        w2_low = handed_over("gpsimd", [P, PASSES, HALF, PACK], "w2_low")
+        w2_00 = round_down("gpsimd", w2_low[:, 0], 0, 0)
+        w2_10 = round_down("gpsimd", w2_low[:, 1], 1, 0, 0, 208)
+        round_down("scalar", w2_10, 1, 0, 208, HALF)
+        for s in range(4):
+            value_products(1, s)
+        slice_products("w1", 1, 6)
+        slice_products("w1", 1, 7)
+        w2_01 = round_down("scalar", in_line("scalar", down_shape, BF16, "w2_01r"), 0, 1)
         w2_11 = round_down("scalar", in_line("scalar", down_shape, BF16, "w2_11r"), 1, 1)
-        silu(1, 3)
-        for s in range(3):
+        silu_slice(1, 6)
+        for s in range(4):
             mult(1, s)
         value_products(1, 4)
         value_products(1, 5)
-        quantise_down(1, 0, w2_10)
-        quantise_h(1, 0)
         value_products(1, 6)
-        down_products(0, CHUNK, 0, [1])
-        mult(1, 3)
-        quantise_down(1, HALF, w2_11)
-        quantise_h(1, CHUNK)
-        down_products(0, CHUNK, 2, [1])
         value_products(1, 7)
+        quantise_both(w2_low)
+        quantise_h(1, 0)
+        down_products(0, CHUNK, 0, tag="held")
+        quantise_h(0, CHUNK)
+        quantise_h(1, CHUNK)
+        down_products(CHUNK, CHUNK, 0, tag="held")
+        quantise_down(0, HALF, w2_01)
+        quantise_down(1, HALF, w2_11)
         store(["scalar"], 0, CHUNK, 0)
-        store(["scalar"], 0, CHUNK, 2)
         store(["scalar"], CHUNK, CHUNK, 0)
+        silu_slice(1, 7)
+        store(["scalar"], 0, CHUNK, 2)
+        down_products(CHUNK, CHUNK, 2, tag="held")
         store(["scalar"], CHUNK, CHUNK, 2)
         mult(1, 4)
         mult(1, 5)
-        quantise_h(0, 3 * CHUNK)
+        quantise_h(0, 2 * CHUNK)
         quantise_h(1, 2 * CHUNK)
+        quantise_h(0, 3 * CHUNK)
         for first in (0, 2):
-            down_products(2 * CHUNK, CHUNK, first, [0])
-        for first in (0, 2):
-            down_products(2 * CHUNK, CHUNK, first, [1])
+            down_products(2 * CHUNK, CHUNK, first, tag="ring" if first else "held")
             store(["scalar"], 2 * CHUNK, CHUNK, first)
         mult(1, 6)
         mult(1, 7)
-        for first in (0, 2):
-            down_products(6 * SLICE, SLICE, first, [0], "held")
-        for first in (0, 2):
-            down_products(7 * SLICE, SLICE, first, [0])
+        for s in (6, 7):
+            for first in (0, 2):
+                down_products(s * SLICE, SLICE, first, [0])
         for s in (6, 7):
             quantise_h(1, s * SLICE, SLICE)
             for first in (0, 2):
                 down_products(s * SLICE, SLICE, first, [1])
-        store(["vector", "vector"], 6 * SLICE, SLICE, 0)
+        store(["vector", "scalar"], 6 * SLICE, SLICE, 0)
         store(["vector", "scalar"], 7 * SLICE, SLICE, 0, nc.scalar)

@@ -18,19 +18,24 @@ ADD = mybir.AluOpType.add
 
 P = 128
 PACK = 4
+PAIR = 2
 PASS = P * PACK
 PASSES = H // PASS
-HALF = 256
-PAIR = 2
+HALF = N // 2
 SLICE = 128
-SLICES = S // SLICE
 CHUNK = 256
-CHUNKS = S // CHUNK
 GROUP = 512
+LAST_SLICES = (S // SLICE - 2, S // SLICE - 1)
+LOW, HIGH = 0, 1
 LIST_ROWS = 16
+QUADRANT, SCALE_ROWS = 32, 4
 BANKS = {"ring": 6, "held": 2}
 SLOTS = {"scalar": 9, "vector": 30}
-VECTOR_SHARE = 84
+
+X_FIRST = 640
+VECTOR_M = 96
+GPSIMD_M = 68
+GPSIMD_COLUMNS = 208
 
 
 def tile_picked_pick_glu_silu_srt_p_kernel(tc, x_words, x_scales, w1, w3, w2, offs, out):
@@ -43,8 +48,11 @@ def tile_picked_pick_glu_silu_srt_p_kernel(tc, x_words, x_scales, w1, w3, w2, of
         def in_line(engine, shape, dtype, name):
             return line.tile(shape, dtype, name=name, tag=engine, bufs=SLOTS[engine], align_bytes=64)
 
-        def handed_over(tag, shape, name):
-            return keep.tile(shape, BF16, name=name, tag=tag, align_bytes=64)
+        def for_gpsimd(shape, name):
+            return keep.tile(shape, BF16, name=name, tag="gpsimd", align_bytes=64)
+
+        def next_bank(shape, tag="ring"):
+            return psum.tile(shape, F32, name="bank", tag=tag, bufs=BANKS[tag])
 
         offsets = keep.tile([P, S // LIST_ROWS], U16, name="offsets")
         word_table = keep.tile([P, T], I32, name="word_table")
@@ -58,23 +66,34 @@ def tile_picked_pick_glu_silu_srt_p_kernel(tc, x_words, x_scales, w1, w3, w2, of
 
         words_dram = x_words[0].rearrange("p n r -> p (n r)").bitcast(I32)
         scales_dram = x_scales[0].bitcast(I32)
-        raw = {}
-
-        planes_of = {}
 
         def window(chunks):
             return chunks * CHUNK + T - S
 
         def load(name, rows):
-            raw[name] = keep.tile([P, PACK, rows.shape[1]], F32, name=name)
-            nc.sync.dma_start(raw[name][:], rows.rearrange("(p j) c -> p j c", j=PACK))
-
-        def load_scales():
-            for r in range(4):
-                nc.sync.dma_start(scale_table[r:P:32, :].bitcast(I32), scales_dram[r:16:4, :])
+            tile = keep.tile([P, PACK, rows.shape[1]], F32, name=name)
+            nc.sync.dma_start(tile[:], rows.rearrange("(p j) c -> p j c", j=PACK))
+            return tile
 
         def load_words(lo, hi):
             nc.sync.dma_start(word_table[:, lo:hi], words_dram[:, lo:hi])
+
+        nc.sync.dma_start(offsets[:], offs)
+        load_words(0, X_FIRST)
+        for r in range(SCALE_ROWS):
+            nc.sync.dma_start(scale_table[r:P:QUADRANT, :].bitcast(I32), scales_dram[r : x_scales.shape[1] : SCALE_ROWS, :])
+        w1_raw0 = load("w1_raw0", w1[:, :PASS])
+        load_words(X_FIRST, window(3))
+        w3_raw0 = load("w3_raw0", w3[:, :PASS])
+        load_words(window(3), T)
+        w1_raw1 = load("w1_raw1", w1[:, PASS:])
+        w3_raw1 = load("w3_raw1", w3[:, PASS:])
+        w2_raw0 = load("w2_raw0", w2[:PASS, :])
+        w2_raw = {(0, half): w2_raw0[:, :, half * HALF : (half + 1) * HALF] for half in (LOW, HIGH)}
+        for half in (LOW, HIGH):
+            w2_raw[1, half] = load("w2_raw1_%d" % half, w2[PASS:, half * HALF : (half + 1) * HALF])
+
+        up, down, x_codes, gate_banks, slice_banks, out_banks, gate, h_rounded, h = {}, {}, {}, {}, {}, {}, {}, {}, {}
 
         def copy_on(engine, dst, src):
             if engine == "scalar":
@@ -84,40 +103,30 @@ def tile_picked_pick_glu_silu_srt_p_kernel(tc, x_words, x_scales, w1, w3, w2, of
             else:
                 nc.gpsimd.tensor_scalar(dst, src, 1.0, 0.0, MULT, ADD)
 
+        def by_slot(raw):
+            return raw[:].rearrange("p j (m t) -> p j m t", t=PACK)
+
+        def round_up(engine, dst, src):
+            copy_on(engine, dst.rearrange("p t m j -> p m j t"), src.rearrange("p j m t -> p m j t"))
+
+        def round_shared(raw, name):
+            rounded = in_line("scalar", [P, PACK, P, PACK], BF16, name)
+            round_up("scalar", rounded[:, :, VECTOR_M:, :], by_slot(raw)[:, :, VECTOR_M:, :])
+            round_up("vector", rounded[:, :, :VECTOR_M, :], by_slot(raw)[:, :, :VECTOR_M, :])
+            return rounded
+
+        def round_pair(engine, dst, raw, first_slot, lo=0, hi=P):
+            round_up(engine, dst[:, :, lo:hi, :], by_slot(raw)[:, :, lo:hi, first_slot : first_slot + PAIR])
+
+        def round_down(engine, dst, g, half, lo=0, hi=HALF):
+            src = w2_raw[g, half][:, :, lo:hi]
+            copy_on(engine, dst[:, lo:hi, :].rearrange("p (c i) j -> p c j i", i=PAIR), src.rearrange("p j (c i) -> p c j i", i=PAIR))
+
         def quantise(src, width, name):
             codes = keep.tile([P, width], U32, name=name + "_codes", align_bytes=64)
             scales = in_line("vector", [P, width], U8, name + "_scales")
             nc.vector.quantize_mx(out=codes[:].bitcast(FP8X4), scales=scales[:], in_=src)
             return codes, scales
-
-        def round_up(engine, dst, src):
-            copy_on(engine, dst.rearrange("p t m j -> p m j t"), src.rearrange("p j m t -> p m j t"))
-
-        def by_slot(name):
-            return raw[name][:].rearrange("p j (m t) -> p j m t", t=PACK)
-
-        def round_shared(name):
-            rounded = in_line("scalar", [P, PACK, P, PACK], BF16, name + "r")
-            round_up("scalar", rounded[:, :, VECTOR_SHARE:, :], by_slot(name)[:, :, VECTOR_SHARE:, :])
-            round_up("vector", rounded[:, :, :VECTOR_SHARE, :], by_slot(name)[:, :, :VECTOR_SHARE, :])
-            return rounded
-
-        def round_halves(name):
-            rounded = in_line("scalar", [P, PACK, P, PACK], BF16, name + "r")
-            round_up("scalar", rounded[:, :, : P // 2, :], by_slot(name + "a"))
-            round_up("vector", rounded[:, :, P // 2 :, :], by_slot(name + "b"))
-            return rounded
-
-        def round_pair(engine, rounded, name, first_slot, lo=0, hi=P):
-            round_up(engine, rounded[:, :, lo:hi, :], by_slot(name)[:, :, lo:hi, first_slot : first_slot + PAIR])
-            return rounded
-
-        def round_down(engine, dst, g, half, lo=0, hi=HALF):
-            src = raw["w2_%d_%d" % (g, half)][:, :, lo:hi]
-            copy_on(engine, dst[:, lo:hi, :].rearrange("p (c i) j -> p c j i", i=PAIR), src.rearrange("p j (c i) -> p c j i", i=PAIR))
-            return dst
-
-        up, down, x_codes, gate_banks, slice_banks, out_banks, gate, gate_of, h_rounded, h = {}, {}, {}, {}, {}, {}, {}, {}, {}, {}
 
         def quantise_up(name, g, rounded, first_slot=0):
             slots = rounded.shape[1]
@@ -125,18 +134,12 @@ def tile_picked_pick_glu_silu_srt_p_kernel(tc, x_words, x_scales, w1, w3, w2, of
             for t in range(slots):
                 up[name, g, first_slot + t] = codes[:, t * P : (t + 1) * P], scales[:, t * P : (t + 1) * P]
 
-        def quantise_down(g, lo, rounded):
-            width = rounded.shape[1]
-            codes, scales = quantise(rounded[:].rearrange("p c j -> p (c j)"), width, "w2_%d_%d" % (g, lo))
-            for at in range(0, width, P):
-                down[g, (lo + at) // P] = codes[:, at : at + P], scales[:, at : at + P]
-
-        def quantise_both(rounded):
-            codes, scales = quantise(rounded[:].rearrange("p g c j -> p (g c j)"), PASSES * HALF, "w2_low")
-            for g in range(PASSES):
-                for r in range(HALF // P):
-                    at = g * HALF + r * P
-                    down[g, r] = codes[:, at : at + P], scales[:, at : at + P]
+        def quantise_down(half, passes, rounded):
+            codes, scales = quantise(rounded, len(passes) * HALF, "w2_%d_%d" % (half, passes[0]))
+            for i, g in enumerate(passes):
+                for r in range(PAIR):
+                    at = i * HALF + r * P
+                    down[g, PAIR * half + r] = codes[:, at : at + P], scales[:, at : at + P]
 
         def gather_words(c):
             if c % PAIR == 0:
@@ -146,23 +149,20 @@ def tile_picked_pick_glu_silu_srt_p_kernel(tc, x_words, x_scales, w1, w3, w2, of
             nc.vector.tensor_copy(x_codes[c // PAIR][:, at : at + CHUNK], word_table[:, : window(c + 1)].bitcast(U32).indirect(entries))
 
         def product(bank, weights, lo, width):
-            c, col = divmod(lo, GROUP)
+            group, col = divmod(lo, GROUP)
             codes, scales = weights
             nc.tensor.matmul_mx(
                 out=bank,
                 lhsT=codes.bitcast(FP8X4),
                 lhsT_scale=scales,
-                rhs=x_codes[c][:, col : col + width].bitcast(FP8X4),
+                rhs=x_codes[group][:, col : col + width].bitcast(FP8X4),
                 rhs_scale=x_bytes[:, lo : lo + width],
                 start=True,
                 stop=True,
             )
 
-        def next_bank(shape, tag="ring"):
-            return psum.tile(shape, F32, name="bank", tag=tag, bufs=BANKS[tag])
-
-        def gate_products(g, c, tag="ring", pairs=range(PAIR)):
-            for a in pairs:
+        def gate_products(g, c, tag="ring"):
+            for a in range(PAIR):
                 gate_banks[g, c, a] = next_bank([P, PAIR, CHUNK], tag)
                 for b in range(PAIR):
                     product(gate_banks[g, c, a][:, b, :], up["w1", g, PAIR * a + b], c * CHUNK, CHUNK)
@@ -172,19 +172,7 @@ def tile_picked_pick_glu_silu_srt_p_kernel(tc, x_words, x_scales, w1, w3, w2, of
             for a in range(PAIR):
                 nc.scalar.activation(planes[:, PAIR * a : PAIR * (a + 1), :], gate_banks[g, c, a][:], SILU)
             for i in range(PAIR):
-                planes_of[g, PAIR * c + i] = planes[:, :, i * SLICE : (i + 1) * SLICE]
-
-        def plane_products(g, slots, tag="ring"):
-            for t in slots:
-                gate_banks[g, t] = next_bank([P, GROUP], tag)
-                product(gate_banks[g, t][:], up["w1", g, t], 0, GROUP)
-
-        def silu_planes(g, order):
-            planes = in_line("scalar", [P, PACK, GROUP], F32, "gate_planes%d" % g)
-            for t in order:
-                nc.scalar.activation(planes[:, t, :], gate_banks[g, t][:], SILU)
-            for s in range(GROUP // SLICE):
-                planes_of[g, s] = planes[:, :, s * SLICE : (s + 1) * SLICE]
+                gate[g, PAIR * c + i] = planes[:, :, i * SLICE : (i + 1) * SLICE]
 
         def slice_products(name, g, s, tag="ring"):
             slice_banks[name, g, s] = next_bank([P, PACK, SLICE], tag)
@@ -192,25 +180,30 @@ def tile_picked_pick_glu_silu_srt_p_kernel(tc, x_words, x_scales, w1, w3, w2, of
                 product(slice_banks[name, g, s][:, t, :], up[name, g, t], s * SLICE, SLICE)
 
         def silu_slice(g, s):
-            planes_of[g, s] = in_line("scalar", [P, PACK, SLICE], F32, "gate_slice%d%d" % (g, s))[:]
-            nc.scalar.activation(planes_of[g, s], slice_banks["w1", g, s][:], SILU)
+            gate[g, s] = in_line("scalar", [P, PACK, SLICE], F32, "gate_slice%d%d" % (g, s))[:]
+            nc.scalar.activation(gate[g, s], slice_banks["w1", g, s][:], SILU)
 
-        def value_products(g, s, tag="ring"):
-            slice_products("w3", g, s, tag)
+        def h_tile(g, first_slice, tile):
+            for i in range(tile.shape[1] // SLICE):
+                h_rounded[g, first_slice + i] = tile[:, i * SLICE :, :]
 
         def mult(g, s):
-            width = GROUP if s < GROUP // SLICE else CHUNK
-            if s * SLICE % width == 0:
-                tile = in_line("vector", [P, CHUNK, PACK], BF16, "h%d_%d" % (g, s)) if width == CHUNK else keep.tile([P, GROUP, PACK], BF16, name="h%d_%d" % (g, s), align_bytes=64)
-                for i in range(width // SLICE):
-                    h_rounded[g, s + i] = tile[:, i * SLICE :, :]
-            dst, bank = h_rounded[g, s][:, :SLICE, :], slice_banks["w3", g, s][:]
             nc.vector.tensor_tensor(
-                dst.rearrange("p (n i) t -> p n t i", i=PACK),
-                bank.rearrange("p t (n i) -> p n t i", i=PACK),
-                planes_of[g, s].rearrange("p t (n i) -> p n t i", i=PACK),
+                h_rounded[g, s][:, :SLICE, :].rearrange("p (n i) t -> p n t i", i=PACK),
+                slice_banks["w3", g, s][:].rearrange("p t (n i) -> p n t i", i=PACK),
+                gate[g, s].rearrange("p t (n i) -> p n t i", i=PACK),
                 MULT,
             )
+
+        def first_group_mults(g):
+            h_tile(g, 0, keep.tile([P, GROUP, PACK], BF16, name="h_group%d" % g, align_bytes=64))
+            for s in range(GROUP // SLICE):
+                mult(g, s)
+
+        def chunk_mults(g, c):
+            h_tile(g, PAIR * c, in_line("vector", [P, CHUNK, PACK], BF16, "h_chunk%d%d" % (g, c)))
+            for s in (PAIR * c, PAIR * c + 1):
+                mult(g, s)
 
         def quantise_h(g, lo, width=CHUNK):
             src = h_rounded[g, lo // SLICE][:, :width, :]
@@ -218,147 +211,133 @@ def tile_picked_pick_glu_silu_srt_p_kernel(tc, x_words, x_scales, w1, w3, w2, of
             for at in range(0, width, SLICE):
                 h[g, lo + at] = codes[:, at:], scales[:, at:]
 
-        def quantise_slices(g, c):
-            codes = keep.tile([P, CHUNK], U32, name="h_%d_%d_codes" % (g, c * CHUNK), align_bytes=64)
-            scales = in_line("vector", [P, CHUNK], U8, "h_%d_%d_scales" % (g, c * CHUNK))
-            for i in range(PAIR):
-                columns = slice(i * SLICE, (i + 1) * SLICE)
-                src = h_rounded[g, PAIR * c + i].rearrange("p n t -> p (n t)")
-                nc.vector.quantize_mx(out=codes[:, columns].bitcast(FP8X4), scales=scales[:, columns], in_=src)
-            h[g, c * CHUNK] = codes[:], scales[:]
-
-        def down_products(lo, width, first, passes=range(PASSES), tag="ring"):
-            blocks = min(PASS // width, PAIR)
+        def down_products(lo, width, half, passes=range(PASSES), tag="ring"):
             if passes[0] == 0:
-                out_banks[lo, first] = next_bank([P, blocks, width], tag)
+                out_banks[lo, half] = next_bank([P, PAIR, width], tag)
             for g in passes:
-                for r in range(blocks):
+                for r in range(PAIR):
                     nc.tensor.matmul_mx(
-                        out=out_banks[lo, first][:, r, :],
-                        lhsT=down[g, first + r][0].bitcast(FP8X4),
-                        lhsT_scale=down[g, first + r][1],
+                        out=out_banks[lo, half][:, r, :],
+                        lhsT=down[g, PAIR * half + r][0].bitcast(FP8X4),
+                        lhsT_scale=down[g, PAIR * half + r][1],
                         rhs=h[g, lo][0][:, :width].bitcast(FP8X4),
                         rhs_scale=h[g, lo][1][:, :width],
                         start=(g == 0 and r == 0),
-                        stop=(g == PASSES - 1 and r == blocks - 1),
+                        stop=(g == PASSES - 1 and r == PAIR - 1),
                     )
 
-        def store(engines, lo, width, first, queue=nc.sync):
-            blocks = min(PASS // width, PAIR)
-            y = in_line(engines[0], [P, blocks * len(engines), width], F32, "y%d_%d" % (lo, first))
-            for i, engine in enumerate(engines):
-                if (lo, first + i * blocks) not in out_banks:
-                    down_products(lo, width, first + i * blocks)
-                copy_on(engine, y[:, i * blocks : (i + 1) * blocks, :], out_banks[lo, first + i * blocks][:])
-            rows = out[first * P : (first + blocks * len(engines)) * P, lo : lo + width]
+        def store_chunk(c, half):
+            y = in_line("scalar", [P, PAIR, CHUNK], F32, "y%d_%d" % (c, half))
+            nc.scalar.copy(y[:], out_banks[c * CHUNK, half][:])
+            rows = out[half * HALF : (half + 1) * HALF, c * CHUNK : (c + 1) * CHUNK]
+            nc.sync.dma_start(rows.rearrange("(r p) n -> p r n", p=P), y[:])
+
+        def store_last_chunk(engine, half, queue):
+            y = in_line(engine, [P, PAIR, CHUNK], F32, "y_last%d" % half)
+            for i, s in enumerate(LAST_SLICES):
+                copy_on(engine, y[:, :, i * SLICE : (i + 1) * SLICE], out_banks[s * SLICE, half][:])
+            rows = out[half * HALF : (half + 1) * HALF, S - CHUNK :]
             queue.dma_start(rows.rearrange("(r p) n -> p r n", p=P), y[:])
 
         pair_shape = [P, PAIR, P, PACK]
-        down_shape = [P, HALF, PACK]
-
-        nc.sync.dma_start(offsets[:], offs)
-        load_words(0, 640)
-        load_scales()
-        load("w1_0", w1[:, :PASS])
-        load_words(640, window(3))
-        load("w3_0a", w3[:, :256])
-        load("w3_0b", w3[:, 256:PASS])
-        load_words(window(3), T)
-        load("w1_1", w1[:, PASS:])
-        load("w3_1", w3[:, PASS:])
-        load("w2_0", w2[:PASS, :])
-        for half in range(2):
-            raw["w2_0_%d" % half] = raw["w2_0"][:, :, half * HALF : (half + 1) * HALF]
-            load("w2_1_%d" % half, w2[PASS:, half * HALF : (half + 1) * HALF])
+        half_shape = [P, HALF, PACK]
 
         x_bytes = in_line("vector", [P, S], U8, "x_bytes")
         nc.vector.tensor_copy(x_bytes[:], scale_table[:].indirect(offsets[:]))
-        quantise_up("w1", 0, round_shared("w1_0"))
+        quantise_up("w1", 0, round_shared(w1_raw0, "w1_first"))
         for c in range(3):
             gather_words(c)
-        quantise_up("w3", 0, round_halves("w3_0"))
+        quantise_up("w3", 0, round_shared(w3_raw0, "w3_first"))
         gather_words(3)
-        for c in range(3):
-            gate_products(0, c, "ring" if c else "held")
+        gate_products(0, 0, "held")
+        silu(0, 0)
+        for c in (1, 2):
+            gate_products(0, c)
             silu(0, c)
-        w1_low = round_pair("gpsimd", handed_over("gpsimd", pair_shape, "w1_low"), "w1_1", 0)
-        w1_high = round_pair("scalar", in_line("scalar", pair_shape, BF16, "w1_high"), "w1_1", PAIR)
-        value_products(0, 0)
-        value_products(0, 1)
-        value_products(0, 2, "held")
-        value_products(0, 3, "held")
+
+        w1_low = for_gpsimd(pair_shape, "w1_low")
+        round_pair("gpsimd", w1_low, w1_raw1, 0)
+        w1_high = in_line("scalar", pair_shape, BF16, "w1_high")
+        round_pair("scalar", w1_high, w1_raw1, PAIR)
+        for s in (0, 1):
+            slice_products("w3", 0, s)
+        for s in (2, 3):
+            slice_products("w3", 0, s, "held")
         gate_products(0, 3)
         silu(0, 3)
-        value_products(0, 4)
-        for s in range(4):
-            mult(0, s)
+        slice_products("w3", 0, 4)
+        first_group_mults(0)
         quantise_up("w1", 1, w1_high, PAIR)
         quantise_up("w1", 1, w1_low)
         quantise_h(0, 0)
-        value_products(0, 5)
-        value_products(0, 6, "held")
-        value_products(0, 7, "held")
+
+        slice_products("w3", 0, 5)
+        for s in (6, 7):
+            slice_products("w3", 0, s, "held")
         gate_products(1, 0)
-        w3_high = round_pair("scalar", in_line("scalar", pair_shape, BF16, "w3_high"), "w3_1", PAIR)
-        w3_low = round_pair("gpsimd", handed_over("gpsimd", pair_shape, "w3_low"), "w3_1", 0, 0, 68)
-        gate_products(1, 1)
-        gate_products(1, 2)
+        w3_high = in_line("scalar", pair_shape, BF16, "w3_high")
+        round_pair("scalar", w3_high, w3_raw1, PAIR)
+        w3_low = for_gpsimd(pair_shape, "w3_low")
+        round_pair("gpsimd", w3_low, w3_raw1, 0, 0, GPSIMD_M)
+        for c in (1, 2):
+            gate_products(1, c)
         for c in range(3):
             silu(1, c)
-        mult(0, 4)
-        mult(0, 5)
-        round_pair("vector", w3_low, "w3_1", 0, 68, P)
+        chunk_mults(0, 2)
+        round_pair("vector", w3_low, w3_raw1, 0, GPSIMD_M, P)
         quantise_up("w3", 1, w3_high, PAIR)
         quantise_up("w3", 1, w3_low)
-        mult(0, 6)
-        mult(0, 7)
-        w2_low = handed_over("gpsimd", [P, PASSES, HALF, PACK], "w2_low")
-        w2_00 = round_down("gpsimd", w2_low[:, 0], 0, 0)
-        w2_10 = round_down("gpsimd", w2_low[:, 1], 1, 0, 0, 208)
-        round_down("scalar", w2_10, 1, 0, 208, HALF)
+
+        chunk_mults(0, 3)
+        w2_low = for_gpsimd([P, PASSES, HALF, PACK], "w2_low")
+        round_down("gpsimd", w2_low[:, 0], 0, LOW)
+        round_down("gpsimd", w2_low[:, 1], 1, LOW, 0, GPSIMD_COLUMNS)
+        round_down("scalar", w2_low[:, 1], 1, LOW, GPSIMD_COLUMNS, HALF)
         for s in range(4):
-            value_products(1, s)
-        slice_products("w1", 1, 6)
-        slice_products("w1", 1, 7)
-        w2_01 = round_down("scalar", in_line("scalar", down_shape, BF16, "w2_01r"), 0, 1)
-        w2_11 = round_down("scalar", in_line("scalar", down_shape, BF16, "w2_11r"), 1, 1)
-        silu_slice(1, 6)
-        for s in range(4):
-            mult(1, s)
-        value_products(1, 4)
-        value_products(1, 5)
-        value_products(1, 6)
-        value_products(1, 7)
-        quantise_both(w2_low)
+            slice_products("w3", 1, s)
+        for s in LAST_SLICES:
+            slice_products("w1", 1, s)
+        w2_high = []
+        for g in range(PASSES):
+            w2_high.append(in_line("scalar", half_shape, BF16, "w2_high%d" % g))
+            round_down("scalar", w2_high[g], g, HIGH)
+        silu_slice(1, LAST_SLICES[0])
+        first_group_mults(1)
+        for s in range(4, 8):
+            slice_products("w3", 1, s)
+
+        quantise_down(LOW, range(PASSES), w2_low[:].rearrange("p g c j -> p (g c j)"))
         quantise_h(1, 0)
-        down_products(0, CHUNK, 0, tag="held")
-        quantise_h(0, CHUNK)
-        quantise_h(1, CHUNK)
-        down_products(CHUNK, CHUNK, 0, tag="held")
-        quantise_down(0, HALF, w2_01)
-        quantise_down(1, HALF, w2_11)
-        store(["scalar"], 0, CHUNK, 0)
-        store(["scalar"], CHUNK, CHUNK, 0)
-        silu_slice(1, 7)
-        store(["scalar"], 0, CHUNK, 2)
-        down_products(CHUNK, CHUNK, 2, tag="held")
-        store(["scalar"], CHUNK, CHUNK, 2)
-        mult(1, 4)
-        mult(1, 5)
-        quantise_h(0, 2 * CHUNK)
-        quantise_h(1, 2 * CHUNK)
+        down_products(0, CHUNK, LOW, tag="held")
+        for g in range(PASSES):
+            quantise_h(g, CHUNK)
+        down_products(CHUNK, CHUNK, LOW, tag="held")
+        for g in range(PASSES):
+            quantise_down(HIGH, [g], w2_high[g][:].rearrange("p c j -> p (c j)"))
+        store_chunk(0, LOW)
+        store_chunk(1, LOW)
+        silu_slice(1, LAST_SLICES[1])
+        down_products(0, CHUNK, HIGH)
+        store_chunk(0, HIGH)
+        down_products(CHUNK, CHUNK, HIGH, tag="held")
+        store_chunk(1, HIGH)
+
+        chunk_mults(1, 2)
+        for g in range(PASSES):
+            quantise_h(g, 2 * CHUNK)
         quantise_h(0, 3 * CHUNK)
-        for first in (0, 2):
-            down_products(2 * CHUNK, CHUNK, first, tag="ring" if first else "held")
-            store(["scalar"], 2 * CHUNK, CHUNK, first)
-        mult(1, 6)
-        mult(1, 7)
-        for s in (6, 7):
-            for first in (0, 2):
-                down_products(s * SLICE, SLICE, first, [0])
-        for s in (6, 7):
+        down_products(2 * CHUNK, CHUNK, LOW, tag="held")
+        store_chunk(2, LOW)
+        down_products(2 * CHUNK, CHUNK, HIGH)
+        store_chunk(2, HIGH)
+
+        chunk_mults(1, 3)
+        for s in LAST_SLICES:
+            for half in (LOW, HIGH):
+                down_products(s * SLICE, SLICE, half, [0])
+        for s in LAST_SLICES:
             quantise_h(1, s * SLICE, SLICE)
-            for first in (0, 2):
-                down_products(s * SLICE, SLICE, first, [1])
-        store(["vector", "scalar"], 6 * SLICE, SLICE, 0)
-        store(["vector", "scalar"], 7 * SLICE, SLICE, 0, nc.scalar)
+            for half in (LOW, HIGH):
+                down_products(s * SLICE, SLICE, half, [1])
+        store_last_chunk("vector", LOW, nc.sync)
+        store_last_chunk("scalar", HIGH, nc.scalar)

@@ -25,17 +25,15 @@ HALF = N // 2
 SLICE = 128
 CHUNK = 256
 GROUP = 512
-LAST_SLICES = (S // SLICE - 2, S // SLICE - 1)
 LOW, HIGH = 0, 1
 LIST_ROWS = 16
 QUADRANT, SCALE_ROWS = 32, 4
-BANKS = {"ring": 6, "held": 2}
-SLOTS = {"scalar": 9, "vector": 30}
+SLOTS = {"scalar": 9, "vector": 26}
 
 X_FIRST = 640
-VECTOR_M = 96
-GPSIMD_M = 68
-GPSIMD_COLUMNS = 208
+SCALAR_M = 72
+GPSIMD_W1_M = 96
+GPSIMD_M = 52
 
 
 def tile_picked_pick_glu_silu_srt_p_kernel(tc, x_words, x_scales, w1, w3, w2, offs, out):
@@ -46,13 +44,12 @@ def tile_picked_pick_glu_silu_srt_p_kernel(tc, x_words, x_scales, w1, w3, w2, of
         psum = ctx.enter_context(tc.psum_pool(name="psum", bufs=1))
 
         def in_line(engine, shape, dtype, name):
+            if engine == "gpsimd":
+                return keep.tile(shape, dtype, name=name, tag="gpsimd", align_bytes=64)
             return line.tile(shape, dtype, name=name, tag=engine, bufs=SLOTS[engine], align_bytes=64)
 
-        def for_gpsimd(shape, name):
-            return keep.tile(shape, BF16, name=name, tag="gpsimd", align_bytes=64)
-
-        def next_bank(shape, tag="ring"):
-            return psum.tile(shape, F32, name="bank", tag=tag, bufs=BANKS[tag])
+        def bank(b, shape):
+            return psum.tile(shape, F32, name="bank%d" % b, tag="bank%d" % b)
 
         offsets = keep.tile([P, S // LIST_ROWS], U16, name="offsets")
         word_table = keep.tile([P, T], I32, name="word_table")
@@ -78,22 +75,11 @@ def tile_picked_pick_glu_silu_srt_p_kernel(tc, x_words, x_scales, w1, w3, w2, of
         def load_words(lo, hi):
             nc.sync.dma_start(word_table[:, lo:hi], words_dram[:, lo:hi])
 
-        nc.sync.dma_start(offsets[:], offs)
-        load_words(0, X_FIRST)
-        for r in range(SCALE_ROWS):
-            nc.sync.dma_start(scale_table[r:P:QUADRANT, :].bitcast(I32), scales_dram[r : x_scales.shape[1] : SCALE_ROWS, :])
-        w1_raw0 = load("w1_raw0", w1[:, :PASS])
-        load_words(X_FIRST, window(3))
-        w3_raw0 = load("w3_raw0", w3[:, :PASS])
-        load_words(window(3), T)
-        w1_raw1 = load("w1_raw1", w1[:, PASS:])
-        w3_raw1 = load("w3_raw1", w3[:, PASS:])
-        w2_raw0 = load("w2_raw0", w2[:PASS, :])
-        w2_raw = {(0, half): w2_raw0[:, :, half * HALF : (half + 1) * HALF] for half in (LOW, HIGH)}
-        for half in (LOW, HIGH):
-            w2_raw[1, half] = load("w2_raw1_%d" % half, w2[PASS:, half * HALF : (half + 1) * HALF])
+        def load_scales(queue):
+            for r in range(SCALE_ROWS):
+                queue.dma_start(scale_table[r:P:QUADRANT, :].bitcast(I32), scales_dram[r : x_scales.shape[1] : SCALE_ROWS, :])
 
-        up, down, x_codes, gate_banks, slice_banks, out_banks, gate, h_rounded, h = {}, {}, {}, {}, {}, {}, {}, {}, {}
+        up, down, x_codes, x_bytes, gate_banks, value_banks, out_banks, gate, planes, h_rounded, h = {}, {}, {}, {}, {}, {}, {}, {}, {}, {}, {}
 
         def copy_on(engine, dst, src):
             if engine == "scalar":
@@ -103,24 +89,16 @@ def tile_picked_pick_glu_silu_srt_p_kernel(tc, x_words, x_scales, w1, w3, w2, of
             else:
                 nc.gpsimd.tensor_scalar(dst, src, 1.0, 0.0, MULT, ADD)
 
-        def by_slot(raw):
-            return raw[:].rearrange("p j (m t) -> p j m t", t=PACK)
+        def round_up(engine, dst, raw, first_slot, lo=0, hi=P):
+            slots = dst.shape[1]
+            src = raw[:].rearrange("p j (m t) -> p j m t", t=PACK)[:, :, lo:hi, first_slot : first_slot + slots]
+            copy_on(engine, dst[:, :, lo:hi, :].rearrange("p t m j -> p m j t"), src.rearrange("p j m t -> p m j t"))
 
-        def round_up(engine, dst, src):
-            copy_on(engine, dst.rearrange("p t m j -> p m j t"), src.rearrange("p j m t -> p m j t"))
+        def up_tile(engine, name, slots=PAIR):
+            return in_line(engine, [P, slots, P, PACK], BF16, name)
 
-        def round_shared(raw, name):
-            rounded = in_line("scalar", [P, PACK, P, PACK], BF16, name)
-            round_up("scalar", rounded[:, :, VECTOR_M:, :], by_slot(raw)[:, :, VECTOR_M:, :])
-            round_up("vector", rounded[:, :, :VECTOR_M, :], by_slot(raw)[:, :, :VECTOR_M, :])
-            return rounded
-
-        def round_pair(engine, dst, raw, first_slot, lo=0, hi=P):
-            round_up(engine, dst[:, :, lo:hi, :], by_slot(raw)[:, :, lo:hi, first_slot : first_slot + PAIR])
-
-        def round_down(engine, dst, g, half, lo=0, hi=HALF):
-            src = w2_raw[g, half][:, :, lo:hi]
-            copy_on(engine, dst[:, lo:hi, :].rearrange("p (c i) j -> p c j i", i=PAIR), src.rearrange("p j (c i) -> p c j i", i=PAIR))
+        def round_down(engine, dst, src):
+            copy_on(engine, dst.rearrange("p (c i) j -> p c j i", i=PAIR), src.rearrange("p j (c i) -> p c j i", i=PAIR))
 
         def quantise(src, width, name):
             codes = keep.tile([P, width], U32, name=name + "_codes", align_bytes=64)
@@ -128,92 +106,104 @@ def tile_picked_pick_glu_silu_srt_p_kernel(tc, x_words, x_scales, w1, w3, w2, of
             nc.vector.quantize_mx(out=codes[:].bitcast(FP8X4), scales=scales[:], in_=src)
             return codes, scales
 
-        def quantise_up(name, g, rounded, first_slot=0):
+        def quantise_up(name, g, rounded, first_slot):
             slots = rounded.shape[1]
             codes, scales = quantise(rounded[:].rearrange("p t m j -> p (t m j)"), slots * P, "%s_%d_%d" % (name, g, first_slot))
             for t in range(slots):
                 up[name, g, first_slot + t] = codes[:, t * P : (t + 1) * P], scales[:, t * P : (t + 1) * P]
 
-        def quantise_down(half, passes, rounded):
-            codes, scales = quantise(rounded, len(passes) * HALF, "w2_%d_%d" % (half, passes[0]))
-            for i, g in enumerate(passes):
-                for r in range(PAIR):
-                    at = i * HALF + r * P
-                    down[g, PAIR * half + r] = codes[:, at : at + P], scales[:, at : at + P]
+        def quantise_down(rounded, blocks):
+            codes, scales = quantise(rounded, len(blocks) * P, "w2_%d_%d" % blocks[0])
+            for i, block in enumerate(blocks):
+                down[block] = codes[:, i * P : (i + 1) * P], scales[:, i * P : (i + 1) * P]
+
+        def entries(lo, width):
+            return offsets[:, lo // LIST_ROWS : (lo + width) // LIST_ROWS]
+
+        def gather_bytes(lo, width):
+            tile = in_line("vector", [P, width], U8, "x_bytes%d" % lo)
+            nc.vector.tensor_copy(tile[:], scale_table[:].indirect(entries(lo, width)))
+            for at in range(0, width, SLICE):
+                x_bytes[lo + at] = tile[:, at:]
 
         def gather_words(c):
-            if c % PAIR == 0:
-                x_codes[c // PAIR] = in_line("vector", [P, GROUP], U32, "x_codes%d" % c)
-            entries = offsets[:, c * CHUNK // LIST_ROWS : (c + 1) * CHUNK // LIST_ROWS]
-            at = c % PAIR * CHUNK
-            nc.vector.tensor_copy(x_codes[c // PAIR][:, at : at + CHUNK], word_table[:, : window(c + 1)].bitcast(U32).indirect(entries))
+            tile = in_line("vector", [P, CHUNK], U32, "x_codes%d" % c)
+            nc.vector.tensor_copy(tile[:], word_table[:, : window(c + 1)].bitcast(U32).indirect(entries(c * CHUNK, CHUNK)))
+            for at in range(0, CHUNK, SLICE):
+                x_codes[c * CHUNK + at] = tile[:, at:]
 
-        def product(bank, weights, lo, width):
-            group, col = divmod(lo, GROUP)
+        def product(dst, weights, lo, width):
             codes, scales = weights
             nc.tensor.matmul_mx(
-                out=bank,
+                out=dst,
                 lhsT=codes.bitcast(FP8X4),
                 lhsT_scale=scales,
-                rhs=x_codes[group][:, col : col + width].bitcast(FP8X4),
-                rhs_scale=x_bytes[:, lo : lo + width],
+                rhs=x_codes[lo][:, :width].bitcast(FP8X4),
+                rhs_scale=x_bytes[lo][:, :width],
                 start=True,
                 stop=True,
             )
 
-        def gate_products(g, c, tag="ring"):
-            for a in range(PAIR):
-                gate_banks[g, c, a] = next_bank([P, PAIR, CHUNK], tag)
-                for b in range(PAIR):
-                    product(gate_banks[g, c, a][:, b, :], up["w1", g, PAIR * a + b], c * CHUNK, CHUNK)
+        def pair_order(g):
+            return (1, 0) if g == 0 else (0, 1)
 
-        def silu(g, c):
-            planes = in_line("scalar", [P, PACK, CHUNK], F32, "gate%d%d" % (g, c))
-            for a in range(PAIR):
-                nc.scalar.activation(planes[:, PAIR * a : PAIR * (a + 1), :], gate_banks[g, c, a][:], SILU)
-            for i in range(PAIR):
-                gate[g, PAIR * c + i] = planes[:, :, i * SLICE : (i + 1) * SLICE]
+        def gate_products(g, c, banks):
+            for a, b in zip(pair_order(g), banks):
+                gate_banks[g, c, a] = bank(b, [P, PAIR, CHUNK])
+                for t in range(PAIR):
+                    product(gate_banks[g, c, a][:, t, :], up["w1", g, PAIR * a + t], c * CHUNK, CHUNK)
 
-        def slice_products(name, g, s, tag="ring"):
-            slice_banks[name, g, s] = next_bank([P, PACK, SLICE], tag)
-            for t in reversed(range(PACK)):
-                product(slice_banks[name, g, s][:, t, :], up[name, g, t], s * SLICE, SLICE)
+        def silu(g, c, pairs=(0, 1)):
+            if 0 in pairs:
+                planes[g, c] = in_line("scalar", [P, PACK, CHUNK], F32, "gate%d%d" % (g, c))
+                for i in range(PAIR):
+                    gate[g, PAIR * c + i] = planes[g, c][:, :, i * SLICE : (i + 1) * SLICE]
+            for i in pairs:
+                a = pair_order(g)[i]
+                nc.scalar.activation(planes[g, c][:, PAIR * a : PAIR * (a + 1), :], gate_banks[g, c, a][:], SILU)
+
+        def gate_slice_products(g, s, b):
+            gate_banks[g, s] = bank(b, [P, PACK, SLICE])
+            for t in range(PACK):
+                product(gate_banks[g, s][:, t, :], up["w1", g, t], s * SLICE, SLICE)
 
         def silu_slice(g, s):
             gate[g, s] = in_line("scalar", [P, PACK, SLICE], F32, "gate_slice%d%d" % (g, s))[:]
-            nc.scalar.activation(gate[g, s], slice_banks["w1", g, s][:], SILU)
+            nc.scalar.activation(gate[g, s], gate_banks[g, s][:], SILU)
 
-        def h_tile(g, first_slice, tile):
-            for i in range(tile.shape[1] // SLICE):
-                h_rounded[g, first_slice + i] = tile[:, i * SLICE :, :]
+        def value_products(g, s, b):
+            value_banks[g, s] = bank(b, [P, PACK, SLICE])
+            for a in pair_order(g):
+                for t in (PAIR * a, PAIR * a + 1):
+                    product(value_banks[g, s][:, t, :], up["w3", g, t], s * SLICE, SLICE)
 
-        def mult(g, s):
-            nc.vector.tensor_tensor(
-                h_rounded[g, s][:, :SLICE, :].rearrange("p (n i) t -> p n t i", i=PACK),
-                slice_banks["w3", g, s][:].rearrange("p t (n i) -> p n t i", i=PACK),
-                gate[g, s].rearrange("p t (n i) -> p n t i", i=PACK),
-                MULT,
-            )
+        def mults(g, first, count, part=None):
+            if (g, first) not in h_rounded:
+                h_rounded[g, first] = in_line("vector", [P, count * SLICE, PACK], BF16, "h%d%d" % (g, first))
+            for i in range(count) if part is None else [part]:
+                nc.vector.tensor_tensor(
+                    h_rounded[g, first][:, i * SLICE : (i + 1) * SLICE, :].rearrange("p (n i) t -> p n t i", i=PACK),
+                    value_banks[g, first + i][:].rearrange("p t (n i) -> p n t i", i=PACK),
+                    gate[g, first + i].rearrange("p t (n i) -> p n t i", i=PACK),
+                    MULT,
+                )
 
-        def first_group_mults(g):
-            h_tile(g, 0, keep.tile([P, GROUP, PACK], BF16, name="h_group%d" % g, align_bytes=64))
-            for s in range(GROUP // SLICE):
-                mult(g, s)
+        def quantise_h(g, first, lo=0, count=None):
+            tile = h_rounded[g, first]
+            if lo == 0:
+                width = tile.shape[1]
+                codes = keep.tile([P, width], U32, name="h_%d_%d_codes" % (g, first), align_bytes=64)
+                scales = in_line("vector", [P, width], U8, "h_%d_%d_scales" % (g, first))
+                for at in range(0, width, SLICE):
+                    h[g, first * SLICE + at] = codes[:, at:], scales[:, at:]
+            width = tile.shape[1] if count is None else count * SLICE
+            codes, scales = h[g, (first + lo) * SLICE]
+            src = tile[:, lo * SLICE : lo * SLICE + width, :].rearrange("p n t -> p (n t)")
+            nc.vector.quantize_mx(out=codes[:, :width].bitcast(FP8X4), scales=scales[:, :width], in_=src)
 
-        def chunk_mults(g, c):
-            h_tile(g, PAIR * c, in_line("vector", [P, CHUNK, PACK], BF16, "h_chunk%d%d" % (g, c)))
-            for s in (PAIR * c, PAIR * c + 1):
-                mult(g, s)
-
-        def quantise_h(g, lo, width=CHUNK):
-            src = h_rounded[g, lo // SLICE][:, :width, :]
-            codes, scales = quantise(src.rearrange("p n t -> p (n t)"), width, "h_%d_%d" % (g, lo))
-            for at in range(0, width, SLICE):
-                h[g, lo + at] = codes[:, at:], scales[:, at:]
-
-        def down_products(lo, width, half, passes=range(PASSES), tag="ring"):
+        def down_products(lo, width, half, passes, b=None):
             if passes[0] == 0:
-                out_banks[lo, half] = next_bank([P, PAIR, width], tag)
+                out_banks[lo, half] = bank(b, [P, PAIR, width])
             for g in passes:
                 for r in range(PAIR):
                     nc.tensor.matmul_mx(
@@ -226,118 +216,161 @@ def tile_picked_pick_glu_silu_srt_p_kernel(tc, x_words, x_scales, w1, w3, w2, of
                         stop=(g == PASSES - 1 and r == PAIR - 1),
                     )
 
-        def store_chunk(c, half):
-            y = in_line("scalar", [P, PAIR, CHUNK], F32, "y%d_%d" % (c, half))
-            nc.scalar.copy(y[:], out_banks[c * CHUNK, half][:])
+        def wide_products(r, passes, b=None):
+            if passes[0] == 0:
+                out_banks["wide", r] = bank(b, [P, GROUP])
+            for g in passes:
+                nc.tensor.matmul_mx(
+                    out=out_banks["wide", r][:],
+                    lhsT=down[g, r][0].bitcast(FP8X4),
+                    lhsT_scale=down[g, r][1],
+                    rhs=h[g, 0][0][:, :GROUP].bitcast(FP8X4),
+                    rhs_scale=h[g, 0][1][:, :GROUP],
+                    start=(g == 0),
+                    stop=(g == PASSES - 1),
+                )
+
+        def store_wide(r):
+            y = in_line("scalar", [P, GROUP], F32, "y_wide%d" % r)
+            nc.scalar.copy(y[:], out_banks["wide", r][:])
+            nc.sync.dma_start(out[r * P : (r + 1) * P, :GROUP], y[:])
+
+        def out_rows(half, c):
             rows = out[half * HALF : (half + 1) * HALF, c * CHUNK : (c + 1) * CHUNK]
-            nc.sync.dma_start(rows.rearrange("(r p) n -> p r n", p=P), y[:])
+            return rows.rearrange("(r p) n -> p r n", p=P)
 
-        def store_last_chunk(engine, half, queue):
-            y = in_line(engine, [P, PAIR, CHUNK], F32, "y_last%d" % half)
-            for i, s in enumerate(LAST_SLICES):
-                copy_on(engine, y[:, :, i * SLICE : (i + 1) * SLICE], out_banks[s * SLICE, half][:])
-            rows = out[half * HALF : (half + 1) * HALF, S - CHUNK :]
-            queue.dma_start(rows.rearrange("(r p) n -> p r n", p=P), y[:])
+        def store_chunk(c, half, engine="scalar"):
+            y = in_line(engine, [P, PAIR, CHUNK], F32, "y%d_%d" % (c, half))
+            copy_on(engine, y[:], out_banks[c * CHUNK, half][:])
+            nc.sync.dma_start(out_rows(half, c), y[:])
 
-        pair_shape = [P, PAIR, P, PACK]
-        half_shape = [P, HALF, PACK]
+        def store_slices(c, half, engine, queue):
+            y = in_line(engine, [P, PAIR, CHUNK], F32, "y%d_%d" % (c, half))
+            for i in range(PAIR):
+                copy_on(engine, y[:, :, i * SLICE : (i + 1) * SLICE], out_banks[c * CHUNK + i * SLICE, half][:])
+            queue.dma_start(out_rows(half, c), y[:])
 
-        x_bytes = in_line("vector", [P, S], U8, "x_bytes")
-        nc.vector.tensor_copy(x_bytes[:], scale_table[:].indirect(offsets[:]))
-        quantise_up("w1", 0, round_shared(w1_raw0, "w1_first"))
-        for c in range(3):
-            gather_words(c)
-        quantise_up("w3", 0, round_shared(w3_raw0, "w3_first"))
-        gather_words(3)
-        gate_products(0, 0, "held")
+        nc.sync.dma_start(offsets[:], offs)
+        load_words(0, X_FIRST)
+        load_scales(nc.sync)
+        w1_raw0 = load("w1_raw0", w1[:, :PASS])
+        load_words(X_FIRST, window(1))
+        load_words(window(1), window(3))
+        w3_raw0 = load("w3_raw0", w3[:, :PASS])
+        load_words(window(3), T)
+        w1_raw1 = load("w1_raw1", w1[:, PASS:])
+        w3_raw1 = load("w3_raw1", w3[:, PASS:])
+        w2_raw0 = load("w2_raw0", w2[:PASS, :])
+        w2_raw1_low = load("w2_raw1_low", w2[PASS:, :HALF])[:]
+        w2_raw1_high = load("w2_raw1_high", w2[PASS:, HALF:])[:]
+
+        gather_bytes(0, S)
+        w1_low = up_tile("scalar", "w1_low0")
+        round_up("scalar", w1_low, w1_raw0, 0)
+        w1_high = up_tile("vector", "w1_high0")
+        round_up("vector", w1_high, w1_raw0, PAIR)
+        gather_words(0)
+        quantise_up("w1", 0, w1_high, PAIR)
+        quantise_up("w1", 0, w1_low, 0)
+        gate_products(0, 0, (0, 1))
         silu(0, 0)
-        for c in (1, 2):
-            gate_products(0, c)
-            silu(0, c)
+        gather_words(1)
+        gate_products(0, 1, (2, 3))
+        gather_words(2)
+        gate_products(0, 2, (0, 1))
+        w3_low = up_tile("scalar", "w3_low0")
+        round_up("scalar", w3_low, w3_raw0, 0, 0, SCALAR_M)
+        w3_high = up_tile("vector", "w3_high0")
+        round_up("vector", w3_high, w3_raw0, PAIR)
+        round_up("vector", w3_low, w3_raw0, 0, SCALAR_M, P)
+        quantise_up("w3", 0, w3_high, PAIR)
+        quantise_up("w3", 0, w3_low, 0)
+        gather_words(3)
+        silu(0, 1)
+        silu(0, 2)
+        for s in range(4):
+            value_products(0, s, 4 + s)
+        gate_products(0, 3, (2, 3))
 
-        w1_low = for_gpsimd(pair_shape, "w1_low")
-        round_pair("gpsimd", w1_low, w1_raw1, 0)
-        w1_high = in_line("scalar", pair_shape, BF16, "w1_high")
-        round_pair("scalar", w1_high, w1_raw1, PAIR)
-        for s in (0, 1):
-            slice_products("w3", 0, s)
-        for s in (2, 3):
-            slice_products("w3", 0, s, "held")
-        gate_products(0, 3)
+        w1_low = up_tile("gpsimd", "w1_low1")
+        round_up("gpsimd", w1_low, w1_raw1, 0, 0, GPSIMD_W1_M)
+        w1_high = up_tile("scalar", "w1_high1")
+        round_up("scalar", w1_high, w1_raw1, PAIR)
+        round_up("scalar", w1_low, w1_raw1, 0, GPSIMD_W1_M, P)
         silu(0, 3)
-        slice_products("w3", 0, 4)
-        first_group_mults(0)
+        mults(0, 0, 4)
+        for s in range(4, 8):
+            value_products(0, s, s)
         quantise_up("w1", 1, w1_high, PAIR)
-        quantise_up("w1", 1, w1_low)
-        quantise_h(0, 0)
+        quantise_up("w1", 1, w1_low, 0)
+        quantise_h(0, 0, 0, 2)
+        gate_products(1, 0, (0, 1))
+        gate_products(1, 1, (2, 3))
+        gate_products(1, 2, (4, 5))
 
-        slice_products("w3", 0, 5)
-        for s in (6, 7):
-            slice_products("w3", 0, s, "held")
-        gate_products(1, 0)
-        w3_high = in_line("scalar", pair_shape, BF16, "w3_high")
-        round_pair("scalar", w3_high, w3_raw1, PAIR)
-        w3_low = for_gpsimd(pair_shape, "w3_low")
-        round_pair("gpsimd", w3_low, w3_raw1, 0, 0, GPSIMD_M)
-        for c in (1, 2):
-            gate_products(1, c)
+        w3_low = up_tile("gpsimd", "w3_low1")
+        round_up("gpsimd", w3_low, w3_raw1, 0, 0, GPSIMD_M)
+        w3_high = up_tile("scalar", "w3_high1")
+        round_up("scalar", w3_high, w3_raw1, PAIR)
         for c in range(3):
             silu(1, c)
-        chunk_mults(0, 2)
-        round_pair("vector", w3_low, w3_raw1, 0, GPSIMD_M, P)
+        mults(0, 4, 2)
+        round_up("vector", w3_low, w3_raw1, 0, GPSIMD_M, P)
+        quantise_h(0, 0, 2, 2)
+        quantise_up("w3", 1, w3_low, 0)
         quantise_up("w3", 1, w3_high, PAIR)
-        quantise_up("w3", 1, w3_low)
+        mults(0, 6, 2)
+        for s, b in enumerate((0, 1, 2, 6, 3, 7)):
+            value_products(1, s, b)
+        gate_slice_products(1, 6, 0)
+        gate_slice_products(1, 7, 1)
+        value_products(1, 6, 4)
+        value_products(1, 7, 5)
 
-        chunk_mults(0, 3)
-        w2_low = for_gpsimd([P, PASSES, HALF, PACK], "w2_low")
-        round_down("gpsimd", w2_low[:, 0], 0, LOW)
-        round_down("gpsimd", w2_low[:, 1], 1, LOW, 0, GPSIMD_COLUMNS)
-        round_down("scalar", w2_low[:, 1], 1, LOW, GPSIMD_COLUMNS, HALF)
-        for s in range(4):
-            slice_products("w3", 1, s)
-        for s in LAST_SLICES:
-            slice_products("w1", 1, s)
-        w2_high = []
-        for g in range(PASSES):
-            w2_high.append(in_line("scalar", half_shape, BF16, "w2_high%d" % g))
-            round_down("scalar", w2_high[g], g, HIGH)
-        silu_slice(1, LAST_SLICES[0])
-        first_group_mults(1)
-        for s in range(4, 8):
-            slice_products("w3", 1, s)
+        def columns(raw, r):
+            return raw[:, :, r * P : (r + 1) * P]
 
-        quantise_down(LOW, range(PASSES), w2_low[:].rearrange("p g c j -> p (g c j)"))
+        w2_gpsimd = in_line("gpsimd", [P, 4 * P, PACK], BF16, "w2_gpsimd")
+        round_down("gpsimd", w2_gpsimd[:, : 3 * P, :], w2_raw0[:, :, : 3 * P])
+        round_down("gpsimd", w2_gpsimd[:, 3 * P :, :], columns(w2_raw1_low, 0))
+        w2_odd = in_line("scalar", [P, HALF, PACK], BF16, "w2_odd")
+        round_down("scalar", w2_odd[:, :P, :], columns(w2_raw0, 3))
+        round_down("scalar", w2_odd[:, P:, :], columns(w2_raw1_low, 1))
+        silu_slice(1, 6)
+        silu_slice(1, 7)
+        w2_last = []
+        for r in range(PAIR):
+            w2_last.append(in_line("scalar", [P, P, PACK], BF16, "w2_last%d" % r))
+            round_down("scalar", w2_last[r][:], columns(w2_raw1_high, r))
+        mults(1, 0, 4)
+        quantise_down(w2_gpsimd[:].rearrange("p c j -> p (c j)"), [(0, 0), (0, 1), (0, 2), (1, 0)])
+        wide_products(0, [0], 2)
+        wide_products(1, [0], 6)
         quantise_h(1, 0)
-        down_products(0, CHUNK, LOW, tag="held")
-        for g in range(PASSES):
-            quantise_h(g, CHUNK)
-        down_products(CHUNK, CHUNK, LOW, tag="held")
-        for g in range(PASSES):
-            quantise_down(HIGH, [g], w2_high[g][:].rearrange("p c j -> p (c j)"))
-        store_chunk(0, LOW)
-        store_chunk(1, LOW)
-        silu_slice(1, LAST_SLICES[1])
-        down_products(0, CHUNK, HIGH)
-        store_chunk(0, HIGH)
-        down_products(CHUNK, CHUNK, HIGH, tag="held")
-        store_chunk(1, HIGH)
-
-        chunk_mults(1, 2)
-        for g in range(PASSES):
-            quantise_h(g, 2 * CHUNK)
-        quantise_h(0, 3 * CHUNK)
-        down_products(2 * CHUNK, CHUNK, LOW, tag="held")
+        wide_products(0, [1])
+        quantise_down(w2_odd[:].rearrange("p c j -> p (c j)"), [(0, 3), (1, 1)])
+        wide_products(1, [1])
+        for r in range(PAIR):
+            mults(1, 4, 2, r)
+            quantise_down(w2_last[r][:].rearrange("p c j -> p (c j)"), [(1, PAIR + r)])
+            wide_products(PAIR + r, [0, 1], r)
+        for r in range(4):
+            store_wide(r)
+        quantise_h(0, 4)
+        quantise_h(1, 4)
+        quantise_h(0, 6)
+        down_products(2 * CHUNK, CHUNK, LOW, [0, 1], 3)
         store_chunk(2, LOW)
-        down_products(2 * CHUNK, CHUNK, HIGH)
+        down_products(2 * CHUNK, CHUNK, HIGH, [0, 1], 7)
         store_chunk(2, HIGH)
-
-        chunk_mults(1, 3)
-        for s in LAST_SLICES:
+        mults(1, 6, 1)
+        mults(1, 7, 1)
+        for s, banks in ((6, (2, 6)), (7, (0, 4))):
             for half in (LOW, HIGH):
-                down_products(s * SLICE, SLICE, half, [0])
-        for s in LAST_SLICES:
-            quantise_h(1, s * SLICE, SLICE)
+                down_products(s * SLICE, SLICE, half, [0], banks[half])
+        for s in (6, 7):
+            quantise_h(1, s)
             for half in (LOW, HIGH):
                 down_products(s * SLICE, SLICE, half, [1])
-        store_last_chunk("vector", LOW, nc.sync)
-        store_last_chunk("scalar", HIGH, nc.scalar)
+        store_slices(3, LOW, "vector", nc.sync)
+        store_slices(3, HIGH, "scalar", nc.scalar)

@@ -230,10 +230,12 @@ def tile_picked_pick_glu_silu_srt_p_kernel(tc, x_words, x_scales, w1, w3, w2, of
                     stop=(g == PASSES - 1),
                 )
 
+        store_queue = (nc.sync, nc.scalar)
+
         def store_wide(r):
             y = in_line("scalar", [P, GROUP], F32, "y_wide%d" % r)
             nc.scalar.copy(y[:], out_banks["wide", r][:])
-            nc.sync.dma_start(out[r * P : (r + 1) * P, :GROUP], y[:])
+            store_queue[r % PAIR].dma_start(out[r * P : (r + 1) * P, :GROUP], y[:])
 
         def out_rows(half, c):
             rows = out[half * HALF : (half + 1) * HALF, c * CHUNK : (c + 1) * CHUNK]
@@ -242,7 +244,7 @@ def tile_picked_pick_glu_silu_srt_p_kernel(tc, x_words, x_scales, w1, w3, w2, of
         def store_chunk(c, half, engine="scalar"):
             y = in_line(engine, [P, PAIR, CHUNK], F32, "y%d_%d" % (c, half))
             copy_on(engine, y[:], out_banks[c * CHUNK, half][:])
-            nc.sync.dma_start(out_rows(half, c), y[:])
+            store_queue[half].dma_start(out_rows(half, c), y[:])
 
         def store_slices(c, half, engine, queue):
             y = in_line(engine, [P, PAIR, CHUNK], F32, "y%d_%d" % (c, half))

from contextlib import ExitStack

import concourse.mybir as mybir

K, T, S, H, N = 512, 2048, 1024, 1024, 512
FLOPS = 2 * S * (2 * K * H + H * N)

F32 = mybir.dt.float32
BF16 = mybir.dt.bfloat16
I32 = mybir.dt.int32
U32 = mybir.dt.uint32
U16 = mybir.dt.uint16
U8 = mybir.dt.uint8
FP8X4 = mybir.dt.float8_e4m3fn_x4
SILU = mybir.ActivationFunctionType.Silu
MULT = mybir.AluOpType.mult
ADD = mybir.AluOpType.add

P = 128
PACK = 4
PAIR = 2
PASS = P * PACK
PASSES = H // PASS
HALF = N // 2
SLICE = 128
CHUNK = 256
GROUP = 512
LOW, HIGH = 0, 1
LIST_ROWS = 16
QUADRANT, SCALE_ROWS = 32, 4
SLOTS = {"scalar": 9, "vector": 26}

X_FIRST = 640
SCALAR_M = 72
GPSIMD_W1_M = 96
GPSIMD_M = 52


def tile_picked_pick_glu_silu_srt_p_kernel(tc, x_words, x_scales, w1, w3, w2, offs, out):
    nc = tc.nc
    with ExitStack() as ctx:
        keep = ctx.enter_context(tc.tile_pool(name="keep", bufs=1))
        line = ctx.enter_context(tc.tile_pool(name="line", bufs=1))
        psum = ctx.enter_context(tc.psum_pool(name="psum", bufs=1))

        def in_line(engine, shape, dtype, name):
            if engine == "gpsimd":
                return keep.tile(shape, dtype, name=name, tag="gpsimd", align_bytes=64)
            return line.tile(shape, dtype, name=name, tag=engine, bufs=SLOTS[engine], align_bytes=64)

        def bank(b, shape):
            return psum.tile(shape, F32, name="bank%d" % b, tag="bank%d" % b)

        offsets = keep.tile([P, S // LIST_ROWS], U16, name="offsets")
        word_table = keep.tile([P, T], I32, name="word_table")
        scale_table = keep.tile([P, T], U8, name="scale_table")
        warm = keep.tile([P, 8], F32, name="warm")
        warm_out = keep.tile([P, 8], F32, name="warm_out")

        nc.vector.memset(scale_table[:].bitcast(I32), 0)
        nc.vector.memset(warm[:], 0.0)
        nc.scalar.activation(warm_out[:], warm[:], SILU)

        words_dram = x_words[0].rearrange("p n r -> p (n r)").bitcast(I32)
        scales_dram = x_scales[0].bitcast(I32)

        def window(chunks):
            return chunks * CHUNK + T - S

        def load(name, rows):
            tile = keep.tile([P, PACK, rows.shape[1]], F32, name=name)
            nc.sync.dma_start(tile[:], rows.rearrange("(p j) c -> p j c", j=PACK))
            return tile

        def load_words(lo, hi):
            nc.sync.dma_start(word_table[:, lo:hi], words_dram[:, lo:hi])

        def load_scales(queue):
            for r in range(SCALE_ROWS):
                queue.dma_start(scale_table[r:P:QUADRANT, :].bitcast(I32), scales_dram[r : x_scales.shape[1] : SCALE_ROWS, :])

        up, down, x_codes, x_bytes, gate_banks, value_banks, out_banks, gate, planes, h_rounded, h = {}, {}, {}, {}, {}, {}, {}, {}, {}, {}, {}

        def copy_on(engine, dst, src):
            if engine == "scalar":
                nc.scalar.copy(dst, src)
            elif engine == "vector":
                nc.vector.tensor_copy(dst, src)
            else:
                nc.gpsimd.tensor_scalar(dst, src, 1.0, 0.0, MULT, ADD)

        def round_up(engine, dst, raw, first_slot, lo=0, hi=P):
            slots = dst.shape[1]
            src = raw[:].rearrange("p j (m t) -> p j m t", t=PACK)[:, :, lo:hi, first_slot : first_slot + slots]
            copy_on(engine, dst[:, :, lo:hi, :].rearrange("p t m j -> p m j t"), src.rearrange("p j m t -> p m j t"))

        def up_tile(engine, name, slots=PAIR):
            return in_line(engine, [P, slots, P, PACK], BF16, name)

        def round_down(engine, dst, src):
            copy_on(engine, dst.rearrange("p (c i) j -> p c j i", i=PAIR), src.rearrange("p j (c i) -> p c j i", i=PAIR))

        def quantise(src, width, name):
            codes = keep.tile([P, width], U32, name=name + "_codes", align_bytes=64)
            scales = in_line("vector", [P, width], U8, name + "_scales")
            nc.vector.quantize_mx(out=codes[:].bitcast(FP8X4), scales=scales[:], in_=src)
            return codes, scales

        def quantise_up(name, g, rounded, first_slot):
            slots = rounded.shape[1]
            codes, scales = quantise(rounded[:].rearrange("p t m j -> p (t m j)"), slots * P, "%s_%d_%d" % (name, g, first_slot))
            for t in range(slots):
                up[name, g, first_slot + t] = codes[:, t * P : (t + 1) * P], scales[:, t * P : (t + 1) * P]

        def quantise_down(rounded, blocks):
            codes, scales = quantise(rounded, len(blocks) * P, "w2_%d_%d" % blocks[0])
            for i, block in enumerate(blocks):
                down[block] = codes[:, i * P : (i + 1) * P], scales[:, i * P : (i + 1) * P]

        def entries(lo, width):
            return offsets[:, lo // LIST_ROWS : (lo + width) // LIST_ROWS]

        def gather_bytes(lo, width):
            tile = in_line("vector", [P, width], U8, "x_bytes%d" % lo)
            nc.vector.tensor_copy(tile[:], scale_table[:].indirect(entries(lo, width)))
            for at in range(0, width, SLICE):
                x_bytes[lo + at] = tile[:, at:]

        def gather_words(c):
            tile = in_line("vector", [P, CHUNK], U32, "x_codes%d" % c)
            nc.vector.tensor_copy(tile[:], word_table[:, : window(c + 1)].bitcast(U32).indirect(entries(c * CHUNK, CHUNK)))
            for at in range(0, CHUNK, SLICE):
                x_codes[c * CHUNK + at] = tile[:, at:]

        def product(dst, weights, lo, width):
            codes, scales = weights
            nc.tensor.matmul_mx(
                out=dst,
                lhsT=codes.bitcast(FP8X4),
                lhsT_scale=scales,
                rhs=x_codes[lo][:, :width].bitcast(FP8X4),
                rhs_scale=x_bytes[lo][:, :width],
                start=True,
                stop=True,
            )

        def pair_order(g):
            return (1, 0) if g == 0 else (0, 1)

        def gate_products(g, c, banks):
            for a, b in zip(pair_order(g), banks):
                gate_banks[g, c, a] = bank(b, [P, PAIR, CHUNK])
                for t in range(PAIR):
                    product(gate_banks[g, c, a][:, t, :], up["w1", g, PAIR * a + t], c * CHUNK, CHUNK)

        def silu(g, c, pairs=(0, 1)):
            if 0 in pairs:
                planes[g, c] = in_line("scalar", [P, PACK, CHUNK], F32, "gate%d%d" % (g, c))
                for i in range(PAIR):
                    gate[g, PAIR * c + i] = planes[g, c][:, :, i * SLICE : (i + 1) * SLICE]
            for i in pairs:
                a = pair_order(g)[i]
                nc.scalar.activation(planes[g, c][:, PAIR * a : PAIR * (a + 1), :], gate_banks[g, c, a][:], SILU)

        def gate_slice_products(g, s, b):
            gate_banks[g, s] = bank(b, [P, PACK, SLICE])
            for t in range(PACK):
                product(gate_banks[g, s][:, t, :], up["w1", g, t], s * SLICE, SLICE)

        def silu_slice(g, s):
            gate[g, s] = in_line("scalar", [P, PACK, SLICE], F32, "gate_slice%d%d" % (g, s))[:]
            nc.scalar.activation(gate[g, s], gate_banks[g, s][:], SILU)

        def value_products(g, s, b):
            value_banks[g, s] = bank(b, [P, PACK, SLICE])
            for a in pair_order(g):
                for t in (PAIR * a, PAIR * a + 1):
                    product(value_banks[g, s][:, t, :], up["w3", g, t], s * SLICE, SLICE)

        def mults(g, first, count, part=None):
            if (g, first) not in h_rounded:
                h_rounded[g, first] = in_line("vector", [P, count * SLICE, PACK], BF16, "h%d%d" % (g, first))
            for i in range(count) if part is None else [part]:
                nc.vector.tensor_tensor(
                    h_rounded[g, first][:, i * SLICE : (i + 1) * SLICE, :].rearrange("p (n i) t -> p n t i", i=PACK),
                    value_banks[g, first + i][:].rearrange("p t (n i) -> p n t i", i=PACK),
                    gate[g, first + i].rearrange("p t (n i) -> p n t i", i=PACK),
                    MULT,
                )

        def quantise_h(g, first, lo=0, count=None):
            tile = h_rounded[g, first]
            if lo == 0:
                width = tile.shape[1]
                codes = keep.tile([P, width], U32, name="h_%d_%d_codes" % (g, first), align_bytes=64)
                scales = in_line("vector", [P, width], U8, "h_%d_%d_scales" % (g, first))
                for at in range(0, width, SLICE):
                    h[g, first * SLICE + at] = codes[:, at:], scales[:, at:]
            width = tile.shape[1] if count is None else count * SLICE
            codes, scales = h[g, (first + lo) * SLICE]
            src = tile[:, lo * SLICE : lo * SLICE + width, :].rearrange("p n t -> p (n t)")
            nc.vector.quantize_mx(out=codes[:, :width].bitcast(FP8X4), scales=scales[:, :width], in_=src)

        def down_products(lo, width, half, passes, b=None):
            if passes[0] == 0:
                out_banks[lo, half] = bank(b, [P, PAIR, width])
            for g in passes:
                for r in range(PAIR):
                    nc.tensor.matmul_mx(
                        out=out_banks[lo, half][:, r, :],
                        lhsT=down[g, PAIR * half + r][0].bitcast(FP8X4),
                        lhsT_scale=down[g, PAIR * half + r][1],
                        rhs=h[g, lo][0][:, :width].bitcast(FP8X4),
                        rhs_scale=h[g, lo][1][:, :width],
                        start=(g == 0 and r == 0),
                        stop=(g == PASSES - 1 and r == PAIR - 1),
                    )

        def wide_products(r, passes, b=None):
            if passes[0] == 0:
                out_banks["wide", r] = bank(b, [P, GROUP])
            for g in passes:
                nc.tensor.matmul_mx(
                    out=out_banks["wide", r][:],
                    lhsT=down[g, r][0].bitcast(FP8X4),
                    lhsT_scale=down[g, r][1],
                    rhs=h[g, 0][0][:, :GROUP].bitcast(FP8X4),
                    rhs_scale=h[g, 0][1][:, :GROUP],
                    start=(g == 0),
                    stop=(g == PASSES - 1),
                )

        store_queue = (nc.sync, nc.scalar)

        def store_wide(r):
            y = in_line("scalar", [P, GROUP], F32, "y_wide%d" % r)
            nc.scalar.copy(y[:], out_banks["wide", r][:])
            store_queue[r % PAIR].dma_start(out[r * P : (r + 1) * P, :GROUP], y[:])

        def out_rows(half, c):
            rows = out[half * HALF : (half + 1) * HALF, c * CHUNK : (c + 1) * CHUNK]
            return rows.rearrange("(r p) n -> p r n", p=P)

        def store_chunk(c, half, engine="scalar"):
            y = in_line(engine, [P, PAIR, CHUNK], F32, "y%d_%d" % (c, half))
            copy_on(engine, y[:], out_banks[c * CHUNK, half][:])
            store_queue[half].dma_start(out_rows(half, c), y[:])

        def store_slices(c, half, engine, queue):
            y = in_line(engine, [P, PAIR, CHUNK], F32, "y%d_%d" % (c, half))
            for i in range(PAIR):
                copy_on(engine, y[:, :, i * SLICE : (i + 1) * SLICE], out_banks[c * CHUNK + i * SLICE, half][:])
            queue.dma_start(out_rows(half, c), y[:])

        nc.sync.dma_start(offsets[:], offs)
        load_words(0, X_FIRST)
        load_scales(nc.sync)
        w1_raw0 = load("w1_raw0", w1[:, :PASS])
        load_words(X_FIRST, window(1))
        load_words(window(1), window(3))
        w3_raw0 = load("w3_raw0", w3[:, :PASS])
        load_words(window(3), T)
        w1_raw1 = load("w1_raw1", w1[:, PASS:])
        w3_raw1 = load("w3_raw1", w3[:, PASS:])
        w2_raw0 = load("w2_raw0", w2[:PASS, :])
        w2_raw1_low = load("w2_raw1_low", w2[PASS:, :HALF])[:]
        w2_raw1_high = load("w2_raw1_high", w2[PASS:, HALF:])[:]

        gather_bytes(0, S)
        w1_low = up_tile("scalar", "w1_low0")
        round_up("scalar", w1_low, w1_raw0, 0)
        w1_high = up_tile("vector", "w1_high0")
        round_up("vector", w1_high, w1_raw0, PAIR)
        gather_words(0)
        quantise_up("w1", 0, w1_high, PAIR)
        quantise_up("w1", 0, w1_low, 0)
        gate_products(0, 0, (0, 1))
        silu(0, 0)
        gather_words(1)
        gate_products(0, 1, (2, 3))
        gather_words(2)
        gate_products(0, 2, (0, 1))
        w3_low = up_tile("scalar", "w3_low0")
        round_up("scalar", w3_low, w3_raw0, 0, 0, SCALAR_M)
        w3_high = up_tile("vector", "w3_high0")
        round_up("vector", w3_high, w3_raw0, PAIR)
        round_up("vector", w3_low, w3_raw0, 0, SCALAR_M, P)
        quantise_up("w3", 0, w3_high, PAIR)
        quantise_up("w3", 0, w3_low, 0)
        gather_words(3)
        silu(0, 1)
        silu(0, 2)
        for s in range(4):
            value_products(0, s, 4 + s)
        gate_products(0, 3, (2, 3))

        w1_low = up_tile("gpsimd", "w1_low1")
        round_up("gpsimd", w1_low, w1_raw1, 0, 0, GPSIMD_W1_M)
        w1_high = up_tile("scalar", "w1_high1")
        round_up("scalar", w1_high, w1_raw1, PAIR)
        round_up("scalar", w1_low, w1_raw1, 0, GPSIMD_W1_M, P)
        silu(0, 3)
        mults(0, 0, 4)
        for s in range(4, 8):
            value_products(0, s, s)
        quantise_up("w1", 1, w1_high, PAIR)
        quantise_up("w1", 1, w1_low, 0)
        quantise_h(0, 0, 0, 2)
        gate_products(1, 0, (0, 1))
        gate_products(1, 1, (2, 3))
        gate_products(1, 2, (4, 5))

        w3_low = up_tile("gpsimd", "w3_low1")
        round_up("gpsimd", w3_low, w3_raw1, 0, 0, GPSIMD_M)
        w3_high = up_tile("scalar", "w3_high1")
        round_up("scalar", w3_high, w3_raw1, PAIR)
        for c in range(3):
            silu(1, c)
        mults(0, 4, 2)
        round_up("vector", w3_low, w3_raw1, 0, GPSIMD_M, P)
        quantise_h(0, 0, 2, 2)
        quantise_up("w3", 1, w3_low, 0)
        quantise_up("w3", 1, w3_high, PAIR)
        mults(0, 6, 2)
        for s, b in enumerate((0, 1, 2, 6, 3, 7)):
            value_products(1, s, b)
        gate_slice_products(1, 6, 0)
        gate_slice_products(1, 7, 1)
        value_products(1, 6, 4)
        value_products(1, 7, 5)

        def columns(raw, r):
            return raw[:, :, r * P : (r + 1) * P]

        w2_gpsimd = in_line("gpsimd", [P, 4 * P, PACK], BF16, "w2_gpsimd")
        round_down("gpsimd", w2_gpsimd[:, : 3 * P, :], w2_raw0[:, :, : 3 * P])
        round_down("gpsimd", w2_gpsimd[:, 3 * P :, :], columns(w2_raw1_low, 0))
        w2_odd = in_line("scalar", [P, HALF, PACK], BF16, "w2_odd")
        round_down("scalar", w2_odd[:, :P, :], columns(w2_raw0, 3))
        round_down("scalar", w2_odd[:, P:, :], columns(w2_raw1_low, 1))
        silu_slice(1, 6)
        silu_slice(1, 7)
        w2_last = []
        for r in range(PAIR):
            w2_last.append(in_line("scalar", [P, P, PACK], BF16, "w2_last%d" % r))
            round_down("scalar", w2_last[r][:], columns(w2_raw1_high, r))
        mults(1, 0, 4)
        quantise_down(w2_gpsimd[:].rearrange("p c j -> p (c j)"), [(0, 0), (0, 1), (0, 2), (1, 0)])
        wide_products(0, [0], 2)
        wide_products(1, [0], 6)
        quantise_h(1, 0)
        wide_products(0, [1])
        quantise_down(w2_odd[:].rearrange("p c j -> p (c j)"), [(0, 3), (1, 1)])
        wide_products(1, [1])
        for r in range(PAIR):
            mults(1, 4, 2, r)
            quantise_down(w2_last[r][:].rearrange("p c j -> p (c j)"), [(1, PAIR + r)])
            wide_products(PAIR + r, [0, 1], r)
        for r in range(4):
            store_wide(r)
        quantise_h(0, 4)
        quantise_h(1, 4)
        quantise_h(0, 6)
        down_products(2 * CHUNK, CHUNK, LOW, [0, 1], 3)
        store_chunk(2, LOW)
        down_products(2 * CHUNK, CHUNK, HIGH, [0, 1], 7)
        store_chunk(2, HIGH)
        mults(1, 6, 1)
        mults(1, 7, 1)
        for s, banks in ((6, (2, 6)), (7, (0, 4))):
            for half in (LOW, HIGH):
                down_products(s * SLICE, SLICE, half, [0], banks[half])
        for s in (6, 7):
            quantise_h(1, s)
            for half in (LOW, HIGH):
                down_products(s * SLICE, SLICE, half, [1])
        store_slices(3, LOW, "vector", nc.sync)
        store_slices(3, HIGH, "scalar", nc.scalar)
